import numpy as np
import ml_dtypes


def mxq(x, axis, fmt="e4m3"):
    dtype, down = {"e4m3": (ml_dtypes.float8_e4m3fn, 7), "e5m2": (ml_dtypes.float8_e5m2, 14)}[fmt]
    v = np.moveaxis(np.asarray(x, np.float32).astype(ml_dtypes.bfloat16).astype(np.float64), axis, -1)
    blocks = v.reshape(v.shape[:-1] + (-1, 32))
    amax = np.abs(blocks).max(-1, keepdims=True)
    byte = np.maximum(np.where(amax > 0, np.frexp(amax)[1] - 1 + 127, 0) - down, 1)
    scale = np.exp2(byte - 127.0)
    codes = (blocks / scale).astype(np.float32).astype(dtype).astype(np.float64)
    return np.moveaxis((codes * scale).reshape(v.shape), -1, axis)


WIDE = False


def mx_kscale(k):
    if not WIDE:
        return np.ones(k)
    levels = np.array([18, -18])
    if k % 512:
        return np.exp2(np.random.permutation(np.resize(levels, k // 32))).repeat(32)
    a = np.empty((k // 512, 16))
    for p in range(k // 512):
        a[p, :8] = np.random.permutation(np.resize(levels, 8))
        for g in range(8):
            far = levels[np.abs(levels - a[p, g]) >= 10]
            a[p, g + 8] = far[np.random.randint(len(far))]
    return np.exp2(a.ravel()).repeat(32)


def f64(x):
    return np.asarray(x).astype(np.float64)


def striped(idx):
    return np.tile(np.asarray(idx).reshape(-1, 16).T, (8, 1)).astype(np.uint16)


def unstriped(offs):
    return offs[:16].T.reshape(-1).astype(np.int64)


def setup_inputs():
    n = np.random.standard_normal
    uni = np.random.uniform
    idx = np.random.permutation(2048)[:512]
    f_d = mx_kscale(512)
    f_i = np.ones(2048)
    f_i[idx] = mx_kscale(512)
    return {
        "xT": (n((512, 2048)) * f_d[:, None] * f_i[None, :]).astype(np.float32),
        "W": (0.5 * n((512, 512)) / np.sqrt(512) / f_d[:, None]).astype(np.float32),
        "dg": (n((512, 512))).astype(np.float32),
        "lb": np.tile(n(512), (128, 1)).astype(np.float32),
        "ce": np.tile(uni(0.75, 1.3, 512), (128, 1)).astype(np.float32),
        "tx": np.tile(uni(0.75, 1.3, 2048) / f_i, (128, 1)).astype(np.float32),
        "offs": striped(idx),
    }


def reference(xT, W, dg, lb, ce, tx, offs):
    idx = unstriped(offs)
    xT_i = f64(xT)[:, idx]
    tx_i = f64(tx)[:1][:, idx]
    tc = tx_i.T
    a = mxq(xT_i, 0, "e4m3").T @ mxq(f64(W), 0, "e4m3")
    z = tc * f64(ce)[:1] * a
    m = (z).max(-1, keepdims=True)
    q = np.exp(z - m)
    tot = (q).sum(-1, keepdims=True)
    p = q / tot
    h = f64(dg) + f64(lb)[:1]
    s = (p * h).sum(-1, keepdims=True)
    g = tc * f64(ce)[:1] * p * (h - s)
    out = mxq(xT_i, 1, "e4m3") @ mxq(g, 0, "e5m2")
    return out

@@ -1,0 +1,173 @@
+from contextlib import ExitStack
+
+import concourse.mybir as mybir
+from concourse.masks import make_identity
+
+F32 = mybir.dt.float32
+BF16 = mybir.dt.bfloat16
+U32 = mybir.dt.uint32
+U16 = mybir.dt.uint16
+U8 = mybir.dt.uint8
+E4M3X4 = mybir.dt.float8_e4m3fn_x4
+E5M2X4 = mybir.dt.float8_e5m2_x4
+ALU = mybir.AluOpType
+ACT = mybir.ActivationFunctionType
+AXIS = mybir.AxisListType
+
+P = 128
+PACK = 4
+D, E, SLOTS, TOKENS = 512, 512, 512, 2048
+HALF = E // 2
+G_SPLIT = 192
+
+FLOPS = 2 * 2 * D * E * SLOTS
+
+
+def interleave(copy, dst, src):
+    copy(out=dst.rearrange("p (c i) t -> p c t i", i=PACK), in_=src.rearrange("p t (c i) -> p c t i", i=PACK))
+
+
+def tile_attend_grouter_W_kernel(tc, xT, W, dg, lb, ce, tx, offs, out):
+    nc = tc.nc
+    with ExitStack() as ctx:
+        sb = ctx.enter_context(tc.tile_pool(name="sb", bufs=1))
+        ps = ctx.enter_context(tc.psum_pool(name="ps", bufs=1))
+
+        offsets = sb.tile([P, SLOTS // 16], U16, name="offsets")
+        nc.sync.dma_start(offsets[:], offs)
+
+        x_rows = xT.rearrange("(p t) n -> t p n", t=PACK)
+        planes = [sb.tile([P, TOKENS], F32, name=f"plane{t}") for t in range(PACK)]
+        for t in range(PACK):
+            nc.sync.dma_start(planes[t][:], x_rows[t])
+
+        w_rows = W.rearrange("(p t) e -> p t e", t=PACK)
+        w_raw = [sb.tile([P, PACK, HALF], F32, name=f"w_raw{h}") for h in range(2)]
+        for h in range(2):
+            nc.sync.dma_start(w_raw[h][:], w_rows[:, :, h * HALF : (h + 1) * HALF])
+
+        ce_sb = sb.tile([P, E], F32, name="ce_sb")
+        nc.sync.dma_start(ce_sb[:], ce)
+        lb_sb = sb.tile([P, E], F32, name="lb_sb")
+        nc.sync.dma_start(lb_sb[:], lb)
+        dg_rows = dg.rearrange("(s r) e -> s r e", r=PACK)
+        dg_sb = [sb.tile([P, 2, E], F32, name=f"dg{h}") for h in range(2)]
+        for h in range(2):
+            nc.sync.dma_start(dg_sb[h][:], dg_rows[:, 2 * h : 2 * h + 2, :])
+
+        tx_pool = sb.tile([P, TOKENS], F32, name="tx_pool")
+        nc.vector.memset(tx_pool[:], 0.0)
+        nc.scalar.dma_start(tx_pool[0:1, :], tx[0:1, :])
+
+        ident = sb.tile([P, P], F32, name="ident")
+        make_identity(nc, ident[:])
+
+        tx_row = sb.tile([P, SLOTS], F32, name="tx_row")
+        nc.vector.tensor_copy(tx_row[:], tx_pool[:].indirect(offsets[:]))
+        tx_bank = ps.tile([P, PACK, P], F32, name="tx_bank", tag="bank0")
+        for r in range(PACK):
+            nc.tensor.transpose(tx_bank[:, r, :], tx_row[:, r::PACK], ident[:])
+        tx_col = sb.tile([P, PACK], F32, name="tx_col")
+        nc.scalar.copy(tx_col[:], tx_bank[:, :, 0])
+
+        x_by_d = sb.tile([P, PACK, P, PACK], BF16, name="x_by_d", align_bytes=64)
+        x_words = x_by_d[:].rearrange("p r s t -> p (r s t)").bitcast(F32)
+        x_by_i = sb.tile([P, PACK, P, PACK], BF16, name="x_by_i", align_bytes=64)
+        for u in range(2):
+            for t in (2 * u, 2 * u + 1):
+                nc.vector.tensor_copy(
+                    x_by_d[:, :, :, t].rearrange("p r s -> p s r"), planes[t][:].indirect(offsets[:])
+                )
+            turned = ps.tile([P, PACK, P], F32, name=f"turned{u}", tag=f"bank{1 + u}")
+            for r in range(PACK):
+                nc.tensor.transpose(turned[:, r, :], x_words[:, 2 * P * r + u : 2 * P * (r + 1) : 2], ident[:])
+            halves = turned[:].rearrange("s r p -> s (r p)").bitcast(BF16)
+            nc.scalar.copy(
+                x_by_i[:, 2 * u : 2 * u + 2, :, :], halves.rearrange("s (r p e) -> s e p r", r=PACK, e=2)
+            )
+
+        xd_codes = sb.tile([P, SLOTS], U32, name="xd_codes", align_bytes=64)
+        xd_scales = sb.tile([P, SLOTS], U8, name="xd_scales", align_bytes=64)
+        nc.vector.quantize_mx(
+            out=xd_codes[:].bitcast(E4M3X4), scales=xd_scales[:], in_=x_by_d[:].rearrange("p r s t -> p (r s t)")
+        )
+
+        w_codes = [sb.tile([P, HALF], U32, name=f"w_codes{h}", align_bytes=64) for h in range(2)]
+        w_scales = [sb.tile([P, HALF], U8, name=f"w_scales{h}", align_bytes=64) for h in range(2)]
+        scores = [ps.tile([P, E], F32, name=f"scores{r}", tag=f"bank{4 + r}") for r in range(PACK)]
+        for h in range(2):
+            w_grouped = sb.tile([P, HALF, PACK], BF16, name=f"w_grouped{h}", align_bytes=64)
+            interleave((nc.scalar.copy, nc.vector.tensor_copy)[h], w_grouped[:], w_raw[h][:])
+            nc.vector.quantize_mx(
+                out=w_codes[h][:].bitcast(E4M3X4), scales=w_scales[h][:], in_=w_grouped[:].rearrange("p e t -> p (e t)")
+            )
+            for r in range(PACK):
+                cols = slice(r * P, (r + 1) * P)
+                nc.tensor.matmul_mx(
+                    out=scores[r][:, h * HALF : (h + 1) * HALF],
+                    lhsT=xd_codes[:, cols].bitcast(E4M3X4),
+                    lhsT_scale=xd_scales[:, cols],
+                    rhs=w_codes[h][:].bitcast(E4M3X4),
+                    rhs_scale=w_scales[h][:],
+                    start=True,
+                    stop=True,
+                )
+
+        xi_codes = sb.tile([P, D], U32, name="xi_codes", align_bytes=64)
+        xi_scales = sb.tile([P, D], U8, name="xi_scales", align_bytes=64)
+        nc.vector.quantize_mx(
+            out=xi_codes[:].bitcast(E4M3X4), scales=xi_scales[:], in_=x_by_i[:].rearrange("s t p r -> s (t p r)")
+        )
+
+        def column(name):
+            return [sb.tile([P, 1], F32, name=f"{name}{r}") for r in range(PACK)]
+
+        def rows(name):
+            return [sb.tile([P, E], F32, name=f"{name}{r}") for r in range(PACK)]
+
+        neg_max, total, inv_total, mean_h, factor = (column(n) for n in ("neg_max", "total", "inv", "mean_h", "factor"))
+        hh, z, q, ph, centred = (rows(n) for n in ("h", "z", "q", "ph", "centred"))
+        g_rows = sb.tile([P, PACK, E], BF16, name="g_rows")
+        for r in range(PACK):
+            nc.gpsimd.tensor_tensor(hh[r][:], dg_sb[r // 2][:, r % 2, :], lb_sb[:], ALU.add)
+        for r in range(PACK):
+            nc.vector.scalar_tensor_tensor(z[r][:], scores[r][:], tx_col[:, r : r + 1], ce_sb[:], ALU.mult, ALU.mult)
+            nc.vector.tensor_reduce(neg_max[r][:], z[r][:], AXIS.X, ALU.max, negate=True)
+            nc.scalar.activation(q[r][:], z[r][:], ACT.Exp, bias=neg_max[r][:], accum_out=total[r][:])
+        for r in range(PACK):
+            nc.vector.reciprocal(inv_total[r][:], total[r][:])
+            nc.vector.tensor_tensor(factor[r][:], inv_total[r][:], tx_col[:, r : r + 1], ALU.mult)
+        for r in range(PACK):
+            nc.vector.scalar_tensor_tensor(
+                ph[r][:], q[r][:], inv_total[r][:], hh[r][:], ALU.mult, ALU.mult, accum_out=mean_h[r][:]
+            )
+        for r in range(PACK):
+            nc.vector.scalar_tensor_tensor(centred[r][:], hh[r][:], mean_h[r][:], q[r][:], ALU.subtract, ALU.mult)
+        for r in range(PACK):
+            nc.vector.scalar_tensor_tensor(g_rows[:, r, :], centred[r][:], factor[r][:], ce_sb[:], ALU.mult, ALU.mult)
+
+        g_by_i = sb.tile([P, E, PACK], BF16, name="g_by_i", align_bytes=64)
+        interleave(nc.scalar.copy, g_by_i[:, :G_SPLIT, :], g_rows[:, :, :G_SPLIT])
+        interleave(nc.vector.tensor_copy, g_by_i[:, G_SPLIT:, :], g_rows[:, :, G_SPLIT:])
+        g_codes = sb.tile([P, E], U32, name="g_codes", align_bytes=64)
+        g_scales = sb.tile([P, E], U8, name="g_scales", align_bytes=64)
+        nc.vector.quantize_mx(
+            out=g_codes[:].bitcast(E5M2X4), scales=g_scales[:], in_=g_by_i[:].rearrange("s e r -> s (e r)")
+        )
+
+        out_rows = out.rearrange("(p t) e -> t p e", t=PACK)
+        for t in range(PACK):
+            cols = slice(t * P, (t + 1) * P)
+            acc = ps.tile([P, E], F32, name=f"acc{t}", tag=f"bank{t}")
+            nc.tensor.matmul_mx(
+                out=acc[:],
+                lhsT=xi_codes[:, cols].bitcast(E4M3X4),
+                lhsT_scale=xi_scales[:, cols],
+                rhs=g_codes[:].bitcast(E5M2X4),
+                rhs_scale=g_scales[:],
+                start=True,
+                stop=True,
+            )
+            result = sb.tile([P, E], F32, name=f"result{t}")
+            (nc.vector.tensor_copy, nc.scalar.copy)[t % 2](result[:], acc[:])
+            nc.sync.dma_start(out_rows[t], result[:])

@@ -35,6 +35,12 @@ def tile_attend_grouter_W_kernel(tc, xT, W, dg, lb, ce, tx, offs, out):
 
         offsets = sb.tile([P, SLOTS // 16], U16, name="offsets")
         nc.sync.dma_start(offsets[:], offs)
+        tx_first = sb.tile([1, TOKENS], F32, name="tx_first")
+        nc.sync.dma_start(tx_first[:], tx[0:1, :])
+        vectors = sb.tile([P, P], F32, name="vectors")
+        for half, source in enumerate((ce, lb)):
+            blocks = source.rearrange("k (j e) -> (k j) e", e=P)
+            nc.scalar.dma_start(vectors[half * P // 2 : (half + 1) * P // 2, :], blocks[: P // 2, :])
 
         x_rows = xT.rearrange("(p t) n -> t p n", t=PACK)
         planes = [sb.tile([P, TOKENS], F32, name=f"plane{t}") for t in range(PACK)]
@@ -42,22 +48,18 @@ def tile_attend_grouter_W_kernel(tc, xT, W, dg, lb, ce, tx, offs, out):
             nc.sync.dma_start(planes[t][:], x_rows[t])
 
         w_rows = W.rearrange("(p t) e -> p t e", t=PACK)
-        w_raw = [sb.tile([P, PACK, HALF], F32, name=f"w_raw{h}") for h in range(2)]
+        w_raw = [sb.tile([P, PACK, HALF], F32, name=f"w_raw{h}", tag=f"w_raw{h}", align_bytes=64) for h in range(2)]
         for h in range(2):
             nc.sync.dma_start(w_raw[h][:], w_rows[:, :, h * HALF : (h + 1) * HALF])
 
-        ce_sb = sb.tile([P, E], F32, name="ce_sb")
-        nc.sync.dma_start(ce_sb[:], ce)
-        lb_sb = sb.tile([P, E], F32, name="lb_sb")
-        nc.sync.dma_start(lb_sb[:], lb)
-        dg_rows = dg.rearrange("(s r) e -> s r e", r=PACK)
-        dg_sb = [sb.tile([P, 2, E], F32, name=f"dg{h}") for h in range(2)]
-        for h in range(2):
-            nc.sync.dma_start(dg_sb[h][:], dg_rows[:, 2 * h : 2 * h + 2, :])
+        dg_rows = dg.rearrange("(s r) e -> r s e", r=PACK)
+        dg_sb = [sb.tile([P, E], F32, name=f"dg{r}") for r in range(PACK)]
+        for r in range(PACK):
+            nc.sync.dma_start(dg_sb[r][:], dg_rows[r])
 
         tx_pool = sb.tile([P, TOKENS], F32, name="tx_pool")
         nc.vector.memset(tx_pool[:], 0.0)
-        nc.scalar.dma_start(tx_pool[0:1, :], tx[0:1, :])
+        nc.vector.tensor_copy(tx_pool[0:1, :], tx_first[:])
 
         ident = sb.tile([P, P], F32, name="ident")
         make_identity(nc, ident[:])
@@ -67,13 +69,31 @@ def tile_attend_grouter_W_kernel(tc, xT, W, dg, lb, ce, tx, offs, out):
         tx_bank = ps.tile([P, PACK, P], F32, name="tx_bank", tag="bank0")
         for r in range(PACK):
             nc.tensor.transpose(tx_bank[:, r, :], tx_row[:, r::PACK], ident[:])
-        tx_col = sb.tile([P, PACK], F32, name="tx_col")
-        nc.scalar.copy(tx_col[:], tx_bank[:, :, 0])
+        neg_tx = sb.tile([P, PACK], F32, name="neg_tx")
+        nc.scalar.activation(neg_tx[:], tx_bank[:, :, 0], ACT.Copy, scale=-1.0)
+
+        turned_vectors = ps.tile([P, 2, P // 2], F32, name="turned_vectors", tag="bank3")
+        nc.tensor.transpose(turned_vectors[:].rearrange("e v k -> e (v k)"), vectors[:], ident[:])
+        columns = sb.tile([P, 2, PACK], F32, name="columns")
+        nc.scalar.copy(columns[:], turned_vectors[:, :, :PACK])
+        spread = [ps.tile([P, E], F32, name=f"spread{v}", tag=f"bank{4 + v}") for v in range(2)]
+        for v in range(2):
+            for j in range(PACK):
+                nc.tensor.transpose(
+                    spread[v][:, j * P : (j + 1) * P], columns[:, v, j : j + 1].to_broadcast([P, P]), ident[:]
+                )
+        lb_sb = sb.tile([P, E], F32, name="lb_sb")
+        nc.scalar.copy(lb_sb[:], spread[1][:])
+        neg_scale = sb.tile([P, PACK, E], F32, name="neg_scale")
+        for r in range(PACK):
+            nc.scalar.activation(neg_scale[:, r, :], spread[0][:], ACT.Copy, scale=neg_tx[:, r : r + 1])
 
         x_by_d = sb.tile([P, PACK, P, PACK], BF16, name="x_by_d", align_bytes=64)
         x_words = x_by_d[:].rearrange("p r s t -> p (r s t)").bitcast(F32)
-        x_by_i = sb.tile([P, PACK, P, PACK], BF16, name="x_by_i", align_bytes=64)
-        for u in range(2):
+        xi_codes = sb.tile([P, D], U32, name="xi_codes", align_bytes=64)
+        xi_scales = sb.tile([P, D], U8, name="xi_scales", align_bytes=64)
+
+        def gather_pair(u):
             for t in (2 * u, 2 * u + 1):
                 nc.vector.tensor_copy(
                     x_by_d[:, :, :, t].rearrange("p r s -> p s r"), planes[t][:].indirect(offsets[:])
@@ -81,10 +101,21 @@ def tile_attend_grouter_W_kernel(tc, xT, W, dg, lb, ce, tx, offs, out):
             turned = ps.tile([P, PACK, P], F32, name=f"turned{u}", tag=f"bank{1 + u}")
             for r in range(PACK):
                 nc.tensor.transpose(turned[:, r, :], x_words[:, 2 * P * r + u : 2 * P * (r + 1) : 2], ident[:])
+            return turned
+
+        def quantise_turned(u, turned, tag):
+            x_by_i = sb.tile([P, 2, P, PACK], BF16, name=f"x_by_i{u}", tag=tag, align_bytes=64)
             halves = turned[:].rearrange("s r p -> s (r p)").bitcast(BF16)
-            nc.scalar.copy(
-                x_by_i[:, 2 * u : 2 * u + 2, :, :], halves.rearrange("s (r p e) -> s e p r", r=PACK, e=2)
+            nc.scalar.copy(x_by_i[:], halves.rearrange("s (r p e) -> s e p r", r=PACK, e=2))
+            cols = slice(2 * P * u, 2 * P * (u + 1))
+            nc.vector.quantize_mx(
+                out=xi_codes[:, cols].bitcast(E4M3X4),
+                scales=xi_scales[:, cols],
+                in_=x_by_i[:].rearrange("s t p r -> s (t p r)"),
             )
+
+        quantise_turned(0, gather_pair(0), "x_by_i0")
+        turned_last = gather_pair(1)
 
         xd_codes = sb.tile([P, SLOTS], U32, name="xd_codes", align_bytes=64)
         xd_scales = sb.tile([P, SLOTS], U8, name="xd_scales", align_bytes=64)
@@ -97,7 +128,10 @@ def tile_attend_grouter_W_kernel(tc, xT, W, dg, lb, ce, tx, offs, out):
         scores = [ps.tile([P, E], F32, name=f"scores{r}", tag=f"bank{4 + r}") for r in range(PACK)]
         for h in range(2):
             w_grouped = sb.tile([P, HALF, PACK], BF16, name=f"w_grouped{h}", align_bytes=64)
-            interleave((nc.scalar.copy, nc.vector.tensor_copy)[h], w_grouped[:], w_raw[h][:])
+            cut = (HALF, HALF // 2)[h]
+            interleave(nc.scalar.copy, w_grouped[:, :cut, :], w_raw[h][:, :, :cut])
+            if cut < HALF:
+                interleave(nc.vector.tensor_copy, w_grouped[:, cut:, :], w_raw[h][:, :, cut:])
             nc.vector.quantize_mx(
                 out=w_codes[h][:].bitcast(E4M3X4), scales=w_scales[h][:], in_=w_grouped[:].rearrange("p e t -> p (e t)")
             )
@@ -113,11 +147,7 @@ def tile_attend_grouter_W_kernel(tc, xT, W, dg, lb, ce, tx, offs, out):
                     stop=True,
                 )
 
-        xi_codes = sb.tile([P, D], U32, name="xi_codes", align_bytes=64)
-        xi_scales = sb.tile([P, D], U8, name="xi_scales", align_bytes=64)
-        nc.vector.quantize_mx(
-            out=xi_codes[:].bitcast(E4M3X4), scales=xi_scales[:], in_=x_by_i[:].rearrange("s t p r -> s (t p r)")
-        )
+        quantise_turned(1, turned_last, "w_raw1")
 
         def column(name):
             return [sb.tile([P, 1], F32, name=f"{name}{r}") for r in range(PACK)]
@@ -126,29 +156,34 @@ def tile_attend_grouter_W_kernel(tc, xT, W, dg, lb, ce, tx, offs, out):
             return [sb.tile([P, E], F32, name=f"{name}{r}") for r in range(PACK)]
 
         neg_max, total, inv_total, mean_h, factor = (column(n) for n in ("neg_max", "total", "inv", "mean_h", "factor"))
-        hh, z, q, ph, centred = (rows(n) for n in ("h", "z", "q", "ph", "centred"))
-        g_rows = sb.tile([P, PACK, E], BF16, name="g_rows")
+        hh, neg_z, q, ph = (rows(n) for n in ("h", "neg_z", "q", "ph"))
+        neg_centred = sb.tile([P, PACK, E], F32, name="neg_centred")
         for r in range(PACK):
-            nc.gpsimd.tensor_tensor(hh[r][:], dg_sb[r // 2][:, r % 2, :], lb_sb[:], ALU.add)
+            nc.gpsimd.tensor_tensor(hh[r][:], dg_sb[r][:], lb_sb[:], ALU.add)
         for r in range(PACK):
-            nc.vector.scalar_tensor_tensor(z[r][:], scores[r][:], tx_col[:, r : r + 1], ce_sb[:], ALU.mult, ALU.mult)
-            nc.vector.tensor_reduce(neg_max[r][:], z[r][:], AXIS.X, ALU.max, negate=True)
-            nc.scalar.activation(q[r][:], z[r][:], ACT.Exp, bias=neg_max[r][:], accum_out=total[r][:])
+            nc.vector.tensor_tensor(neg_z[r][:], scores[r][:], neg_scale[:, r, :], ALU.mult)
+            nc.vector.tensor_reduce(neg_max[r][:], neg_z[r][:], AXIS.X, ALU.min)
+            nc.scalar.activation(
+                q[r][:], neg_z[r][:], ACT.Exp, bias=neg_max[r][:], scale=-1.0, accum_out=total[r][:]
+            )
         for r in range(PACK):
             nc.vector.reciprocal(inv_total[r][:], total[r][:])
-            nc.vector.tensor_tensor(factor[r][:], inv_total[r][:], tx_col[:, r : r + 1], ALU.mult)
-        for r in range(PACK):
             nc.vector.scalar_tensor_tensor(
                 ph[r][:], q[r][:], inv_total[r][:], hh[r][:], ALU.mult, ALU.mult, accum_out=mean_h[r][:]
             )
+            nc.scalar.activation(factor[r][:], mean_h[r][:], ACT.Copy, scale=inv_total[r][:])
         for r in range(PACK):
-            nc.vector.scalar_tensor_tensor(centred[r][:], hh[r][:], mean_h[r][:], q[r][:], ALU.subtract, ALU.mult)
-        for r in range(PACK):
-            nc.vector.scalar_tensor_tensor(g_rows[:, r, :], centred[r][:], factor[r][:], ce_sb[:], ALU.mult, ALU.mult)
+            nc.vector.scalar_tensor_tensor(
+                neg_centred[:, r, :], q[r][:], factor[r][:], ph[r][:], ALU.mult, ALU.subtract
+            )
 
         g_by_i = sb.tile([P, E, PACK], BF16, name="g_by_i", align_bytes=64)
-        interleave(nc.scalar.copy, g_by_i[:, :G_SPLIT, :], g_rows[:, :, :G_SPLIT])
-        interleave(nc.vector.tensor_copy, g_by_i[:, G_SPLIT:, :], g_rows[:, :, G_SPLIT:])
+        nc.vector.tensor_tensor(
+            g_by_i[:].rearrange("s (c i) r -> s c r i", i=PACK),
+            neg_centred[:].rearrange("s r (c i) -> s c r i", i=PACK),
+            neg_scale[:].rearrange("s r (c i) -> s c r i", i=PACK),
+            ALU.mult,
+        )
         g_codes = sb.tile([P, E], U32, name="g_codes", align_bytes=64)
         g_scales = sb.tile([P, E], U8, name="g_scales", align_bytes=64)
         nc.vector.quantize_mx(

@@ -12,7 +12,6 @@ E4M3X4 = mybir.dt.float8_e4m3fn_x4
 E5M2X4 = mybir.dt.float8_e5m2_x4
 ALU = mybir.AluOpType
 ACT = mybir.ActivationFunctionType
-AXIS = mybir.AxisListType
 
 P = 128
 PACK = 4
@@ -48,12 +47,12 @@ def tile_attend_grouter_W_kernel(tc, xT, W, dg, lb, ce, tx, offs, out):
             nc.sync.dma_start(planes[t][:], x_rows[t])
 
         w_rows = W.rearrange("(p t) e -> p t e", t=PACK)
-        w_raw = [sb.tile([P, PACK, HALF], F32, name=f"w_raw{h}", tag=f"w_raw{h}", align_bytes=64) for h in range(2)]
+        w_raw = [sb.tile([P, PACK, HALF], F32, name=f"w_raw{h}") for h in range(2)]
         for h in range(2):
             nc.sync.dma_start(w_raw[h][:], w_rows[:, :, h * HALF : (h + 1) * HALF])
 
         dg_rows = dg.rearrange("(s r) e -> r s e", r=PACK)
-        dg_sb = [sb.tile([P, E], F32, name=f"dg{r}") for r in range(PACK)]
+        dg_sb = [sb.tile([P, E], F32, name=f"dg{r}", tag=f"dg{r}", align_bytes=64) for r in range(PACK)]
         for r in range(PACK):
             nc.sync.dma_start(dg_sb[r][:], dg_rows[r])
 
@@ -71,6 +70,8 @@ def tile_attend_grouter_W_kernel(tc, xT, W, dg, lb, ce, tx, offs, out):
             nc.tensor.transpose(tx_bank[:, r, :], tx_row[:, r::PACK], ident[:])
         neg_tx = sb.tile([P, PACK], F32, name="neg_tx")
         nc.scalar.activation(neg_tx[:], tx_bank[:, :, 0], ACT.Copy, scale=-1.0)
+        tx_col = sb.tile([P, PACK], F32, name="tx_col")
+        nc.scalar.copy(tx_col[:], tx_bank[:, :, 0])
 
         turned_vectors = ps.tile([P, 2, P // 2], F32, name="turned_vectors", tag="bank3")
         nc.tensor.transpose(turned_vectors[:].rearrange("e v k -> e (v k)"), vectors[:], ident[:])
@@ -84,70 +85,74 @@ def tile_attend_grouter_W_kernel(tc, xT, W, dg, lb, ce, tx, offs, out):
                 )
         lb_sb = sb.tile([P, E], F32, name="lb_sb")
         nc.scalar.copy(lb_sb[:], spread[1][:])
-        neg_scale = sb.tile([P, PACK, E], F32, name="neg_scale")
+        scale = [sb.tile([P, E], F32, name=f"scale{r}") for r in range(PACK)]
         for r in range(PACK):
-            nc.scalar.activation(neg_scale[:, r, :], spread[0][:], ACT.Copy, scale=neg_tx[:, r : r + 1])
+            nc.scalar.activation(scale[r][:], spread[0][:], ACT.Copy, scale=tx_col[:, r : r + 1])
 
-        x_by_d = sb.tile([P, PACK, P, PACK], BF16, name="x_by_d", align_bytes=64)
-        x_words = x_by_d[:].rearrange("p r s t -> p (r s t)").bitcast(F32)
+        x_by_d = sb.tile([P, SLOTS, PACK], BF16, name="x_by_d", align_bytes=64)
         xi_codes = sb.tile([P, D], U32, name="xi_codes", align_bytes=64)
         xi_scales = sb.tile([P, D], U8, name="xi_scales", align_bytes=64)
 
-        def gather_pair(u):
-            for t in (2 * u, 2 * u + 1):
-                nc.vector.tensor_copy(
-                    x_by_d[:, :, :, t].rearrange("p r s -> p s r"), planes[t][:].indirect(offsets[:])
-                )
-            turned = ps.tile([P, PACK, P], F32, name=f"turned{u}", tag=f"bank{1 + u}")
-            for r in range(PACK):
-                nc.tensor.transpose(turned[:, r, :], x_words[:, 2 * P * r + u : 2 * P * (r + 1) : 2], ident[:])
+        def gather_and_turn(t, picked):
+            nc.vector.tensor_copy(picked, planes[t][:].indirect(offsets[:]))
+            words = picked.bitcast(F32)
+            turned = ps.tile([P, 2, P], F32, name=f"turned{t}", tag=f"bank{1 + t % 2}")
+            for u in range(2):
+                nc.tensor.transpose(turned[:, u, :], words[:, u::2], ident[:])
             return turned
 
-        def quantise_turned(u, turned, tag):
-            x_by_i = sb.tile([P, 2, P, PACK], BF16, name=f"x_by_i{u}", tag=tag, align_bytes=64)
-            halves = turned[:].rearrange("s r p -> s (r p)").bitcast(BF16)
-            nc.scalar.copy(x_by_i[:], halves.rearrange("s (r p e) -> s e p r", r=PACK, e=2))
-            cols = slice(2 * P * u, 2 * P * (u + 1))
+        def quantise_turned(t, turned, tag):
+            x_by_i = sb.tile([P, P, 2], F32, name=f"x_by_i{t}", tag=tag, align_bytes=64)
+            nc.scalar.copy(x_by_i[:], turned[:].rearrange("s u p -> s p u"))
+            cols = slice(P * t, P * (t + 1))
             nc.vector.quantize_mx(
                 out=xi_codes[:, cols].bitcast(E4M3X4),
                 scales=xi_scales[:, cols],
-                in_=x_by_i[:].rearrange("s t p r -> s (t p r)"),
+                in_=x_by_i[:].rearrange("s p u -> s (p u)").bitcast(BF16),
             )
 
-        quantise_turned(0, gather_pair(0), "x_by_i0")
-        turned_last = gather_pair(1)
+        for pair in range(2):
+            picked = sb.tile([P, 2, SLOTS], BF16, name=f"picked{pair}")
+            for e in range(2):
+                t = 2 * pair + e
+                turned = gather_and_turn(t, picked[:, e, :])
+                if t < PACK - 1:
+                    quantise_turned(t, turned, f"x_by_i{t}")
+            interleave(nc.vector.tensor_copy, x_by_d[:, :, 2 * pair : 2 * pair + 2], picked[:])
 
         xd_codes = sb.tile([P, SLOTS], U32, name="xd_codes", align_bytes=64)
         xd_scales = sb.tile([P, SLOTS], U8, name="xd_scales", align_bytes=64)
         nc.vector.quantize_mx(
-            out=xd_codes[:].bitcast(E4M3X4), scales=xd_scales[:], in_=x_by_d[:].rearrange("p r s t -> p (r s t)")
+            out=xd_codes[:].bitcast(E4M3X4), scales=xd_scales[:], in_=x_by_d[:].rearrange("p i t -> p (i t)")
         )
 
-        w_codes = [sb.tile([P, HALF], U32, name=f"w_codes{h}", align_bytes=64) for h in range(2)]
-        w_scales = [sb.tile([P, HALF], U8, name=f"w_scales{h}", align_bytes=64) for h in range(2)]
-        scores = [ps.tile([P, E], F32, name=f"scores{r}", tag=f"bank{4 + r}") for r in range(PACK)]
+        by_expert = [sb.tile([P, PACK, P], F32, name=f"by_expert{j}") for j in range(PACK)]
         for h in range(2):
-            w_grouped = sb.tile([P, HALF, PACK], BF16, name=f"w_grouped{h}", align_bytes=64)
-            cut = (HALF, HALF // 2)[h]
-            interleave(nc.scalar.copy, w_grouped[:, :cut, :], w_raw[h][:, :, :cut])
-            if cut < HALF:
-                interleave(nc.vector.tensor_copy, w_grouped[:, cut:, :], w_raw[h][:, :, cut:])
+            w_grouped = sb.tile([P, HALF, PACK], BF16, name=f"w_grouped{h}", tag=f"w_grouped{h}", align_bytes=64)
+            interleave(nc.scalar.copy, w_grouped[:], w_raw[h][:])
+            w_codes = sb.tile([P, HALF], U32, name=f"w_codes{h}", align_bytes=64)
+            w_scales = sb.tile([P, HALF], U8, name=f"w_scales{h}", align_bytes=64)
             nc.vector.quantize_mx(
-                out=w_codes[h][:].bitcast(E4M3X4), scales=w_scales[h][:], in_=w_grouped[:].rearrange("p e t -> p (e t)")
+                out=w_codes[:].bitcast(E4M3X4), scales=w_scales[:], in_=w_grouped[:].rearrange("p e t -> p (e t)")
             )
-            for r in range(PACK):
-                cols = slice(r * P, (r + 1) * P)
+            for j in (2 * h, 2 * h + 1):
+                cols = slice(j % 2 * P, (j % 2 + 1) * P)
+                a_turned = ps.tile([P, SLOTS], F32, name=f"a_turned{j}", tag=f"bank{4 + j}")
                 nc.tensor.matmul_mx(
-                    out=scores[r][:, h * HALF : (h + 1) * HALF],
-                    lhsT=xd_codes[:, cols].bitcast(E4M3X4),
-                    lhsT_scale=xd_scales[:, cols],
-                    rhs=w_codes[h][:].bitcast(E4M3X4),
-                    rhs_scale=w_scales[h][:],
+                    out=a_turned[:],
+                    lhsT=w_codes[:, cols].bitcast(E4M3X4),
+                    lhsT_scale=w_scales[:, cols],
+                    rhs=xd_codes[:].bitcast(E4M3X4),
+                    rhs_scale=xd_scales[:],
                     start=True,
                     stop=True,
                 )
-
-        quantise_turned(1, turned_last, "w_raw1")
+                nc.scalar.activation(
+                    by_expert[j][:],
+                    a_turned[:].rearrange("e (s r) -> e r s", r=PACK),
+                    ACT.Copy,
+                    scale=columns[:, 0, j : j + 1],
+                )
 
         def column(name):
             return [sb.tile([P, 1], F32, name=f"{name}{r}") for r in range(PACK)]
@@ -155,35 +160,36 @@ def tile_attend_grouter_W_kernel(tc, xT, W, dg, lb, ce, tx, offs, out):
         def rows(name):
             return [sb.tile([P, E], F32, name=f"{name}{r}") for r in range(PACK)]
 
-        neg_max, total, inv_total, mean_h, factor = (column(n) for n in ("neg_max", "total", "inv", "mean_h", "factor"))
-        hh, neg_z, q, ph = (rows(n) for n in ("h", "neg_z", "q", "ph"))
-        neg_centred = sb.tile([P, PACK, E], F32, name="neg_centred")
+        neg_max, total, inv_total, mean_h = (column(n) for n in ("neg_max", "total", "inv", "mean_h"))
+        neg_z, q, ph, centred = (rows(n) for n in ("neg_z", "q", "ph", "centred"))
+        hh = sb.tile([P, PACK, E], F32, name="h", tag="w_grouped1", align_bytes=64)
+        g_rows = sb.tile([P, PACK, E], BF16, name="g_rows")
         for r in range(PACK):
-            nc.gpsimd.tensor_tensor(hh[r][:], dg_sb[r][:], lb_sb[:], ALU.add)
+            nc.vector.tensor_tensor(hh[:, r, :], dg_sb[r][:], lb_sb[:], ALU.add)
+        quantise_turned(PACK - 1, turned, f"dg{PACK - 1}")
         for r in range(PACK):
-            nc.vector.tensor_tensor(neg_z[r][:], scores[r][:], neg_scale[:, r, :], ALU.mult)
-            nc.vector.tensor_reduce(neg_max[r][:], neg_z[r][:], AXIS.X, ALU.min)
+            scores = ps.tile([P, E], F32, name=f"scores{r}", tag=f"bank{6 + r % 2}")
+            for j in range(PACK):
+                nc.tensor.transpose(scores[:, j * P : (j + 1) * P], by_expert[j][:, r, :], ident[:])
+            nc.vector.tensor_scalar(
+                neg_z[r][:], scores[:], neg_tx[:, r : r + 1], None, ALU.mult, ALU.min, accum_out=neg_max[r][:]
+            )
             nc.scalar.activation(
                 q[r][:], neg_z[r][:], ACT.Exp, bias=neg_max[r][:], scale=-1.0, accum_out=total[r][:]
             )
         for r in range(PACK):
             nc.vector.reciprocal(inv_total[r][:], total[r][:])
             nc.vector.scalar_tensor_tensor(
-                ph[r][:], q[r][:], inv_total[r][:], hh[r][:], ALU.mult, ALU.mult, accum_out=mean_h[r][:]
+                ph[r][:], q[r][:], inv_total[r][:], hh[:, r, :], ALU.mult, ALU.mult, accum_out=mean_h[r][:]
             )
-            nc.scalar.activation(factor[r][:], mean_h[r][:], ACT.Copy, scale=inv_total[r][:])
         for r in range(PACK):
-            nc.vector.scalar_tensor_tensor(
-                neg_centred[:, r, :], q[r][:], factor[r][:], ph[r][:], ALU.mult, ALU.subtract
-            )
+            nc.vector.scalar_tensor_tensor(centred[r][:], hh[:, r, :], mean_h[r][:], q[r][:], ALU.subtract, ALU.mult)
+        for r in range(PACK):
+            nc.vector.scalar_tensor_tensor(g_rows[:, r, :], centred[r][:], inv_total[r][:], scale[r][:], ALU.mult, ALU.mult)
 
         g_by_i = sb.tile([P, E, PACK], BF16, name="g_by_i", align_bytes=64)
-        nc.vector.tensor_tensor(
-            g_by_i[:].rearrange("s (c i) r -> s c r i", i=PACK),
-            neg_centred[:].rearrange("s r (c i) -> s c r i", i=PACK),
-            neg_scale[:].rearrange("s r (c i) -> s c r i", i=PACK),
-            ALU.mult,
-        )
+        interleave(nc.scalar.copy, g_by_i[:, :G_SPLIT, :], g_rows[:, :, :G_SPLIT])
+        interleave(nc.vector.tensor_copy, g_by_i[:, G_SPLIT:, :], g_rows[:, :, G_SPLIT:])
         g_codes = sb.tile([P, E], U32, name="g_codes", align_bytes=64)
         g_scales = sb.tile([P, E], U8, name="g_scales", align_bytes=64)
         nc.vector.quantize_mx(
@@ -203,6 +209,10 @@ def tile_attend_grouter_W_kernel(tc, xT, W, dg, lb, ce, tx, offs, out):
                 start=True,
                 stop=True,
             )
-            result = sb.tile([P, E], F32, name=f"result{t}")
-            (nc.vector.tensor_copy, nc.scalar.copy)[t % 2](result[:], acc[:])
-            nc.sync.dma_start(out_rows[t], result[:])
+            copy = (nc.scalar.copy, nc.vector.tensor_copy)[t % 2]
+            pieces = 2 if t == PACK - 1 else 1
+            for piece in range(pieces):
+                part = slice(piece * E // pieces, (piece + 1) * E // pieces)
+                result = sb.tile([P, E // pieces], F32, name=f"result{t}_{piece}")
+                copy(result[:], acc[:, part])
+                nc.sync.dma_start(out_rows[t][:, part], result[:])

@@ -17,7 +17,6 @@ P = 128
 PACK = 4
 D, E, SLOTS, TOKENS = 512, 512, 512, 2048
 HALF = E // 2
-G_SPLIT = 192
 
 FLOPS = 2 * 2 * D * E * SLOTS
 
@@ -70,8 +69,6 @@ def tile_attend_grouter_W_kernel(tc, xT, W, dg, lb, ce, tx, offs, out):
             nc.tensor.transpose(tx_bank[:, r, :], tx_row[:, r::PACK], ident[:])
         neg_tx = sb.tile([P, PACK], F32, name="neg_tx")
         nc.scalar.activation(neg_tx[:], tx_bank[:, :, 0], ACT.Copy, scale=-1.0)
-        tx_col = sb.tile([P, PACK], F32, name="tx_col")
-        nc.scalar.copy(tx_col[:], tx_bank[:, :, 0])
 
         turned_vectors = ps.tile([P, 2, P // 2], F32, name="turned_vectors", tag="bank3")
         nc.tensor.transpose(turned_vectors[:].rearrange("e v k -> e (v k)"), vectors[:], ident[:])
@@ -85,9 +82,9 @@ def tile_attend_grouter_W_kernel(tc, xT, W, dg, lb, ce, tx, offs, out):
                 )
         lb_sb = sb.tile([P, E], F32, name="lb_sb")
         nc.scalar.copy(lb_sb[:], spread[1][:])
-        scale = [sb.tile([P, E], F32, name=f"scale{r}") for r in range(PACK)]
+        neg_scale = sb.tile([P, PACK, E], F32, name="neg_scale")
         for r in range(PACK):
-            nc.scalar.activation(scale[r][:], spread[0][:], ACT.Copy, scale=tx_col[:, r : r + 1])
+            nc.scalar.activation(neg_scale[:, r, :], spread[0][:], ACT.Copy, scale=neg_tx[:, r : r + 1])
 
         x_by_d = sb.tile([P, SLOTS, PACK], BF16, name="x_by_d", align_bytes=64)
         xi_codes = sb.tile([P, D], U32, name="xi_codes", align_bytes=64)
@@ -113,9 +110,9 @@ def tile_attend_grouter_W_kernel(tc, xT, W, dg, lb, ce, tx, offs, out):
 
         for pair in range(2):
             picked = sb.tile([P, 2, SLOTS], BF16, name=f"picked{pair}")
-            for e in range(2):
-                t = 2 * pair + e
-                turned = gather_and_turn(t, picked[:, e, :])
+            for member in range(2):
+                t = 2 * pair + member
+                turned = gather_and_turn(t, picked[:, member, :])
                 if t < PACK - 1:
                     quantise_turned(t, turned, f"x_by_i{t}")
             interleave(nc.vector.tensor_copy, x_by_d[:, :, 2 * pair : 2 * pair + 2], picked[:])
@@ -160,13 +157,17 @@ def tile_attend_grouter_W_kernel(tc, xT, W, dg, lb, ce, tx, offs, out):
         def rows(name):
             return [sb.tile([P, E], F32, name=f"{name}{r}") for r in range(PACK)]
 
-        neg_max, total, inv_total, mean_h = (column(n) for n in ("neg_max", "total", "inv", "mean_h"))
-        neg_z, q, ph, centred = (rows(n) for n in ("neg_z", "q", "ph", "centred"))
-        hh = sb.tile([P, PACK, E], F32, name="h", tag="w_grouped1", align_bytes=64)
-        g_rows = sb.tile([P, PACK, E], BF16, name="g_rows")
+        neg_max, mean_h, factor = (column(n) for n in ("neg_max", "mean_h", "factor"))
+        total = [sb.tile([P, 2], F32, name=f"total{pair}") for pair in range(2)]
+        inv_total = [sb.tile([P, 2], F32, name=f"inv_total{pair}") for pair in range(2)]
+        inv = [inv_total[r // 2][:, r % 2 : r % 2 + 1] for r in range(PACK)]
+        neg_z, q, ph = (rows(n) for n in ("neg_z", "q", "ph"))
+        h_rows = sb.tile([P, PACK, E], F32, name="h", tag="w_grouped1", align_bytes=64)
+        neg_centred = sb.tile([P, PACK, E], F32, name="neg_centred")
         for r in range(PACK):
-            nc.vector.tensor_tensor(hh[:, r, :], dg_sb[r][:], lb_sb[:], ALU.add)
+            nc.vector.tensor_tensor(h_rows[:, r, :], dg_sb[r][:], lb_sb[:], ALU.add)
         quantise_turned(PACK - 1, turned, f"dg{PACK - 1}")
+
         for r in range(PACK):
             scores = ps.tile([P, E], F32, name=f"scores{r}", tag=f"bank{6 + r % 2}")
             for j in range(PACK):
@@ -175,26 +176,42 @@ def tile_attend_grouter_W_kernel(tc, xT, W, dg, lb, ce, tx, offs, out):
                 neg_z[r][:], scores[:], neg_tx[:, r : r + 1], None, ALU.mult, ALU.min, accum_out=neg_max[r][:]
             )
             nc.scalar.activation(
-                q[r][:], neg_z[r][:], ACT.Exp, bias=neg_max[r][:], scale=-1.0, accum_out=total[r][:]
+                q[r][:],
+                neg_z[r][:],
+                ACT.Exp,
+                bias=neg_max[r][:],
+                scale=-1.0,
+                accum_out=total[r // 2][:, r % 2 : r % 2 + 1],
             )
         for r in range(PACK):
-            nc.vector.reciprocal(inv_total[r][:], total[r][:])
+            if r % 2 == 0:
+                nc.vector.reciprocal(inv_total[r // 2][:], total[r // 2][:])
             nc.vector.scalar_tensor_tensor(
-                ph[r][:], q[r][:], inv_total[r][:], hh[:, r, :], ALU.mult, ALU.mult, accum_out=mean_h[r][:]
+                ph[r][:], q[r][:], inv[r], h_rows[:, r, :], ALU.mult, ALU.mult, accum_out=mean_h[r][:]
             )
+            nc.scalar.activation(factor[r][:], mean_h[r][:], ACT.Copy, scale=inv[r])
         for r in range(PACK):
-            nc.vector.scalar_tensor_tensor(centred[r][:], hh[:, r, :], mean_h[r][:], q[r][:], ALU.subtract, ALU.mult)
-        for r in range(PACK):
-            nc.vector.scalar_tensor_tensor(g_rows[:, r, :], centred[r][:], inv_total[r][:], scale[r][:], ALU.mult, ALU.mult)
+            nc.vector.scalar_tensor_tensor(
+                neg_centred[:, r, :], q[r][:], factor[r][:], ph[r][:], ALU.mult, ALU.subtract
+            )
 
-        g_by_i = sb.tile([P, E, PACK], BF16, name="g_by_i", align_bytes=64)
-        interleave(nc.scalar.copy, g_by_i[:, :G_SPLIT, :], g_rows[:, :, :G_SPLIT])
-        interleave(nc.vector.tensor_copy, g_by_i[:, G_SPLIT:, :], g_rows[:, :, G_SPLIT:])
         g_codes = sb.tile([P, E], U32, name="g_codes", align_bytes=64)
         g_scales = sb.tile([P, E], U8, name="g_scales", align_bytes=64)
-        nc.vector.quantize_mx(
-            out=g_codes[:].bitcast(E5M2X4), scales=g_scales[:], in_=g_by_i[:].rearrange("s e r -> s (e r)")
-        )
+        halves = [slice(h * HALF, (h + 1) * HALF) for h in range(2)]
+        g_by_i = [sb.tile([P, HALF, PACK], BF16, name=f"g_by_i{h}", align_bytes=64) for h in range(2)]
+        for h in range(2):
+            nc.vector.tensor_tensor(
+                g_by_i[h][:].rearrange("s (c i) r -> s c r i", i=PACK),
+                neg_centred[:, :, halves[h]].rearrange("s r (c i) -> s c r i", i=PACK),
+                neg_scale[:, :, halves[h]].rearrange("s r (c i) -> s c r i", i=PACK),
+                ALU.mult,
+            )
+        for h in range(2):
+            nc.vector.quantize_mx(
+                out=g_codes[:, halves[h]].bitcast(E5M2X4),
+                scales=g_scales[:, halves[h]],
+                in_=g_by_i[h][:].rearrange("s e r -> s (e r)"),
+            )
 
         out_rows = out.rearrange("(p t) e -> t p e", t=PACK)
         for t in range(PACK):

@@ -41,7 +41,7 @@ def tile_attend_grouter_W_kernel(tc, xT, W, dg, lb, ce, tx, offs, out):
             nc.scalar.dma_start(vectors[half * P // 2 : (half + 1) * P // 2, :], blocks[: P // 2, :])
 
         x_rows = xT.rearrange("(p t) n -> t p n", t=PACK)
-        planes = [sb.tile([P, TOKENS], F32, name=f"plane{t}") for t in range(PACK)]
+        planes = [sb.tile([P, TOKENS], F32, name=f"plane{t}", tag=f"plane{t}", align_bytes=64) for t in range(PACK)]
         for t in range(PACK):
             nc.sync.dma_start(planes[t][:], x_rows[t])
 
@@ -56,19 +56,11 @@ def tile_attend_grouter_W_kernel(tc, xT, W, dg, lb, ce, tx, offs, out):
             nc.sync.dma_start(dg_sb[r][:], dg_rows[r])
 
         tx_pool = sb.tile([P, TOKENS], F32, name="tx_pool")
-        nc.vector.memset(tx_pool[:], 0.0)
+        nc.gpsimd.memset(tx_pool[:], 0.0)
         nc.vector.tensor_copy(tx_pool[0:1, :], tx_first[:])
 
         ident = sb.tile([P, P], F32, name="ident")
         make_identity(nc, ident[:])
-
-        tx_row = sb.tile([P, SLOTS], F32, name="tx_row")
-        nc.vector.tensor_copy(tx_row[:], tx_pool[:].indirect(offsets[:]))
-        tx_bank = ps.tile([P, PACK, P], F32, name="tx_bank", tag="bank0")
-        for r in range(PACK):
-            nc.tensor.transpose(tx_bank[:, r, :], tx_row[:, r::PACK], ident[:])
-        neg_tx = sb.tile([P, PACK], F32, name="neg_tx")
-        nc.scalar.activation(neg_tx[:], tx_bank[:, :, 0], ACT.Copy, scale=-1.0)
 
         turned_vectors = ps.tile([P, 2, P // 2], F32, name="turned_vectors", tag="bank3")
         nc.tensor.transpose(turned_vectors[:].rearrange("e v k -> e (v k)"), vectors[:], ident[:])
@@ -82,74 +74,107 @@ def tile_attend_grouter_W_kernel(tc, xT, W, dg, lb, ce, tx, offs, out):
                 )
         lb_sb = sb.tile([P, E], F32, name="lb_sb")
         nc.scalar.copy(lb_sb[:], spread[1][:])
+
+        tx_row = sb.tile([P, SLOTS], F32, name="tx_row")
+        nc.vector.tensor_copy(tx_row[:], tx_pool[:].indirect(offsets[:]))
+        tx_bank = ps.tile([P, PACK, P], F32, name="tx_bank", tag="bank0")
+        for r in range(PACK):
+            nc.tensor.transpose(tx_bank[:, r, :], tx_row[:, r::PACK], ident[:])
+        neg_tx = sb.tile([P, PACK], F32, name="neg_tx")
+        nc.scalar.activation(neg_tx[:], tx_bank[:, :, 0], ACT.Copy, scale=-1.0)
         neg_scale = sb.tile([P, PACK, E], F32, name="neg_scale")
         for r in range(PACK):
             nc.scalar.activation(neg_scale[:, r, :], spread[0][:], ACT.Copy, scale=neg_tx[:, r : r + 1])
 
-        x_by_d = sb.tile([P, SLOTS, PACK], BF16, name="x_by_d", align_bytes=64)
-        xi_codes = sb.tile([P, D], U32, name="xi_codes", align_bytes=64)
+
+        x_by_d = sb.tile([P, PACK, P, PACK], BF16, name="x_by_d", align_bytes=64)
+        x_words = x_by_d[:].rearrange("p r s t -> p (r s t)").bitcast(F32).rearrange("p (r s u) -> p r s u", r=PACK, u=2)
+        xi_codes = sb.tile([P, D], U32, name="xi_codes", tag="plane2", align_bytes=64)
         xi_scales = sb.tile([P, D], U8, name="xi_scales", align_bytes=64)
 
-        def gather_and_turn(t, picked):
-            nc.vector.tensor_copy(picked, planes[t][:].indirect(offsets[:]))
-            words = picked.bitcast(F32)
-            turned = ps.tile([P, 2, P], F32, name=f"turned{t}", tag=f"bank{1 + t % 2}")
-            for u in range(2):
-                nc.tensor.transpose(turned[:, u, :], words[:, u::2], ident[:])
-            return turned
+        x_by_i = [sb.tile([P, 2, P, PACK], BF16, name=f"x_by_i{u}", align_bytes=64) for u in range(2)]
 
-        def quantise_turned(t, turned, tag):
-            x_by_i = sb.tile([P, P, 2], F32, name=f"x_by_i{t}", tag=tag, align_bytes=64)
-            nc.scalar.copy(x_by_i[:], turned[:].rearrange("s u p -> s p u"))
-            cols = slice(P * t, P * (t + 1))
+        def turn_plane(t, picked):
+            turned = ps.tile([P, 2, P], F32, name=f"turned{t}", tag=f"bank{1 + t}")
+            for u in range(2):
+                nc.tensor.transpose(turned[:, u, :], picked.bitcast(F32)[:, u::2], ident[:])
+            words = x_by_i[0][:, t].rearrange("s p r -> s (p r)").bitcast(F32)
+            nc.scalar.copy(words.rearrange("s (p u) -> s p u", u=2), turned[:].rearrange("s u p -> s p u"))
+
+        def turn_last_pair():
+            turned = ps.tile([P, PACK, P], F32, name="turned_last", tag="bank7")
+            for r in range(PACK):
+                nc.tensor.transpose(turned[:, r, :], x_words[:, r, :, 1], ident[:])
+            values = turned[:].rearrange("s r p -> s (r p)").bitcast(BF16)
+            nc.scalar.copy(x_by_i[1][:], values.rearrange("s (r p t) -> s t p r", r=PACK, t=2))
+
+        def quantise_turned(u):
+            cols = slice(2 * P * u, 2 * P * (u + 1))
             nc.vector.quantize_mx(
                 out=xi_codes[:, cols].bitcast(E4M3X4),
                 scales=xi_scales[:, cols],
-                in_=x_by_i[:].rearrange("s p u -> s (p u)").bitcast(BF16),
+                in_=x_by_i[u][:].rearrange("s t p r -> s (t p r)"),
             )
 
-        for pair in range(2):
-            picked = sb.tile([P, 2, SLOTS], BF16, name=f"picked{pair}")
-            for member in range(2):
-                t = 2 * pair + member
-                turned = gather_and_turn(t, picked[:, member, :])
-                if t < PACK - 1:
-                    quantise_turned(t, turned, f"x_by_i{t}")
-            interleave(nc.vector.tensor_copy, x_by_d[:, :, 2 * pair : 2 * pair + 2], picked[:])
+        picked = sb.tile([P, 2, SLOTS], BF16, name="picked")
+        for t in range(2):
+            nc.vector.tensor_copy(picked[:, t, :], planes[t][:].indirect(offsets[:]))
+            turn_plane(t, picked[:, t, :])
+        nc.vector.tensor_copy(
+            x_by_d[:, :, :, 0:2].rearrange("p r s t -> p s t r"), picked[:].rearrange("p t (s r) -> p s t r", r=PACK)
+        )
+        for t in range(2, PACK):
+            place = x_by_d[:, :, :, t].rearrange("p r s -> p s r")
+            nc.vector.tensor_copy(place, planes[t][:].indirect(offsets[:]))
+            if t == 2:
+                quantise_turned(0)
 
         xd_codes = sb.tile([P, SLOTS], U32, name="xd_codes", align_bytes=64)
         xd_scales = sb.tile([P, SLOTS], U8, name="xd_scales", align_bytes=64)
         nc.vector.quantize_mx(
-            out=xd_codes[:].bitcast(E4M3X4), scales=xd_scales[:], in_=x_by_d[:].rearrange("p i t -> p (i t)")
+            out=xd_codes[:].bitcast(E4M3X4), scales=xd_scales[:], in_=x_by_d[:].rearrange("p r s t -> p (r s t)")
         )
 
-        by_expert = [sb.tile([P, PACK, P], F32, name=f"by_expert{j}") for j in range(PACK)]
+        w_codes = sb.tile([P, E], U32, name="w_codes", align_bytes=64)
+        w_scales = sb.tile([P, E], U8, name="w_scales", align_bytes=64)
+        halves = [slice(h * HALF, (h + 1) * HALF) for h in range(2)]
         for h in range(2):
             w_grouped = sb.tile([P, HALF, PACK], BF16, name=f"w_grouped{h}", tag=f"w_grouped{h}", align_bytes=64)
             interleave(nc.scalar.copy, w_grouped[:], w_raw[h][:])
-            w_codes = sb.tile([P, HALF], U32, name=f"w_codes{h}", align_bytes=64)
-            w_scales = sb.tile([P, HALF], U8, name=f"w_scales{h}", align_bytes=64)
             nc.vector.quantize_mx(
-                out=w_codes[:].bitcast(E4M3X4), scales=w_scales[:], in_=w_grouped[:].rearrange("p e t -> p (e t)")
+                out=w_codes[:, halves[h]].bitcast(E4M3X4),
+                scales=w_scales[:, halves[h]],
+                in_=w_grouped[:].rearrange("p e t -> p (e t)"),
             )
-            for j in (2 * h, 2 * h + 1):
-                cols = slice(j % 2 * P, (j % 2 + 1) * P)
-                a_turned = ps.tile([P, SLOTS], F32, name=f"a_turned{j}", tag=f"bank{4 + j}")
-                nc.tensor.matmul_mx(
-                    out=a_turned[:],
-                    lhsT=w_codes[:, cols].bitcast(E4M3X4),
-                    lhsT_scale=w_scales[:, cols],
-                    rhs=xd_codes[:].bitcast(E4M3X4),
-                    rhs_scale=xd_scales[:],
-                    start=True,
-                    stop=True,
-                )
+
+        scores = [ps.tile([P, E], F32, name=f"scores{r}", tag=f"bank{r}") for r in range(PACK)]
+        a_turned = {}
+        for h in range(2):
+            for pair in range(2):
+                bank = ps.tile([P, 2, HALF], F32, name=f"a_turned{pair}{h}", tag=f"bank{4 + 2 * pair + h}")
+                for k in range(2):
+                    j = 2 * h + k
+                    cols = slice(j * P, (j + 1) * P)
+                    nc.tensor.matmul_mx(
+                        out=bank[:, k, :],
+                        lhsT=w_codes[:, cols].bitcast(E4M3X4),
+                        lhsT_scale=w_scales[:, cols],
+                        rhs=xd_codes[:, halves[pair]].bitcast(E4M3X4),
+                        rhs_scale=xd_scales[:, halves[pair]],
+                        start=True,
+                        stop=True,
+                    )
+                    a_turned[pair, j] = bank[:, k, :]
+        for pair in range(2):
+            for j in range(PACK):
+                by_expert = sb.tile([P, 2, P], F32, name=f"by_expert{pair}{j}")
                 nc.scalar.activation(
-                    by_expert[j][:],
-                    a_turned[:].rearrange("e (s r) -> e r s", r=PACK),
-                    ACT.Copy,
-                    scale=columns[:, 0, j : j + 1],
+                    by_expert[:].rearrange("e r s -> e (r s)"), a_turned[pair, j], ACT.Copy, scale=columns[:, 0, j : j + 1]
                 )
+                for member in range(2):
+                    nc.tensor.transpose(
+                        scores[2 * pair + member][:, j * P : (j + 1) * P], by_expert[:, member, :], ident[:]
+                    )
 
         def column(name):
             return [sb.tile([P, 1], F32, name=f"{name}{r}") for r in range(PACK)]
@@ -162,18 +187,16 @@ def tile_attend_grouter_W_kernel(tc, xT, W, dg, lb, ce, tx, offs, out):
         inv_total = [sb.tile([P, 2], F32, name=f"inv_total{pair}") for pair in range(2)]
         inv = [inv_total[r // 2][:, r % 2 : r % 2 + 1] for r in range(PACK)]
         neg_z, q, ph = (rows(n) for n in ("neg_z", "q", "ph"))
-        h_rows = sb.tile([P, PACK, E], F32, name="h", tag="w_grouped1", align_bytes=64)
+        h_first = sb.tile([P, E], F32, name="h_first", tag="w_grouped0", align_bytes=64)
+        h_rest = sb.tile([P, PACK - 1, E], F32, name="h_rest", tag="w_grouped1", align_bytes=64)
+        h_rows = [h_first[:]] + [h_rest[:, r, :] for r in range(PACK - 1)]
         neg_centred = sb.tile([P, PACK, E], F32, name="neg_centred")
         for r in range(PACK):
-            nc.vector.tensor_tensor(h_rows[:, r, :], dg_sb[r][:], lb_sb[:], ALU.add)
-        quantise_turned(PACK - 1, turned, f"dg{PACK - 1}")
+            nc.vector.tensor_tensor(h_rows[r], dg_sb[r][:], lb_sb[:], ALU.add)
 
         for r in range(PACK):
-            scores = ps.tile([P, E], F32, name=f"scores{r}", tag=f"bank{6 + r % 2}")
-            for j in range(PACK):
-                nc.tensor.transpose(scores[:, j * P : (j + 1) * P], by_expert[j][:, r, :], ident[:])
             nc.vector.tensor_scalar(
-                neg_z[r][:], scores[:], neg_tx[:, r : r + 1], None, ALU.mult, ALU.min, accum_out=neg_max[r][:]
+                neg_z[r][:], scores[r][:], neg_tx[:, r : r + 1], None, ALU.mult, ALU.min, accum_out=neg_max[r][:]
             )
             nc.scalar.activation(
                 q[r][:],
@@ -183,11 +206,12 @@ def tile_attend_grouter_W_kernel(tc, xT, W, dg, lb, ce, tx, offs, out):
                 scale=-1.0,
                 accum_out=total[r // 2][:, r % 2 : r % 2 + 1],
             )
+        turn_last_pair()
         for r in range(PACK):
             if r % 2 == 0:
                 nc.vector.reciprocal(inv_total[r // 2][:], total[r // 2][:])
             nc.vector.scalar_tensor_tensor(
-                ph[r][:], q[r][:], inv[r], h_rows[:, r, :], ALU.mult, ALU.mult, accum_out=mean_h[r][:]
+                ph[r][:], q[r][:], inv[r], h_rows[r], ALU.mult, ALU.mult, accum_out=mean_h[r][:]
             )
             nc.scalar.activation(factor[r][:], mean_h[r][:], ACT.Copy, scale=inv[r])
         for r in range(PACK):
@@ -197,7 +221,6 @@ def tile_attend_grouter_W_kernel(tc, xT, W, dg, lb, ce, tx, offs, out):
 
         g_codes = sb.tile([P, E], U32, name="g_codes", align_bytes=64)
         g_scales = sb.tile([P, E], U8, name="g_scales", align_bytes=64)
-        halves = [slice(h * HALF, (h + 1) * HALF) for h in range(2)]
         g_by_i = [sb.tile([P, HALF, PACK], BF16, name=f"g_by_i{h}", align_bytes=64) for h in range(2)]
         for h in range(2):
             nc.vector.tensor_tensor(
@@ -206,6 +229,7 @@ def tile_attend_grouter_W_kernel(tc, xT, W, dg, lb, ce, tx, offs, out):
                 neg_scale[:, :, halves[h]].rearrange("s r (c i) -> s c r i", i=PACK),
                 ALU.mult,
             )
+        quantise_turned(1)
         for h in range(2):
             nc.vector.quantize_mx(
                 out=g_codes[:, halves[h]].bitcast(E5M2X4),

@@ -46,7 +46,7 @@ def tile_attend_grouter_W_kernel(tc, xT, W, dg, lb, ce, tx, offs, out):
             nc.sync.dma_start(planes[t][:], x_rows[t])
 
         w_rows = W.rearrange("(p t) e -> p t e", t=PACK)
-        w_raw = [sb.tile([P, PACK, HALF], F32, name=f"w_raw{h}") for h in range(2)]
+        w_raw = [sb.tile([P, PACK, HALF], F32, name=f"w_raw{h}", tag=f"w_raw{h}", align_bytes=64) for h in range(2)]
         for h in range(2):
             nc.sync.dma_start(w_raw[h][:], w_rows[:, :, h * HALF : (h + 1) * HALF])
 
@@ -66,14 +66,17 @@ def tile_attend_grouter_W_kernel(tc, xT, W, dg, lb, ce, tx, offs, out):
         nc.tensor.transpose(turned_vectors[:].rearrange("e v k -> e (v k)"), vectors[:], ident[:])
         columns = sb.tile([P, 2, PACK], F32, name="columns")
         nc.scalar.copy(columns[:], turned_vectors[:, :, :PACK])
-        spread = [ps.tile([P, E], F32, name=f"spread{v}", tag=f"bank{4 + v}") for v in range(2)]
+        blocks_spread = ((2, 3), range(PACK))
+        spread = [ps.tile([P, len(blocks_spread[v]) * P], F32, name=f"spread{v}", tag=f"bank{4 + v}") for v in range(2)]
         for v in range(2):
-            for j in range(PACK):
+            for k, j in enumerate(blocks_spread[v]):
                 nc.tensor.transpose(
-                    spread[v][:, j * P : (j + 1) * P], columns[:, v, j : j + 1].to_broadcast([P, P]), ident[:]
+                    spread[v][:, k * P : (k + 1) * P], columns[:, v, j : j + 1].to_broadcast([P, P]), ident[:]
                 )
-        lb_sb = sb.tile([P, E], F32, name="lb_sb")
-        nc.scalar.copy(lb_sb[:], spread[1][:])
+        neg_ce_rows = sb.tile([P, 1, HALF], F32, name="neg_ce_rows")
+        nc.scalar.activation(neg_ce_rows[:, 0, :], spread[0][:], ACT.Copy, scale=-1.0)
+        neg_ce_columns = sb.tile([P, 2], F32, name="neg_ce_columns")
+        nc.scalar.activation(neg_ce_columns[:], columns[:, 0, :2], ACT.Copy, scale=-1.0)
 
         tx_row = sb.tile([P, SLOTS], F32, name="tx_row")
         nc.vector.tensor_copy(tx_row[:], tx_pool[:].indirect(offsets[:]))
@@ -82,9 +85,9 @@ def tile_attend_grouter_W_kernel(tc, xT, W, dg, lb, ce, tx, offs, out):
             nc.tensor.transpose(tx_bank[:, r, :], tx_row[:, r::PACK], ident[:])
         neg_tx = sb.tile([P, PACK], F32, name="neg_tx")
         nc.scalar.activation(neg_tx[:], tx_bank[:, :, 0], ACT.Copy, scale=-1.0)
-        neg_scale = sb.tile([P, PACK, E], F32, name="neg_scale")
+        neg_lb = sb.tile([P, PACK, E], F32, name="neg_lb")
         for r in range(PACK):
-            nc.scalar.activation(neg_scale[:, r, :], spread[0][:], ACT.Copy, scale=neg_tx[:, r : r + 1])
+            nc.scalar.activation(neg_lb[:, r, :], spread[1][:], ACT.Copy, scale=neg_tx[:, r : r + 1])
 
 
         x_by_d = sb.tile([P, PACK, P, PACK], BF16, name="x_by_d", align_bytes=64)
@@ -92,7 +95,10 @@ def tile_attend_grouter_W_kernel(tc, xT, W, dg, lb, ce, tx, offs, out):
         xi_codes = sb.tile([P, D], U32, name="xi_codes", tag="plane2", align_bytes=64)
         xi_scales = sb.tile([P, D], U8, name="xi_scales", align_bytes=64)
 
-        x_by_i = [sb.tile([P, 2, P, PACK], BF16, name=f"x_by_i{u}", align_bytes=64) for u in range(2)]
+        x_by_i = [
+            sb.tile([P, 2, P, PACK], BF16, name=f"x_by_i{u}", tag=tag, align_bytes=64)
+            for u, tag in enumerate(("x_by_i0", "w_raw1"))
+        ]
 
         def turn_plane(t, picked):
             turned = ps.tile([P, 2, P], F32, name=f"turned{t}", tag=f"bank{1 + t}")
@@ -102,7 +108,7 @@ def tile_attend_grouter_W_kernel(tc, xT, W, dg, lb, ce, tx, offs, out):
             nc.scalar.copy(words.rearrange("s (p u) -> s p u", u=2), turned[:].rearrange("s u p -> s p u"))
 
         def turn_last_pair():
-            turned = ps.tile([P, PACK, P], F32, name="turned_last", tag="bank7")
+            turned = ps.tile([P, PACK, P], F32, name="turned_last", tag="bank2")
             for r in range(PACK):
                 nc.tensor.transpose(turned[:, r, :], x_words[:, r, :, 1], ident[:])
             values = turned[:].rearrange("s r p -> s (r p)").bitcast(BF16)
@@ -140,12 +146,18 @@ def tile_attend_grouter_W_kernel(tc, xT, W, dg, lb, ce, tx, offs, out):
         halves = [slice(h * HALF, (h + 1) * HALF) for h in range(2)]
         for h in range(2):
             w_grouped = sb.tile([P, HALF, PACK], BF16, name=f"w_grouped{h}", tag=f"w_grouped{h}", align_bytes=64)
-            interleave(nc.scalar.copy, w_grouped[:], w_raw[h][:])
+            if h == 0:
+                interleave(nc.scalar.copy, w_grouped[:], w_raw[h][:])
+            else:
+                interleave(nc.scalar.copy, w_grouped[:, :P], w_raw[h][:, :, :P])
+                interleave(nc.vector.tensor_copy, w_grouped[:, P:], w_raw[h][:, :, P:])
             nc.vector.quantize_mx(
                 out=w_codes[:, halves[h]].bitcast(E4M3X4),
                 scales=w_scales[:, halves[h]],
                 in_=w_grouped[:].rearrange("p e t -> p (e t)"),
             )
+
+        turn_last_pair()
 
         scores = [ps.tile([P, E], F32, name=f"scores{r}", tag=f"bank{r}") for r in range(PACK)]
         a_turned = {}
@@ -183,54 +195,87 @@ def tile_attend_grouter_W_kernel(tc, xT, W, dg, lb, ce, tx, offs, out):
             return [sb.tile([P, E], F32, name=f"{name}{r}") for r in range(PACK)]
 
         neg_max, mean_h, factor = (column(n) for n in ("neg_max", "mean_h", "factor"))
-        total = [sb.tile([P, 2], F32, name=f"total{pair}") for pair in range(2)]
-        inv_total = [sb.tile([P, 2], F32, name=f"inv_total{pair}") for pair in range(2)]
-        inv = [inv_total[r // 2][:, r % 2 : r % 2 + 1] for r in range(PACK)]
+        total, inv = column("total"), column("inv")
+        neg_inv = column("neg_inv")
         neg_z, q, ph = (rows(n) for n in ("neg_z", "q", "ph"))
         h_first = sb.tile([P, E], F32, name="h_first", tag="w_grouped0", align_bytes=64)
         h_rest = sb.tile([P, PACK - 1, E], F32, name="h_rest", tag="w_grouped1", align_bytes=64)
         h_rows = [h_first[:]] + [h_rest[:, r, :] for r in range(PACK - 1)]
-        neg_centred = sb.tile([P, PACK, E], F32, name="neg_centred")
+        neg_centred = sb.tile([P, PACK, HALF], F32, name="neg_centred")
         for r in range(PACK):
-            nc.vector.tensor_tensor(h_rows[r], dg_sb[r][:], lb_sb[:], ALU.add)
+            nc.vector.scalar_tensor_tensor(
+                h_rows[r], dg_sb[r][:], neg_tx[:, r : r + 1], neg_lb[:, r, :], ALU.mult, ALU.add
+            )
+        quantise_turned(1)
 
-        for r in range(PACK):
+        g_turned = [ps.tile([P, PACK, P], F32, name=f"g_turned{j}", tag=f"bank{4 + j}") for j in range(2)]
+
+        def exponentials(r):
             nc.vector.tensor_scalar(
                 neg_z[r][:], scores[r][:], neg_tx[:, r : r + 1], None, ALU.mult, ALU.min, accum_out=neg_max[r][:]
             )
             nc.scalar.activation(
-                q[r][:],
-                neg_z[r][:],
-                ACT.Exp,
-                bias=neg_max[r][:],
-                scale=-1.0,
-                accum_out=total[r // 2][:, r % 2 : r % 2 + 1],
+                q[r][:], neg_z[r][:], ACT.Exp, bias=neg_max[r][:], scale=-1.0, accum_out=total[r][:]
             )
-        turn_last_pair()
-        for r in range(PACK):
-            if r % 2 == 0:
-                nc.vector.reciprocal(inv_total[r // 2][:], total[r // 2][:])
+
+        def inverse(r):
+            nc.vector.reciprocal(inv[r][:], total[r][:])
+
+        def weighted_sum(r):
             nc.vector.scalar_tensor_tensor(
-                ph[r][:], q[r][:], inv[r], h_rows[r], ALU.mult, ALU.mult, accum_out=mean_h[r][:]
+                ph[r][:], q[r][:], inv[r][:], h_rows[r], ALU.mult, ALU.mult, accum_out=mean_h[r][:]
             )
-            nc.scalar.activation(factor[r][:], mean_h[r][:], ACT.Copy, scale=inv[r])
+            nc.scalar.activation(neg_inv[r][:], inv[r][:], ACT.Copy, scale=-1.0)
+            nc.scalar.activation(factor[r][:], mean_h[r][:], ACT.Copy, scale=neg_inv[r][:])
+            scaled_q = sb.tile([P, HALF], F32, name=f"scaled_q{r}")
+            nc.scalar.activation(scaled_q[:], q[r][:, halves[0]], ACT.Copy, scale=factor[r][:])
+            for term, source in enumerate((ph[r], scaled_q)):
+                for j in range(2):
+                    nc.tensor.matmul(
+                        g_turned[j][:, r, :],
+                        source[:, j * P : (j + 1) * P],
+                        ident[:],
+                        is_transpose=True,
+                        start=term == 0,
+                        stop=term == 1,
+                    )
+
+        for step in range(PACK + 3):
+            for stage, lag in ((exponentials, 0), (inverse, 2), (weighted_sum, 3)):
+                if 0 <= step - lag < PACK:
+                    stage(step - lag)
         for r in range(PACK):
             nc.vector.scalar_tensor_tensor(
-                neg_centred[:, r, :], q[r][:], factor[r][:], ph[r][:], ALU.mult, ALU.subtract
+                neg_centred[:, r, :], q[r][:, halves[1]], factor[r][:], ph[r][:, halves[1]], ALU.mult, ALU.add
             )
 
         g_codes = sb.tile([P, E], U32, name="g_codes", align_bytes=64)
         g_scales = sb.tile([P, E], U8, name="g_scales", align_bytes=64)
         g_by_i = [sb.tile([P, HALF, PACK], BF16, name=f"g_by_i{h}", align_bytes=64) for h in range(2)]
-        for h in range(2):
-            nc.vector.tensor_tensor(
-                g_by_i[h][:].rearrange("s (c i) r -> s c r i", i=PACK),
-                neg_centred[:, :, halves[h]].rearrange("s r (c i) -> s c r i", i=PACK),
-                neg_scale[:, :, halves[h]].rearrange("s r (c i) -> s c r i", i=PACK),
-                ALU.mult,
+        nc.vector.tensor_tensor(
+            g_by_i[1][:].rearrange("s (c i) r -> s c r i", i=PACK),
+            neg_centred[:].rearrange("s r (c i) -> s c r i", i=PACK),
+            neg_ce_rows[:].to_broadcast([P, PACK, HALF]).rearrange("s r (c i) -> s c r i", i=PACK),
+            ALU.mult,
+        )
+        g_words = g_by_i[0][:].rearrange("s e r -> s (e r)").bitcast(F32).rearrange("s (j e u) -> s j e u", j=2, u=2)
+        by_expert_pairs = []
+        for j in range(2):
+            pairs = sb.tile([P, 2, P, 2], BF16, name=f"g_pairs{j}")
+            nc.scalar.activation(
+                pairs[:],
+                g_turned[j][:].rearrange("e (u k) s -> e u s k", k=2),
+                ACT.Copy,
+                scale=neg_ce_columns[:, j : j + 1],
             )
-        quantise_turned(1)
-        for h in range(2):
+            by_expert_pairs.append(pairs)
+        for j in range(2):
+            words = by_expert_pairs[j][:].rearrange("e u s k -> e (u s k)").bitcast(F32)
+            back = ps.tile([P, 2, P], F32, name=f"g_back{j}", tag=f"bank{6 + j}")
+            for u in range(2):
+                nc.tensor.transpose(back[:, u, :], words[:, u * P : (u + 1) * P], ident[:])
+            (nc.scalar.copy, nc.vector.tensor_copy)[j](g_words[:, j], back[:].rearrange("s u e -> s e u"))
+        for h in (1, 0):
             nc.vector.quantize_mx(
                 out=g_codes[:, halves[h]].bitcast(E5M2X4),
                 scales=g_scales[:, halves[h]],

@@ -35,10 +35,12 @@ def tile_attend_grouter_W_kernel(tc, xT, W, dg, lb, ce, tx, offs, out):
         nc.sync.dma_start(offsets[:], offs)
         tx_first = sb.tile([1, TOKENS], F32, name="tx_first")
         nc.sync.dma_start(tx_first[:], tx[0:1, :])
+        vector_rows = sb.tile([2 * PACK, P], F32, name="vector_rows")
+        for v, source in enumerate((ce, lb)):
+            nc.scalar.dma_start(vector_rows[v * PACK : (v + 1) * PACK, :], source[0].rearrange("(j e) -> j e", e=P))
         vectors = sb.tile([P, P], F32, name="vectors")
-        for half, source in enumerate((ce, lb)):
-            blocks = source.rearrange("k (j e) -> (k j) e", e=P)
-            nc.scalar.dma_start(vectors[half * P // 2 : (half + 1) * P // 2, :], blocks[: P // 2, :])
+        nc.vector.memset(vectors[:], 0.0)
+        nc.vector.tensor_copy(vectors[: 2 * PACK, :], vector_rows[:])
 
         x_rows = xT.rearrange("(p t) n -> t p n", t=PACK)
         planes = [sb.tile([P, TOKENS], F32, name=f"plane{t}", tag=f"plane{t}", align_bytes=64) for t in range(PACK)]
@@ -50,10 +52,10 @@ def tile_attend_grouter_W_kernel(tc, xT, W, dg, lb, ce, tx, offs, out):
         for h in range(2):
             nc.sync.dma_start(w_raw[h][:], w_rows[:, :, h * HALF : (h + 1) * HALF])
 
-        dg_rows = dg.rearrange("(s r) e -> r s e", r=PACK)
-        dg_sb = [sb.tile([P, E], F32, name=f"dg{r}", tag=f"dg{r}", align_bytes=64) for r in range(PACK)]
-        for r in range(PACK):
-            nc.sync.dma_start(dg_sb[r][:], dg_rows[r])
+        dg_rows = dg.rearrange("(s r) e -> s r e", r=PACK)
+        dg_sb = [sb.tile([P, 2, E], F32, name=f"dg{pair}") for pair in range(2)]
+        for pair in range(2):
+            nc.sync.dma_start(dg_sb[pair][:], dg_rows[:, 2 * pair : 2 * pair + 2, :])
 
         tx_pool = sb.tile([P, TOKENS], F32, name="tx_pool")
         nc.gpsimd.memset(tx_pool[:], 0.0)
@@ -62,10 +64,10 @@ def tile_attend_grouter_W_kernel(tc, xT, W, dg, lb, ce, tx, offs, out):
         ident = sb.tile([P, P], F32, name="ident")
         make_identity(nc, ident[:])
 
-        turned_vectors = ps.tile([P, 2, P // 2], F32, name="turned_vectors", tag="bank3")
-        nc.tensor.transpose(turned_vectors[:].rearrange("e v k -> e (v k)"), vectors[:], ident[:])
+        turned_vectors = ps.tile([P, P], F32, name="turned_vectors", tag="bank3")
+        nc.tensor.transpose(turned_vectors[:], vectors[:], ident[:])
         columns = sb.tile([P, 2, PACK], F32, name="columns")
-        nc.scalar.copy(columns[:], turned_vectors[:, :, :PACK])
+        nc.scalar.copy(columns[:].rearrange("e v j -> e (v j)"), turned_vectors[:, : 2 * PACK])
         blocks_spread = ((2, 3), range(PACK))
         spread = [ps.tile([P, len(blocks_spread[v]) * P], F32, name=f"spread{v}", tag=f"bank{4 + v}") for v in range(2)]
         for v in range(2):
@@ -204,7 +206,7 @@ def tile_attend_grouter_W_kernel(tc, xT, W, dg, lb, ce, tx, offs, out):
         neg_centred = sb.tile([P, PACK, HALF], F32, name="neg_centred")
         for r in range(PACK):
             nc.vector.scalar_tensor_tensor(
-                h_rows[r], dg_sb[r][:], neg_tx[:, r : r + 1], neg_lb[:, r, :], ALU.mult, ALU.add
+                h_rows[r], dg_sb[r // 2][:, r % 2, :], neg_tx[:, r : r + 1], neg_lb[:, r, :], ALU.mult, ALU.add
             )
         quantise_turned(1)
 
@@ -249,8 +251,10 @@ def tile_attend_grouter_W_kernel(tc, xT, W, dg, lb, ce, tx, offs, out):
                 neg_centred[:, r, :], q[r][:, halves[1]], factor[r][:], ph[r][:, halves[1]], ALU.mult, ALU.add
             )
 
-        g_codes = sb.tile([P, E], U32, name="g_codes", align_bytes=64)
-        g_scales = sb.tile([P, E], U8, name="g_scales", align_bytes=64)
+        g_codes = sb.tile([P, 3, HALF], U32, name="g_codes", align_bytes=64)
+        g_scales = sb.tile([P, 3, HALF], U8, name="g_scales", align_bytes=64)
+        nc.gpsimd.memset(g_codes[:, 2, :], 0)
+        nc.gpsimd.memset(g_scales[:, 2, :], 0)
         g_by_i = [sb.tile([P, HALF, PACK], BF16, name=f"g_by_i{h}", align_bytes=64) for h in range(2)]
         nc.vector.tensor_tensor(
             g_by_i[1][:].rearrange("s (c i) r -> s c r i", i=PACK),
@@ -275,30 +279,43 @@ def tile_attend_grouter_W_kernel(tc, xT, W, dg, lb, ce, tx, offs, out):
             for u in range(2):
                 nc.tensor.transpose(back[:, u, :], words[:, u * P : (u + 1) * P], ident[:])
             (nc.scalar.copy, nc.vector.tensor_copy)[j](g_words[:, j], back[:].rearrange("s u e -> s e u"))
-        for h in (1, 0):
+        out_rows = out.rearrange("(p t) e -> t p e", t=PACK)
+
+        def quantise_g(h):
             nc.vector.quantize_mx(
-                out=g_codes[:, halves[h]].bitcast(E5M2X4),
-                scales=g_scales[:, halves[h]],
+                out=g_codes[:, h, :].bitcast(E5M2X4),
+                scales=g_scales[:, h, :],
                 in_=g_by_i[h][:].rearrange("s e r -> s (e r)"),
             )
 
-        out_rows = out.rearrange("(p t) e -> t p e", t=PACK)
-        for t in range(PACK):
+        def product(t, first, bank):
             cols = slice(t * P, (t + 1) * P)
-            acc = ps.tile([P, E], F32, name=f"acc{t}", tag=f"bank{t}")
+            acc = ps.tile([P, 2, HALF], F32, name=f"acc{t}_{first}", tag=f"bank{bank}")
             nc.tensor.matmul_mx(
-                out=acc[:],
+                out=acc[:].rearrange("d k e -> d (k e)"),
                 lhsT=xi_codes[:, cols].bitcast(E4M3X4),
                 lhsT_scale=xi_scales[:, cols],
-                rhs=g_codes[:].bitcast(E5M2X4),
-                rhs_scale=g_scales[:],
+                rhs=g_codes[:, first : first + 2, :].rearrange("s k e -> s (k e)").bitcast(E5M2X4),
+                rhs_scale=g_scales[:, first : first + 2, :].rearrange("s k e -> s (k e)"),
                 start=True,
                 stop=True,
             )
+            return acc
+
+        def store(t, h, source, copy):
+            result = sb.tile([P, HALF], F32, name=f"result{t}_{h}")
+            copy(result[:], source)
+            nc.sync.dma_start(out_rows[t][:, halves[h]], result[:])
+
+        quantise_g(1)
+        for t in range(2):
+            store(t, 1, product(t, 1, t)[:, 0, :], nc.scalar.copy)
+        quantise_g(0)
+        store(0, 0, product(0, 0, 4)[:, 0, :], nc.vector.tensor_copy)
+        for t in (2, 3):
+            acc = product(t, 0, t)
+            result = sb.tile([P, E], F32, name=f"result{t}")
             copy = (nc.scalar.copy, nc.vector.tensor_copy)[t % 2]
-            pieces = 2 if t == PACK - 1 else 1
-            for piece in range(pieces):
-                part = slice(piece * E // pieces, (piece + 1) * E // pieces)
-                result = sb.tile([P, E // pieces], F32, name=f"result{t}_{piece}")
-                copy(result[:], acc[:, part])
-                nc.sync.dma_start(out_rows[t][:, part], result[:])
+            copy(result[:], acc[:].rearrange("d k e -> d (k e)"))
+            nc.sync.dma_start(out_rows[t], result[:])
+        store(1, 0, product(1, 0, 5)[:, 0, :], nc.scalar.copy)

@@ -39,8 +39,8 @@ def tile_attend_grouter_W_kernel(tc, xT, W, dg, lb, ce, tx, offs, out):
         for v, source in enumerate((ce, lb)):
             nc.scalar.dma_start(vector_rows[v * PACK : (v + 1) * PACK, :], source[0].rearrange("(j e) -> j e", e=P))
         vectors = sb.tile([P, P], F32, name="vectors")
-        nc.vector.memset(vectors[:], 0.0)
-        nc.vector.tensor_copy(vectors[: 2 * PACK, :], vector_rows[:])
+        nc.gpsimd.memset(vectors[:], 0.0)
+        nc.gpsimd.tensor_copy(vectors[: 2 * PACK, :], vector_rows[:])
 
         x_rows = xT.rearrange("(p t) n -> t p n", t=PACK)
         planes = [sb.tile([P, TOKENS], F32, name=f"plane{t}", tag=f"plane{t}", align_bytes=64) for t in range(PACK)]
@@ -52,10 +52,10 @@ def tile_attend_grouter_W_kernel(tc, xT, W, dg, lb, ce, tx, offs, out):
         for h in range(2):
             nc.sync.dma_start(w_raw[h][:], w_rows[:, :, h * HALF : (h + 1) * HALF])
 
-        dg_rows = dg.rearrange("(s r) e -> s r e", r=PACK)
-        dg_sb = [sb.tile([P, 2, E], F32, name=f"dg{pair}") for pair in range(2)]
-        for pair in range(2):
-            nc.sync.dma_start(dg_sb[pair][:], dg_rows[:, 2 * pair : 2 * pair + 2, :])
+        dg_rows = dg.rearrange("(s r) e -> r s e", r=PACK)
+        dg_sb = [sb.tile([P, E], F32, name=f"dg{r}") for r in range(PACK)]
+        for r in range(PACK):
+            nc.sync.dma_start(dg_sb[r][:], dg_rows[r])
 
         tx_pool = sb.tile([P, TOKENS], F32, name="tx_pool")
         nc.gpsimd.memset(tx_pool[:], 0.0)
@@ -94,9 +94,6 @@ def tile_attend_grouter_W_kernel(tc, xT, W, dg, lb, ce, tx, offs, out):
 
         x_by_d = sb.tile([P, PACK, P, PACK], BF16, name="x_by_d", align_bytes=64)
         x_words = x_by_d[:].rearrange("p r s t -> p (r s t)").bitcast(F32).rearrange("p (r s u) -> p r s u", r=PACK, u=2)
-        xi_codes = sb.tile([P, D], U32, name="xi_codes", tag="plane2", align_bytes=64)
-        xi_scales = sb.tile([P, D], U8, name="xi_scales", align_bytes=64)
-
         x_by_i = [
             sb.tile([P, 2, P, PACK], BF16, name=f"x_by_i{u}", tag=tag, align_bytes=64)
             for u, tag in enumerate(("x_by_i0", "w_raw1"))
@@ -134,8 +131,6 @@ def tile_attend_grouter_W_kernel(tc, xT, W, dg, lb, ce, tx, offs, out):
         for t in range(2, PACK):
             place = x_by_d[:, :, :, t].rearrange("p r s -> p s r")
             nc.vector.tensor_copy(place, planes[t][:].indirect(offsets[:]))
-            if t == 2:
-                quantise_turned(0)
 
         xd_codes = sb.tile([P, SLOTS], U32, name="xd_codes", align_bytes=64)
         xd_scales = sb.tile([P, SLOTS], U8, name="xd_scales", align_bytes=64)
@@ -200,15 +195,13 @@ def tile_attend_grouter_W_kernel(tc, xT, W, dg, lb, ce, tx, offs, out):
         total, inv = column("total"), column("inv")
         neg_inv = column("neg_inv")
         neg_z, q, ph = (rows(n) for n in ("neg_z", "q", "ph"))
-        h_first = sb.tile([P, E], F32, name="h_first", tag="w_grouped0", align_bytes=64)
-        h_rest = sb.tile([P, PACK - 1, E], F32, name="h_rest", tag="w_grouped1", align_bytes=64)
-        h_rows = [h_first[:]] + [h_rest[:, r, :] for r in range(PACK - 1)]
-        neg_centred = sb.tile([P, PACK, HALF], F32, name="neg_centred")
+        h_tile = sb.tile([P, PACK, E], F32, name="h", tag="w_grouped1", align_bytes=64)
+        h_rows = [h_tile[:, r, :] for r in range(PACK)]
+        neg_centred = sb.tile([P, PACK, HALF], F32, name="neg_centred", tag="neg_centred", align_bytes=64)
         for r in range(PACK):
             nc.vector.scalar_tensor_tensor(
-                h_rows[r], dg_sb[r // 2][:, r % 2, :], neg_tx[:, r : r + 1], neg_lb[:, r, :], ALU.mult, ALU.add
+                h_rows[r], dg_sb[r][:], neg_tx[:, r : r + 1], neg_lb[:, r, :], ALU.mult, ALU.add
             )
-        quantise_turned(1)
 
         g_turned = [ps.tile([P, PACK, P], F32, name=f"g_turned{j}", tag=f"bank{4 + j}") for j in range(2)]
 
@@ -251,10 +244,8 @@ def tile_attend_grouter_W_kernel(tc, xT, W, dg, lb, ce, tx, offs, out):
                 neg_centred[:, r, :], q[r][:, halves[1]], factor[r][:], ph[r][:, halves[1]], ALU.mult, ALU.add
             )
 
-        g_codes = sb.tile([P, 3, HALF], U32, name="g_codes", align_bytes=64)
-        g_scales = sb.tile([P, 3, HALF], U8, name="g_scales", align_bytes=64)
-        nc.gpsimd.memset(g_codes[:, 2, :], 0)
-        nc.gpsimd.memset(g_scales[:, 2, :], 0)
+        g_codes = sb.tile([P, E], U32, name="g_codes", align_bytes=64)
+        g_scales = sb.tile([P, E], U8, name="g_scales", align_bytes=64)
         g_by_i = [sb.tile([P, HALF, PACK], BF16, name=f"g_by_i{h}", align_bytes=64) for h in range(2)]
         nc.vector.tensor_tensor(
             g_by_i[1][:].rearrange("s (c i) r -> s c r i", i=PACK),
@@ -262,6 +253,10 @@ def tile_attend_grouter_W_kernel(tc, xT, W, dg, lb, ce, tx, offs, out):
             neg_ce_rows[:].to_broadcast([P, PACK, HALF]).rearrange("s r (c i) -> s c r i", i=PACK),
             ALU.mult,
         )
+        xi_codes = sb.tile([P, D], U32, name="xi_codes", tag="neg_centred", align_bytes=64)
+        xi_scales = sb.tile([P, D], U8, name="xi_scales", align_bytes=64)
+        for u in range(2):
+            quantise_turned(u)
         g_words = g_by_i[0][:].rearrange("s e r -> s (e r)").bitcast(F32).rearrange("s (j e u) -> s j e u", j=2, u=2)
         by_expert_pairs = []
         for j in range(2):
@@ -279,43 +274,30 @@ def tile_attend_grouter_W_kernel(tc, xT, W, dg, lb, ce, tx, offs, out):
             for u in range(2):
                 nc.tensor.transpose(back[:, u, :], words[:, u * P : (u + 1) * P], ident[:])
             (nc.scalar.copy, nc.vector.tensor_copy)[j](g_words[:, j], back[:].rearrange("s u e -> s e u"))
-        out_rows = out.rearrange("(p t) e -> t p e", t=PACK)
-
-        def quantise_g(h):
+        for h in (1, 0):
             nc.vector.quantize_mx(
-                out=g_codes[:, h, :].bitcast(E5M2X4),
-                scales=g_scales[:, h, :],
+                out=g_codes[:, halves[h]].bitcast(E5M2X4),
+                scales=g_scales[:, halves[h]],
                 in_=g_by_i[h][:].rearrange("s e r -> s (e r)"),
             )
 
-        def product(t, first, bank):
+        out_rows = out.rearrange("(p t) e -> t p e", t=PACK)
+        for t in range(PACK):
             cols = slice(t * P, (t + 1) * P)
-            acc = ps.tile([P, 2, HALF], F32, name=f"acc{t}_{first}", tag=f"bank{bank}")
+            acc = ps.tile([P, E], F32, name=f"acc{t}", tag=f"bank{t}")
             nc.tensor.matmul_mx(
-                out=acc[:].rearrange("d k e -> d (k e)"),
+                out=acc[:],
                 lhsT=xi_codes[:, cols].bitcast(E4M3X4),
                 lhsT_scale=xi_scales[:, cols],
-                rhs=g_codes[:, first : first + 2, :].rearrange("s k e -> s (k e)").bitcast(E5M2X4),
-                rhs_scale=g_scales[:, first : first + 2, :].rearrange("s k e -> s (k e)"),
+                rhs=g_codes[:].bitcast(E5M2X4),
+                rhs_scale=g_scales[:],
                 start=True,
                 stop=True,
             )
-            return acc
-
-        def store(t, h, source, copy):
-            result = sb.tile([P, HALF], F32, name=f"result{t}_{h}")
-            copy(result[:], source)
-            nc.sync.dma_start(out_rows[t][:, halves[h]], result[:])
-
-        quantise_g(1)
-        for t in range(2):
-            store(t, 1, product(t, 1, t)[:, 0, :], nc.scalar.copy)
-        quantise_g(0)
-        store(0, 0, product(0, 0, 4)[:, 0, :], nc.vector.tensor_copy)
-        for t in (2, 3):
-            acc = product(t, 0, t)
-            result = sb.tile([P, E], F32, name=f"result{t}")
             copy = (nc.scalar.copy, nc.vector.tensor_copy)[t % 2]
-            copy(result[:], acc[:].rearrange("d k e -> d (k e)"))
-            nc.sync.dma_start(out_rows[t], result[:])
-        store(1, 0, product(1, 0, 5)[:, 0, :], nc.scalar.copy)
+            pieces = 2 if t == PACK - 1 else 1
+            for piece in range(pieces):
+                part = slice(piece * E // pieces, (piece + 1) * E // pieces)
+                result = sb.tile([P, E // pieces], F32, name=f"result{t}_{piece}")
+                copy(result[:], acc[:, part])
+                nc.sync.dma_start(out_rows[t][:, part], result[:])

@@ -94,6 +94,8 @@ def tile_attend_grouter_W_kernel(tc, xT, W, dg, lb, ce, tx, offs, out):
 
         x_by_d = sb.tile([P, PACK, P, PACK], BF16, name="x_by_d", align_bytes=64)
         x_words = x_by_d[:].rearrange("p r s t -> p (r s t)").bitcast(F32).rearrange("p (r s u) -> p r s u", r=PACK, u=2)
+        xi_codes = sb.tile([P, D], U32, name="xi_codes", tag="plane2", align_bytes=64)
+        xi_scales = sb.tile([P, D], U8, name="xi_scales", align_bytes=64)
         x_by_i = [
             sb.tile([P, 2, P, PACK], BF16, name=f"x_by_i{u}", tag=tag, align_bytes=64)
             for u, tag in enumerate(("x_by_i0", "w_raw1"))
@@ -131,6 +133,8 @@ def tile_attend_grouter_W_kernel(tc, xT, W, dg, lb, ce, tx, offs, out):
         for t in range(2, PACK):
             place = x_by_d[:, :, :, t].rearrange("p r s -> p s r")
             nc.vector.tensor_copy(place, planes[t][:].indirect(offsets[:]))
+            if t == 2:
+                quantise_turned(0)
 
         xd_codes = sb.tile([P, SLOTS], U32, name="xd_codes", align_bytes=64)
         xd_scales = sb.tile([P, SLOTS], U8, name="xd_scales", align_bytes=64)
@@ -192,18 +196,22 @@ def tile_attend_grouter_W_kernel(tc, xT, W, dg, lb, ce, tx, offs, out):
             return [sb.tile([P, E], F32, name=f"{name}{r}") for r in range(PACK)]
 
         neg_max, mean_h, factor = (column(n) for n in ("neg_max", "mean_h", "factor"))
-        total, inv = column("total"), column("inv")
-        neg_inv = column("neg_inv")
+        total = column("total")
+        inv = sb.tile([P, PACK], F32, name="inv")
         neg_z, q, ph = (rows(n) for n in ("neg_z", "q", "ph"))
         h_tile = sb.tile([P, PACK, E], F32, name="h", tag="w_grouped1", align_bytes=64)
         h_rows = [h_tile[:, r, :] for r in range(PACK)]
-        neg_centred = sb.tile([P, PACK, HALF], F32, name="neg_centred", tag="neg_centred", align_bytes=64)
+        neg_centred = sb.tile([P, PACK, HALF], F32, name="neg_centred")
         for r in range(PACK):
             nc.vector.scalar_tensor_tensor(
                 h_rows[r], dg_sb[r][:], neg_tx[:, r : r + 1], neg_lb[:, r, :], ALU.mult, ALU.add
             )
+        quantise_turned(1)
 
-        g_turned = [ps.tile([P, PACK, P], F32, name=f"g_turned{j}", tag=f"bank{4 + j}") for j in range(2)]
+        g_turned = [
+            [ps.tile([P, 2, P], F32, name=f"g_turned{u}{j}", tag=f"bank{4 + 2 * u + j}") for j in range(2)]
+            for u in range(2)
+        ]
 
         def exponentials(r):
             nc.vector.tensor_scalar(
@@ -214,20 +222,24 @@ def tile_attend_grouter_W_kernel(tc, xT, W, dg, lb, ce, tx, offs, out):
             )
 
         def inverse(r):
-            nc.vector.reciprocal(inv[r][:], total[r][:])
+            nc.vector.reciprocal(inv[:, r : r + 1], total[r][:])
 
         def weighted_sum(r):
             nc.vector.scalar_tensor_tensor(
-                ph[r][:], q[r][:], inv[r][:], h_rows[r], ALU.mult, ALU.mult, accum_out=mean_h[r][:]
+                ph[r][:], q[r][:], inv[:, r : r + 1], h_rows[r], ALU.mult, ALU.mult, accum_out=mean_h[r][:]
             )
-            nc.scalar.activation(neg_inv[r][:], inv[r][:], ACT.Copy, scale=-1.0)
-            nc.scalar.activation(factor[r][:], mean_h[r][:], ACT.Copy, scale=neg_inv[r][:])
+
+        def centre_turned(r):
+            nc.vector.tensor_scalar(factor[r][:], mean_h[r][:], inv[:, r : r + 1], -1.0, ALU.mult, ALU.mult)
             scaled_q = sb.tile([P, HALF], F32, name=f"scaled_q{r}")
-            nc.scalar.activation(scaled_q[:], q[r][:, halves[0]], ACT.Copy, scale=factor[r][:])
+            pieces = 2 if r == PACK - 1 else 1
+            for piece in range(pieces):
+                part = slice(piece * HALF // pieces, (piece + 1) * HALF // pieces)
+                nc.scalar.activation(scaled_q[:, part], q[r][:, part], ACT.Copy, scale=factor[r][:])
             for term, source in enumerate((ph[r], scaled_q)):
                 for j in range(2):
                     nc.tensor.matmul(
-                        g_turned[j][:, r, :],
+                        g_turned[r // 2][j][:, r % 2, :],
                         source[:, j * P : (j + 1) * P],
                         ident[:],
                         is_transpose=True,
@@ -235,8 +247,8 @@ def tile_attend_grouter_W_kernel(tc, xT, W, dg, lb, ce, tx, offs, out):
                         stop=term == 1,
                     )
 
-        for step in range(PACK + 3):
-            for stage, lag in ((exponentials, 0), (inverse, 2), (weighted_sum, 3)):
+        for step in range(PACK + 4):
+            for stage, lag in ((exponentials, 0), (inverse, 2), (centre_turned, 4), (weighted_sum, 3)):
                 if 0 <= step - lag < PACK:
                     stage(step - lag)
         for r in range(PACK):
@@ -253,38 +265,30 @@ def tile_attend_grouter_W_kernel(tc, xT, W, dg, lb, ce, tx, offs, out):
             neg_ce_rows[:].to_broadcast([P, PACK, HALF]).rearrange("s r (c i) -> s c r i", i=PACK),
             ALU.mult,
         )
-        xi_codes = sb.tile([P, D], U32, name="xi_codes", tag="neg_centred", align_bytes=64)
-        xi_scales = sb.tile([P, D], U8, name="xi_scales", align_bytes=64)
-        for u in range(2):
-            quantise_turned(u)
         g_words = g_by_i[0][:].rearrange("s e r -> s (e r)").bitcast(F32).rearrange("s (j e u) -> s j e u", j=2, u=2)
-        by_expert_pairs = []
+        back = [ps.tile([P, 2, P], F32, name=f"g_back{j}", tag=f"bank{j}") for j in range(2)]
+        for u in range(2):
+            for j in range(2):
+                pairs = sb.tile([P, P, 2], BF16, name=f"g_pairs{u}{j}")
+                nc.scalar.activation(
+                    pairs[:], g_turned[u][j][:].rearrange("e k s -> e s k"), ACT.Copy, scale=neg_ce_columns[:, j : j + 1]
+                )
+                words = pairs[:].rearrange("e s k -> e (s k)").bitcast(F32)
+                nc.tensor.transpose(back[j][:, u, :], words, ident[:])
         for j in range(2):
-            pairs = sb.tile([P, 2, P, 2], BF16, name=f"g_pairs{j}")
-            nc.scalar.activation(
-                pairs[:],
-                g_turned[j][:].rearrange("e (u k) s -> e u s k", k=2),
-                ACT.Copy,
-                scale=neg_ce_columns[:, j : j + 1],
-            )
-            by_expert_pairs.append(pairs)
-        for j in range(2):
-            words = by_expert_pairs[j][:].rearrange("e u s k -> e (u s k)").bitcast(F32)
-            back = ps.tile([P, 2, P], F32, name=f"g_back{j}", tag=f"bank{6 + j}")
-            for u in range(2):
-                nc.tensor.transpose(back[:, u, :], words[:, u * P : (u + 1) * P], ident[:])
-            (nc.scalar.copy, nc.vector.tensor_copy)[j](g_words[:, j], back[:].rearrange("s u e -> s e u"))
-        for h in (1, 0):
+            nc.scalar.copy(g_words[:, j], back[j][:].rearrange("s u e -> s e u"))
+        for h, part in ((1, slice(0, HALF)), (0, slice(0, P)), (0, slice(P, HALF))):
+            cols = slice(h * HALF + part.start, h * HALF + part.stop)
             nc.vector.quantize_mx(
-                out=g_codes[:, halves[h]].bitcast(E5M2X4),
-                scales=g_scales[:, halves[h]],
-                in_=g_by_i[h][:].rearrange("s e r -> s (e r)"),
+                out=g_codes[:, cols].bitcast(E5M2X4),
+                scales=g_scales[:, cols],
+                in_=g_by_i[h][:, part].rearrange("s e r -> s (e r)"),
             )
 
         out_rows = out.rearrange("(p t) e -> t p e", t=PACK)
         for t in range(PACK):
             cols = slice(t * P, (t + 1) * P)
-            acc = ps.tile([P, E], F32, name=f"acc{t}", tag=f"bank{t}")
+            acc = ps.tile([P, E], F32, name=f"acc{t}", tag=f"bank{2 + t}")
             nc.tensor.matmul_mx(
                 out=acc[:],
                 lhsT=xi_codes[:, cols].bitcast(E4M3X4),
@@ -295,7 +299,7 @@ def tile_attend_grouter_W_kernel(tc, xT, W, dg, lb, ce, tx, offs, out):
                 stop=True,
             )
             copy = (nc.scalar.copy, nc.vector.tensor_copy)[t % 2]
-            pieces = 2 if t == PACK - 1 else 1
+            pieces = 2 if t in (0, PACK - 1) else 1
             for piece in range(pieces):
                 part = slice(piece * E // pieces, (piece + 1) * E // pieces)
                 result = sb.tile([P, E // pieces], F32, name=f"result{t}_{piece}")

@@ -68,10 +68,10 @@ def tile_attend_grouter_W_kernel(tc, xT, W, dg, lb, ce, tx, offs, out):
         nc.tensor.transpose(turned_vectors[:], vectors[:], ident[:])
         columns = sb.tile([P, 2, PACK], F32, name="columns")
         nc.scalar.copy(columns[:].rearrange("e v j -> e (v j)"), turned_vectors[:, : 2 * PACK])
-        blocks_spread = ((2, 3), range(PACK))
-        spread = [ps.tile([P, len(blocks_spread[v]) * P], F32, name=f"spread{v}", tag=f"bank{4 + v}") for v in range(2)]
+        spread_blocks = ((2, 3), range(PACK))
+        spread = [ps.tile([P, len(spread_blocks[v]) * P], F32, name=f"spread{v}", tag=f"bank{4 + v}") for v in range(2)]
         for v in range(2):
-            for k, j in enumerate(blocks_spread[v]):
+            for k, j in enumerate(spread_blocks[v]):
                 nc.tensor.transpose(
                     spread[v][:, k * P : (k + 1) * P], columns[:, v, j : j + 1].to_broadcast([P, P]), ident[:]
                 )
@@ -91,35 +91,35 @@ def tile_attend_grouter_W_kernel(tc, xT, W, dg, lb, ce, tx, offs, out):
         for r in range(PACK):
             nc.scalar.activation(neg_lb[:, r, :], spread[1][:], ACT.Copy, scale=neg_tx[:, r : r + 1])
 
-
         x_by_d = sb.tile([P, PACK, P, PACK], BF16, name="x_by_d", align_bytes=64)
-        x_words = x_by_d[:].rearrange("p r s t -> p (r s t)").bitcast(F32).rearrange("p (r s u) -> p r s u", r=PACK, u=2)
-        xi_codes = sb.tile([P, D], U32, name="xi_codes", tag="plane2", align_bytes=64)
-        xi_scales = sb.tile([P, D], U8, name="xi_scales", align_bytes=64)
+        x_flat = x_by_d[:].rearrange("p r s t -> p (r s t)")
+        xi_codes, xi_scales = [], []
         x_by_i = [
             sb.tile([P, 2, P, PACK], BF16, name=f"x_by_i{u}", tag=tag, align_bytes=64)
             for u, tag in enumerate(("x_by_i0", "w_raw1"))
         ]
 
-        def turn_plane(t, picked):
+        def turn_plane(t, gathered):
             turned = ps.tile([P, 2, P], F32, name=f"turned{t}", tag=f"bank{1 + t}")
-            for u in range(2):
-                nc.tensor.transpose(turned[:, u, :], picked.bitcast(F32)[:, u::2], ident[:])
+            for w in range(2):
+                nc.tensor.transpose(turned[:, w, :], gathered.bitcast(F32)[:, w::2], ident[:])
             words = x_by_i[0][:, t].rearrange("s p r -> s (p r)").bitcast(F32)
-            nc.scalar.copy(words.rearrange("s (p u) -> s p u", u=2), turned[:].rearrange("s u p -> s p u"))
+            nc.scalar.copy(words.rearrange("s (p w) -> s p w", w=2), turned[:].rearrange("s w p -> s p w"))
 
-        def turn_last_pair():
+        def turn_last_planes():
+            words = x_flat.bitcast(F32).rearrange("p (r s u) -> p r s u", r=PACK, u=2)
             turned = ps.tile([P, PACK, P], F32, name="turned_last", tag="bank2")
             for r in range(PACK):
-                nc.tensor.transpose(turned[:, r, :], x_words[:, r, :, 1], ident[:])
+                nc.tensor.transpose(turned[:, r, :], words[:, r, :, 1], ident[:])
             values = turned[:].rearrange("s r p -> s (r p)").bitcast(BF16)
             nc.scalar.copy(x_by_i[1][:], values.rearrange("s (r p t) -> s t p r", r=PACK, t=2))
 
-        def quantise_turned(u):
-            cols = slice(2 * P * u, 2 * P * (u + 1))
+        def quantise_turned(u, tag):
+            xi_codes.append(sb.tile([P, 2, P], U32, name=f"xi_codes{u}", tag=tag, align_bytes=64))
+            xi_scales.append(sb.tile([P, 2, P], U8, name=f"xi_scales{u}", align_bytes=64))
             nc.vector.quantize_mx(
-                out=xi_codes[:, cols].bitcast(E4M3X4),
-                scales=xi_scales[:, cols],
+                out=xi_codes[u][:].rearrange("s t p -> s (t p)").bitcast(E4M3X4),
+                scales=xi_scales[u][:].rearrange("s t p -> s (t p)"),
                 in_=x_by_i[u][:].rearrange("s t p r -> s (t p r)"),
             )
 
@@ -134,13 +134,11 @@ def tile_attend_grouter_W_kernel(tc, xT, W, dg, lb, ce, tx, offs, out):
             place = x_by_d[:, :, :, t].rearrange("p r s -> p s r")
             nc.vector.tensor_copy(place, planes[t][:].indirect(offsets[:]))
             if t == 2:
-                quantise_turned(0)
+                quantise_turned(0, "plane2")
 
         xd_codes = sb.tile([P, SLOTS], U32, name="xd_codes", align_bytes=64)
         xd_scales = sb.tile([P, SLOTS], U8, name="xd_scales", align_bytes=64)
-        nc.vector.quantize_mx(
-            out=xd_codes[:].bitcast(E4M3X4), scales=xd_scales[:], in_=x_by_d[:].rearrange("p r s t -> p (r s t)")
-        )
+        nc.vector.quantize_mx(out=xd_codes[:].bitcast(E4M3X4), scales=xd_scales[:], in_=x_flat)
 
         w_codes = sb.tile([P, E], U32, name="w_codes", align_bytes=64)
         w_scales = sb.tile([P, E], U8, name="w_scales", align_bytes=64)
@@ -158,13 +156,14 @@ def tile_attend_grouter_W_kernel(tc, xT, W, dg, lb, ce, tx, offs, out):
                 in_=w_grouped[:].rearrange("p e t -> p (e t)"),
             )
 
-        turn_last_pair()
+        turn_last_planes()
 
         scores = [ps.tile([P, E], F32, name=f"scores{r}", tag=f"bank{r}") for r in range(PACK)]
         a_turned = {}
         for h in range(2):
             for pair in range(2):
-                bank = ps.tile([P, 2, HALF], F32, name=f"a_turned{pair}{h}", tag=f"bank{4 + 2 * pair + h}")
+                pair_slots = slice(2 * P * pair, 2 * P * (pair + 1))
+                bank = ps.tile([P, 2, 2 * P], F32, name=f"a_turned{pair}{h}", tag=f"bank{4 + 2 * pair + h}")
                 for k in range(2):
                     j = 2 * h + k
                     cols = slice(j * P, (j + 1) * P)
@@ -172,8 +171,8 @@ def tile_attend_grouter_W_kernel(tc, xT, W, dg, lb, ce, tx, offs, out):
                         out=bank[:, k, :],
                         lhsT=w_codes[:, cols].bitcast(E4M3X4),
                         lhsT_scale=w_scales[:, cols],
-                        rhs=xd_codes[:, halves[pair]].bitcast(E4M3X4),
-                        rhs_scale=xd_scales[:, halves[pair]],
+                        rhs=xd_codes[:, pair_slots].bitcast(E4M3X4),
+                        rhs_scale=xd_scales[:, pair_slots],
                         start=True,
                         stop=True,
                     )
@@ -181,8 +180,9 @@ def tile_attend_grouter_W_kernel(tc, xT, W, dg, lb, ce, tx, offs, out):
         for pair in range(2):
             for j in range(PACK):
                 by_expert = sb.tile([P, 2, P], F32, name=f"by_expert{pair}{j}")
+                ce_column = columns[:, 0, j : j + 1]
                 nc.scalar.activation(
-                    by_expert[:].rearrange("e r s -> e (r s)"), a_turned[pair, j], ACT.Copy, scale=columns[:, 0, j : j + 1]
+                    by_expert[:].rearrange("e r s -> e (r s)"), a_turned[pair, j], ACT.Copy, scale=ce_column
                 )
                 for member in range(2):
                     nc.tensor.transpose(
@@ -195,22 +195,19 @@ def tile_attend_grouter_W_kernel(tc, xT, W, dg, lb, ce, tx, offs, out):
         def rows(name):
             return [sb.tile([P, E], F32, name=f"{name}{r}") for r in range(PACK)]
 
-        neg_max, mean_h, factor = (column(n) for n in ("neg_max", "mean_h", "factor"))
-        total = column("total")
-        inv = sb.tile([P, PACK], F32, name="inv")
-        neg_z, q, ph = (rows(n) for n in ("neg_z", "q", "ph"))
-        h_tile = sb.tile([P, PACK, E], F32, name="h", tag="w_grouped1", align_bytes=64)
-        h_rows = [h_tile[:, r, :] for r in range(PACK)]
-        neg_centred = sb.tile([P, PACK, HALF], F32, name="neg_centred")
+        neg_max, neg_s, factor, total = (column(n) for n in ("neg_max", "neg_s", "factor", "total"))
+        inv_total = sb.tile([P, PACK], F32, name="inv_total")
+        neg_z, q, neg_ph = (rows(n) for n in ("neg_z", "q", "neg_ph"))
+        neg_h = sb.tile([P, PACK, E], F32, name="neg_h", tag="w_grouped1", align_bytes=64)
+        neg_centred = sb.tile([P, PACK, HALF], F32, name="neg_centred", tag="neg_centred", align_bytes=64)
         for r in range(PACK):
             nc.vector.scalar_tensor_tensor(
-                h_rows[r], dg_sb[r][:], neg_tx[:, r : r + 1], neg_lb[:, r, :], ALU.mult, ALU.add
+                neg_h[:, r, :], dg_sb[r][:], neg_tx[:, r : r + 1], neg_lb[:, r, :], ALU.mult, ALU.add
             )
-        quantise_turned(1)
 
-        g_turned = [
-            [ps.tile([P, 2, P], F32, name=f"g_turned{u}{j}", tag=f"bank{4 + 2 * u + j}") for j in range(2)]
-            for u in range(2)
+        centred_turned = [
+            [ps.tile([P, 2, P], F32, name=f"centred{pair}{j}", tag=f"bank{4 + 2 * pair + j}") for j in range(2)]
+            for pair in range(2)
         ]
 
         def exponentials(r):
@@ -222,24 +219,24 @@ def tile_attend_grouter_W_kernel(tc, xT, W, dg, lb, ce, tx, offs, out):
             )
 
         def inverse(r):
-            nc.vector.reciprocal(inv[:, r : r + 1], total[r][:])
+            nc.vector.reciprocal(inv_total[:, r : r + 1], total[r][:])
 
         def weighted_sum(r):
             nc.vector.scalar_tensor_tensor(
-                ph[r][:], q[r][:], inv[:, r : r + 1], h_rows[r], ALU.mult, ALU.mult, accum_out=mean_h[r][:]
+                neg_ph[r][:], q[r][:], inv_total[:, r : r + 1], neg_h[:, r, :], ALU.mult, ALU.mult, accum_out=neg_s[r][:]
             )
 
         def centre_turned(r):
-            nc.vector.tensor_scalar(factor[r][:], mean_h[r][:], inv[:, r : r + 1], -1.0, ALU.mult, ALU.mult)
+            nc.vector.tensor_scalar(factor[r][:], neg_s[r][:], inv_total[:, r : r + 1], -1.0, ALU.mult, ALU.mult)
             scaled_q = sb.tile([P, HALF], F32, name=f"scaled_q{r}")
             pieces = 2 if r == PACK - 1 else 1
             for piece in range(pieces):
                 part = slice(piece * HALF // pieces, (piece + 1) * HALF // pieces)
                 nc.scalar.activation(scaled_q[:, part], q[r][:, part], ACT.Copy, scale=factor[r][:])
-            for term, source in enumerate((ph[r], scaled_q)):
+            for term, source in enumerate((neg_ph[r], scaled_q)):
                 for j in range(2):
                     nc.tensor.matmul(
-                        g_turned[r // 2][j][:, r % 2, :],
+                        centred_turned[r // 2][j][:, r % 2, :],
                         source[:, j * P : (j + 1) * P],
                         ident[:],
                         is_transpose=True,
@@ -247,15 +244,16 @@ def tile_attend_grouter_W_kernel(tc, xT, W, dg, lb, ce, tx, offs, out):
                         stop=term == 1,
                     )
 
-        for step in range(PACK + 4):
-            for stage, lag in ((exponentials, 0), (inverse, 2), (centre_turned, 4), (weighted_sum, 3)):
+        stages = ((exponentials, 0), (inverse, 2), (centre_turned, 4), (weighted_sum, 3))
+        for step in range(PACK + max(lag for stage, lag in stages)):
+            for stage, lag in stages:
                 if 0 <= step - lag < PACK:
                     stage(step - lag)
+
         for r in range(PACK):
             nc.vector.scalar_tensor_tensor(
-                neg_centred[:, r, :], q[r][:, halves[1]], factor[r][:], ph[r][:, halves[1]], ALU.mult, ALU.add
+                neg_centred[:, r, :], q[r][:, halves[1]], factor[r][:], neg_ph[r][:, halves[1]], ALU.mult, ALU.add
             )
-
         g_codes = sb.tile([P, E], U32, name="g_codes", align_bytes=64)
         g_scales = sb.tile([P, E], U8, name="g_scales", align_bytes=64)
         g_by_i = [sb.tile([P, HALF, PACK], BF16, name=f"g_by_i{h}", align_bytes=64) for h in range(2)]
@@ -265,18 +263,23 @@ def tile_attend_grouter_W_kernel(tc, xT, W, dg, lb, ce, tx, offs, out):
             neg_ce_rows[:].to_broadcast([P, PACK, HALF]).rearrange("s r (c i) -> s c r i", i=PACK),
             ALU.mult,
         )
-        g_words = g_by_i[0][:].rearrange("s e r -> s (e r)").bitcast(F32).rearrange("s (j e u) -> s j e u", j=2, u=2)
+        quantise_turned(1, "neg_centred")
+
+        g_words = g_by_i[0][:].rearrange("s e r -> s (e r)").bitcast(F32).rearrange("s (j e w) -> s j e w", j=2, w=2)
         back = [ps.tile([P, 2, P], F32, name=f"g_back{j}", tag=f"bank{j}") for j in range(2)]
-        for u in range(2):
+        for pair in range(2):
             for j in range(2):
-                pairs = sb.tile([P, P, 2], BF16, name=f"g_pairs{u}{j}")
+                g_turned = sb.tile([P, P, 2], BF16, name=f"g_turned{pair}{j}")
                 nc.scalar.activation(
-                    pairs[:], g_turned[u][j][:].rearrange("e k s -> e s k"), ACT.Copy, scale=neg_ce_columns[:, j : j + 1]
+                    g_turned[:],
+                    centred_turned[pair][j][:].rearrange("e k s -> e s k"),
+                    ACT.Copy,
+                    scale=neg_ce_columns[:, j : j + 1],
                 )
-                words = pairs[:].rearrange("e s k -> e (s k)").bitcast(F32)
-                nc.tensor.transpose(back[j][:, u, :], words, ident[:])
+                words = g_turned[:].rearrange("e s k -> e (s k)").bitcast(F32)
+                nc.tensor.transpose(back[j][:, pair, :], words, ident[:])
         for j in range(2):
-            nc.scalar.copy(g_words[:, j], back[j][:].rearrange("s u e -> s e u"))
+            nc.scalar.copy(g_words[:, j], back[j][:].rearrange("s w e -> s e w"))
         for h, part in ((1, slice(0, HALF)), (0, slice(0, P)), (0, slice(P, HALF))):
             cols = slice(h * HALF + part.start, h * HALF + part.stop)
             nc.vector.quantize_mx(
@@ -287,12 +290,11 @@ def tile_attend_grouter_W_kernel(tc, xT, W, dg, lb, ce, tx, offs, out):
 
         out_rows = out.rearrange("(p t) e -> t p e", t=PACK)
         for t in range(PACK):
-            cols = slice(t * P, (t + 1) * P)
             acc = ps.tile([P, E], F32, name=f"acc{t}", tag=f"bank{2 + t}")
             nc.tensor.matmul_mx(
                 out=acc[:],
-                lhsT=xi_codes[:, cols].bitcast(E4M3X4),
-                lhsT_scale=xi_scales[:, cols],
+                lhsT=xi_codes[t // 2][:, t % 2, :].bitcast(E4M3X4),
+                lhsT_scale=xi_scales[t // 2][:, t % 2, :],
                 rhs=g_codes[:].bitcast(E5M2X4),
                 rhs_scale=g_scales[:],
                 start=True,

@@ -17,6 +17,7 @@ P = 128
 PACK = 4
 D, E, SLOTS, TOKENS = 512, 512, 512, 2048
 HALF = E // 2
+SCALAR_W = 96
 
 FLOPS = 2 * 2 * D * E * SLOTS
 
@@ -31,20 +32,21 @@ def tile_attend_grouter_W_kernel(tc, xT, W, dg, lb, ce, tx, offs, out):
         sb = ctx.enter_context(tc.tile_pool(name="sb", bufs=1))
         ps = ctx.enter_context(tc.psum_pool(name="ps", bufs=1))
 
-        offsets = sb.tile([P, SLOTS // 16], U16, name="offsets")
-        nc.sync.dma_start(offsets[:], offs)
-        tx_first = sb.tile([1, TOKENS], F32, name="tx_first")
-        nc.sync.dma_start(tx_first[:], tx[0:1, :])
-        vector_rows = sb.tile([2 * PACK, P], F32, name="vector_rows")
-        for v, source in enumerate((ce, lb)):
-            nc.scalar.dma_start(vector_rows[v * PACK : (v + 1) * PACK, :], source[0].rearrange("(j e) -> j e", e=P))
         vectors = sb.tile([P, P], F32, name="vectors")
         nc.gpsimd.memset(vectors[:], 0.0)
-        nc.gpsimd.tensor_copy(vectors[: 2 * PACK, :], vector_rows[:])
+        ident = sb.tile([P, P], F32, name="ident")
+        make_identity(nc, ident[:])
 
+        offsets = sb.tile([P, SLOTS // 16], U16, name="offsets")
+        nc.sync.dma_start(offsets[:], offs)
+        tx_first = sb.tile([1, TOKENS], F32, name="tx_first", tag="tx_first")
+        nc.sync.dma_start(tx_first[:], tx[0:1, :])
         x_rows = xT.rearrange("(p t) n -> t p n", t=PACK)
         planes = [sb.tile([P, TOKENS], F32, name=f"plane{t}", tag=f"plane{t}", align_bytes=64) for t in range(PACK)]
-        for t in range(PACK):
+        nc.sync.dma_start(planes[0][:], x_rows[0])
+        for v, source in enumerate((ce, lb)):
+            nc.sync.dma_start(vectors[v * PACK : (v + 1) * PACK, :], source[0].rearrange("(j e) -> j e", e=P))
+        for t in range(1, PACK):
             nc.sync.dma_start(planes[t][:], x_rows[t])
 
         w_rows = W.rearrange("(p t) e -> p t e", t=PACK)
@@ -53,16 +55,13 @@ def tile_attend_grouter_W_kernel(tc, xT, W, dg, lb, ce, tx, offs, out):
             nc.sync.dma_start(w_raw[h][:], w_rows[:, :, h * HALF : (h + 1) * HALF])
 
         dg_rows = dg.rearrange("(s r) e -> r s e", r=PACK)
-        dg_sb = [sb.tile([P, E], F32, name=f"dg{r}") for r in range(PACK)]
+        dg_sb = [sb.tile([P, E], F32, name=f"dg{r}", tag=f"dg{r}", align_bytes=64) for r in range(PACK)]
         for r in range(PACK):
             nc.sync.dma_start(dg_sb[r][:], dg_rows[r])
 
         tx_pool = sb.tile([P, TOKENS], F32, name="tx_pool")
-        nc.gpsimd.memset(tx_pool[:], 0.0)
+        nc.vector.memset(tx_pool[:], 0.0)
         nc.vector.tensor_copy(tx_pool[0:1, :], tx_first[:])
-
-        ident = sb.tile([P, P], F32, name="ident")
-        make_identity(nc, ident[:])
 
         turned_vectors = ps.tile([P, P], F32, name="turned_vectors", tag="bank3")
         nc.tensor.transpose(turned_vectors[:], vectors[:], ident[:])
@@ -75,66 +74,64 @@ def tile_attend_grouter_W_kernel(tc, xT, W, dg, lb, ce, tx, offs, out):
                 nc.tensor.transpose(
                     spread[v][:, k * P : (k + 1) * P], columns[:, v, j : j + 1].to_broadcast([P, P]), ident[:]
                 )
-        neg_ce_rows = sb.tile([P, 1, HALF], F32, name="neg_ce_rows")
+        neg_ce_rows = sb.tile([P, 1, HALF], F32, name="neg_ce_rows", tag="neg_ce_rows", align_bytes=64)
         nc.scalar.activation(neg_ce_rows[:, 0, :], spread[0][:], ACT.Copy, scale=-1.0)
         neg_ce_columns = sb.tile([P, 2], F32, name="neg_ce_columns")
         nc.scalar.activation(neg_ce_columns[:], columns[:, 0, :2], ACT.Copy, scale=-1.0)
 
         tx_row = sb.tile([P, SLOTS], F32, name="tx_row")
         nc.vector.tensor_copy(tx_row[:], tx_pool[:].indirect(offsets[:]))
-        tx_bank = ps.tile([P, PACK, P], F32, name="tx_bank", tag="bank0")
+        tx_bank = ps.tile([P, PACK, P], F32, name="tx_bank", tag="bank3")
         for r in range(PACK):
             nc.tensor.transpose(tx_bank[:, r, :], tx_row[:, r::PACK], ident[:])
         neg_tx = sb.tile([P, PACK], F32, name="neg_tx")
         nc.scalar.activation(neg_tx[:], tx_bank[:, :, 0], ACT.Copy, scale=-1.0)
-        neg_lb = sb.tile([P, PACK, E], F32, name="neg_lb")
+        neg_lb = [sb.tile([P, E], F32, name=f"neg_lb{r}", tag=f"neg_lb{r}") for r in range(PACK)]
         for r in range(PACK):
-            nc.scalar.activation(neg_lb[:, r, :], spread[1][:], ACT.Copy, scale=neg_tx[:, r : r + 1])
+            nc.scalar.activation(neg_lb[r][:], spread[1][:], ACT.Copy, scale=neg_tx[:, r : r + 1])
 
         x_by_d = sb.tile([P, PACK, P, PACK], BF16, name="x_by_d", align_bytes=64)
         x_flat = x_by_d[:].rearrange("p r s t -> p (r s t)")
-        xi_codes, xi_scales = [], []
-        x_by_i = [
-            sb.tile([P, 2, P, PACK], BF16, name=f"x_by_i{u}", tag=tag, align_bytes=64)
-            for u, tag in enumerate(("x_by_i0", "w_raw1"))
-        ]
+        x_by_i = {
+            planes_of: sb.tile([P, len(planes_of), P, PACK], BF16, name=f"x_by_i{planes_of[0]}", tag=tag, align_bytes=64)
+            for planes_of, tag in (((0, 1), "x_by_i0"), ((2,), "x_by_i2"))
+        }
+        xi_codes, xi_scales = {}, {}
 
-        def turn_plane(t, gathered):
-            turned = ps.tile([P, 2, P], F32, name=f"turned{t}", tag=f"bank{1 + t}")
+        def turn_plane(t, gathered, turned_plane):
+            turned = ps.tile([P, 2, P], F32, name=f"turned{t}", tag=f"bank{(4, 3, 4)[t]}")
             for w in range(2):
                 nc.tensor.transpose(turned[:, w, :], gathered.bitcast(F32)[:, w::2], ident[:])
-            words = x_by_i[0][:, t].rearrange("s p r -> s (p r)").bitcast(F32)
+            words = turned_plane.rearrange("s p r -> s (p r)").bitcast(F32)
             nc.scalar.copy(words.rearrange("s (p w) -> s p w", w=2), turned[:].rearrange("s w p -> s p w"))
 
-        def turn_last_planes():
-            words = x_flat.bitcast(F32).rearrange("p (r s u) -> p r s u", r=PACK, u=2)
-            turned = ps.tile([P, PACK, P], F32, name="turned_last", tag="bank2")
-            for r in range(PACK):
-                nc.tensor.transpose(turned[:, r, :], words[:, r, :, 1], ident[:])
-            values = turned[:].rearrange("s r p -> s (r p)").bitcast(BF16)
-            nc.scalar.copy(x_by_i[1][:], values.rearrange("s (r p t) -> s t p r", r=PACK, t=2))
-
-        def quantise_turned(u, tag):
-            xi_codes.append(sb.tile([P, 2, P], U32, name=f"xi_codes{u}", tag=tag, align_bytes=64))
-            xi_scales.append(sb.tile([P, 2, P], U8, name=f"xi_scales{u}", align_bytes=64))
+        def quantise_turned(planes_of, tag):
+            n = len(planes_of)
+            codes = sb.tile([P, n, P], U32, name=f"xi_codes{planes_of[0]}", tag=tag, align_bytes=64)
+            scales = sb.tile([P, n, P], U8, name=f"xi_scales{planes_of[0]}", align_bytes=64)
             nc.vector.quantize_mx(
-                out=xi_codes[u][:].rearrange("s t p -> s (t p)").bitcast(E4M3X4),
-                scales=xi_scales[u][:].rearrange("s t p -> s (t p)"),
-                in_=x_by_i[u][:].rearrange("s t p r -> s (t p r)"),
+                out=codes[:].rearrange("s t p -> s (t p)").bitcast(E4M3X4),
+                scales=scales[:].rearrange("s t p -> s (t p)"),
+                in_=x_by_i[planes_of][:].rearrange("s t p r -> s (t p r)"),
             )
+            for k, t in enumerate(planes_of):
+                xi_codes[t], xi_scales[t] = codes[:, k, :], scales[:, k, :]
 
-        picked = sb.tile([P, 2, SLOTS], BF16, name="picked")
+        picked = sb.tile([P, 2, SLOTS], BF16, name="picked", tag="tx_first")
         for t in range(2):
             nc.vector.tensor_copy(picked[:, t, :], planes[t][:].indirect(offsets[:]))
-            turn_plane(t, picked[:, t, :])
+            turn_plane(t, picked[:, t, :], x_by_i[0, 1][:, t])
         nc.vector.tensor_copy(
             x_by_d[:, :, :, 0:2].rearrange("p r s t -> p s t r"), picked[:].rearrange("p t (s r) -> p s t r", r=PACK)
         )
-        for t in range(2, PACK):
-            place = x_by_d[:, :, :, t].rearrange("p r s -> p s r")
-            nc.vector.tensor_copy(place, planes[t][:].indirect(offsets[:]))
-            if t == 2:
-                quantise_turned(0, "plane2")
+        picked_third = sb.tile([P, SLOTS], BF16, name="picked_third")
+        nc.vector.tensor_copy(picked_third[:], planes[2][:].indirect(offsets[:]))
+        turn_plane(2, picked_third[:], x_by_i[(2,)][:, 0])
+        quantise_turned((0, 1), "plane2")
+        nc.vector.tensor_copy(
+            x_by_d[:, :, :, 2].rearrange("p r s -> p s r"), picked_third[:].rearrange("p (s r) -> p s r", r=PACK)
+        )
+        nc.vector.tensor_copy(x_by_d[:, :, :, 3].rearrange("p r s -> p s r"), planes[3][:].indirect(offsets[:]))
 
         xd_codes = sb.tile([P, SLOTS], U32, name="xd_codes", align_bytes=64)
         xd_scales = sb.tile([P, SLOTS], U8, name="xd_scales", align_bytes=64)
@@ -148,22 +145,25 @@ def tile_attend_grouter_W_kernel(tc, xT, W, dg, lb, ce, tx, offs, out):
             if h == 0:
                 interleave(nc.scalar.copy, w_grouped[:], w_raw[h][:])
             else:
-                interleave(nc.scalar.copy, w_grouped[:, :P], w_raw[h][:, :, :P])
-                interleave(nc.vector.tensor_copy, w_grouped[:, P:], w_raw[h][:, :, P:])
+                interleave(nc.scalar.copy, w_grouped[:, :SCALAR_W], w_raw[h][:, :, :SCALAR_W])
+                interleave(nc.vector.tensor_copy, w_grouped[:, SCALAR_W:], w_raw[h][:, :, SCALAR_W:])
             nc.vector.quantize_mx(
                 out=w_codes[:, halves[h]].bitcast(E4M3X4),
                 scales=w_scales[:, halves[h]],
                 in_=w_grouped[:].rearrange("p e t -> p (e t)"),
             )
 
-        turn_last_planes()
+        words = x_flat.bitcast(F32).rearrange("p (r s u) -> p r s u", r=PACK, u=2)
+        turned_last = ps.tile([P, PACK, P], F32, name="turned_last", tag="bank7")
+        for r in range(PACK):
+            nc.tensor.transpose(turned_last[:, r, :], words[:, r, :, 1], ident[:])
 
         scores = [ps.tile([P, E], F32, name=f"scores{r}", tag=f"bank{r}") for r in range(PACK)]
         a_turned = {}
         for h in range(2):
             for pair in range(2):
                 pair_slots = slice(2 * P * pair, 2 * P * (pair + 1))
-                bank = ps.tile([P, 2, 2 * P], F32, name=f"a_turned{pair}{h}", tag=f"bank{4 + 2 * pair + h}")
+                bank = ps.tile([P, 2, 2 * P], F32, name=f"a_turned{pair}{h}", tag=f"bank{4 + (2 * h + pair) % 3}")
                 for k in range(2):
                     j = 2 * h + k
                     cols = slice(j * P, (j + 1) * P)
@@ -179,7 +179,7 @@ def tile_attend_grouter_W_kernel(tc, xT, W, dg, lb, ce, tx, offs, out):
                     a_turned[pair, j] = bank[:, k, :]
         for pair in range(2):
             for j in range(PACK):
-                by_expert = sb.tile([P, 2, P], F32, name=f"by_expert{pair}{j}")
+                by_expert = sb.tile([P, 2, P], F32, name=f"by_expert{pair}{j}", tag=f"by_expert{pair}{j}", align_bytes=64)
                 ce_column = columns[:, 0, j : j + 1]
                 nc.scalar.activation(
                     by_expert[:].rearrange("e r s -> e (r s)"), a_turned[pair, j], ACT.Copy, scale=ce_column
@@ -197,13 +197,16 @@ def tile_attend_grouter_W_kernel(tc, xT, W, dg, lb, ce, tx, offs, out):
 
         neg_max, neg_s, factor, total = (column(n) for n in ("neg_max", "neg_s", "factor", "total"))
         inv_total = sb.tile([P, PACK], F32, name="inv_total")
-        neg_z, q, neg_ph = (rows(n) for n in ("neg_z", "q", "neg_ph"))
-        neg_h = sb.tile([P, PACK, E], F32, name="neg_h", tag="w_grouped1", align_bytes=64)
-        neg_centred = sb.tile([P, PACK, HALF], F32, name="neg_centred", tag="neg_centred", align_bytes=64)
+        q, neg_ph = (rows(n) for n in ("q", "neg_ph"))
+        neg_h = [
+            sb.tile([P, E], F32, name=f"neg_h{r}", tag=f"neg_h{r}" if r else "w_grouped1", align_bytes=64)
+            for r in range(PACK)
+        ]
         for r in range(PACK):
             nc.vector.scalar_tensor_tensor(
-                neg_h[:, r, :], dg_sb[r][:], neg_tx[:, r : r + 1], neg_lb[:, r, :], ALU.mult, ALU.add
+                neg_h[r][:], dg_sb[r][:], neg_tx[:, r : r + 1], neg_lb[r][:], ALU.mult, ALU.add
             )
+        neg_z = sb.tile([P, PACK, E], F32, name="neg_z", tag=f"neg_lb{PACK - 1}")
 
         centred_turned = [
             [ps.tile([P, 2, P], F32, name=f"centred{pair}{j}", tag=f"bank{4 + 2 * pair + j}") for j in range(2)]
@@ -212,10 +215,10 @@ def tile_attend_grouter_W_kernel(tc, xT, W, dg, lb, ce, tx, offs, out):
 
         def exponentials(r):
             nc.vector.tensor_scalar(
-                neg_z[r][:], scores[r][:], neg_tx[:, r : r + 1], None, ALU.mult, ALU.min, accum_out=neg_max[r][:]
+                neg_z[:, r, :], scores[r][:], neg_tx[:, r : r + 1], None, ALU.mult, ALU.min, accum_out=neg_max[r][:]
             )
             nc.scalar.activation(
-                q[r][:], neg_z[r][:], ACT.Exp, bias=neg_max[r][:], scale=-1.0, accum_out=total[r][:]
+                q[r][:], neg_z[:, r, :], ACT.Exp, bias=neg_max[r][:], scale=-1.0, accum_out=total[r][:]
             )
 
         def inverse(r):
@@ -223,16 +226,22 @@ def tile_attend_grouter_W_kernel(tc, xT, W, dg, lb, ce, tx, offs, out):
 
         def weighted_sum(r):
             nc.vector.scalar_tensor_tensor(
-                neg_ph[r][:], q[r][:], inv_total[:, r : r + 1], neg_h[:, r, :], ALU.mult, ALU.mult, accum_out=neg_s[r][:]
+                neg_ph[r][:], q[r][:], inv_total[:, r : r + 1], neg_h[r][:], ALU.mult, ALU.mult, accum_out=neg_s[r][:]
             )
 
         def centre_turned(r):
             nc.vector.tensor_scalar(factor[r][:], neg_s[r][:], inv_total[:, r : r + 1], -1.0, ALU.mult, ALU.mult)
             scaled_q = sb.tile([P, HALF], F32, name=f"scaled_q{r}")
-            pieces = 2 if r == PACK - 1 else 1
-            for piece in range(pieces):
-                part = slice(piece * HALF // pieces, (piece + 1) * HALF // pieces)
-                nc.scalar.activation(scaled_q[:, part], q[r][:, part], ACT.Copy, scale=factor[r][:])
+            if r < PACK - 1:
+                nc.scalar.activation(scaled_q[:], q[r][:, :HALF], ACT.Copy, scale=factor[r][:])
+            else:
+                neg_inv = sb.tile([P, 1], F32, name="neg_inv")
+                nc.scalar.activation(neg_inv[:], inv_total[:, r : r + 1], ACT.Copy, scale=-1.0)
+                neg_p = sb.tile([P, HALF], F32, name="neg_p")
+                nc.scalar.activation(neg_p[:], q[r][:, :HALF], ACT.Copy, scale=neg_inv[:])
+                for j in range(2):
+                    part = slice(j * P, (j + 1) * P)
+                    nc.scalar.activation(scaled_q[:, part], neg_p[:, part], ACT.Copy, scale=neg_s[r][:])
             for term, source in enumerate((neg_ph[r], scaled_q)):
                 for j in range(2):
                     nc.tensor.matmul(
@@ -250,20 +259,25 @@ def tile_attend_grouter_W_kernel(tc, xT, W, dg, lb, ce, tx, offs, out):
                 if 0 <= step - lag < PACK:
                     stage(step - lag)
 
+        x_by_i[(3,)] = sb.tile([P, 1, P, PACK], BF16, name="x_by_i3", tag="by_expert13", align_bytes=64)
+        values = turned_last[:].rearrange("s r p -> s (r p)").bitcast(BF16)
+        nc.scalar.copy(x_by_i[(3,)][:, 0], values.rearrange("s (r p t) -> s t p r", r=PACK, t=2)[:, 1])
+
+        neg_centred = sb.tile([P, PACK, HALF], F32, name="neg_centred", tag=f"neg_h{PACK - 1}", align_bytes=64)
         for r in range(PACK):
             nc.vector.scalar_tensor_tensor(
                 neg_centred[:, r, :], q[r][:, halves[1]], factor[r][:], neg_ph[r][:, halves[1]], ALU.mult, ALU.add
             )
         g_codes = sb.tile([P, E], U32, name="g_codes", align_bytes=64)
         g_scales = sb.tile([P, E], U8, name="g_scales", align_bytes=64)
-        g_by_i = [sb.tile([P, HALF, PACK], BF16, name=f"g_by_i{h}", align_bytes=64) for h in range(2)]
+        g_by_i = [sb.tile([P, HALF, PACK], BF16, name=f"g_by_i{h}", tag=f"g_by_i{h}", align_bytes=64) for h in range(2)]
         nc.vector.tensor_tensor(
             g_by_i[1][:].rearrange("s (c i) r -> s c r i", i=PACK),
             neg_centred[:].rearrange("s r (c i) -> s c r i", i=PACK),
             neg_ce_rows[:].to_broadcast([P, PACK, HALF]).rearrange("s r (c i) -> s c r i", i=PACK),
             ALU.mult,
         )
-        quantise_turned(1, "neg_centred")
+        quantise_turned((2,), f"neg_h{PACK - 1}")
 
         g_words = g_by_i[0][:].rearrange("s e r -> s (e r)").bitcast(F32).rearrange("s (j e w) -> s j e w", j=2, w=2)
         back = [ps.tile([P, 2, P], F32, name=f"g_back{j}", tag=f"bank{j}") for j in range(2)]
@@ -288,13 +302,15 @@ def tile_attend_grouter_W_kernel(tc, xT, W, dg, lb, ce, tx, offs, out):
                 in_=g_by_i[h][:, part].rearrange("s e r -> s (e r)"),
             )
 
+        quantise_turned((3,), "g_by_i0")
+
         out_rows = out.rearrange("(p t) e -> t p e", t=PACK)
         for t in range(PACK):
             acc = ps.tile([P, E], F32, name=f"acc{t}", tag=f"bank{2 + t}")
             nc.tensor.matmul_mx(
                 out=acc[:],
-                lhsT=xi_codes[t // 2][:, t % 2, :].bitcast(E4M3X4),
-                lhsT_scale=xi_scales[t // 2][:, t % 2, :],
+                lhsT=xi_codes[t].bitcast(E4M3X4),
+                lhsT_scale=xi_scales[t],
                 rhs=g_codes[:].bitcast(E5M2X4),
                 rhs_scale=g_scales[:],
                 start=True,

@@ -67,17 +67,15 @@ def tile_attend_grouter_W_kernel(tc, xT, W, dg, lb, ce, tx, offs, out):
         nc.tensor.transpose(turned_vectors[:], vectors[:], ident[:])
         columns = sb.tile([P, 2, PACK], F32, name="columns")
         nc.scalar.copy(columns[:].rearrange("e v j -> e (v j)"), turned_vectors[:, : 2 * PACK])
-        spread_blocks = ((2, 3), range(PACK))
-        spread = [ps.tile([P, len(spread_blocks[v]) * P], F32, name=f"spread{v}", tag=f"bank{4 + v}") for v in range(2)]
-        for v in range(2):
-            for k, j in enumerate(spread_blocks[v]):
+        spread = [ps.tile([P, E], F32, name=f"spread{v}", tag=f"bank{4 + 2 * v}") for v in range(2)]
+        ce_rows = sb.tile([P, 1, E], F32, name="ce_rows")
+        lb_rows = sb.tile([P, E], F32, name="lb_rows")
+        for v, vector_rows in enumerate((ce_rows[:, 0, :], lb_rows[:])):
+            for j in range(PACK):
                 nc.tensor.transpose(
-                    spread[v][:, k * P : (k + 1) * P], columns[:, v, j : j + 1].to_broadcast([P, P]), ident[:]
+                    spread[v][:, j * P : (j + 1) * P], columns[:, v, j : j + 1].to_broadcast([P, P]), ident[:]
                 )
-        neg_ce_rows = sb.tile([P, 1, HALF], F32, name="neg_ce_rows", tag="neg_ce_rows", align_bytes=64)
-        nc.scalar.activation(neg_ce_rows[:, 0, :], spread[0][:], ACT.Copy, scale=-1.0)
-        neg_ce_columns = sb.tile([P, 2], F32, name="neg_ce_columns")
-        nc.scalar.activation(neg_ce_columns[:], columns[:, 0, :2], ACT.Copy, scale=-1.0)
+            nc.scalar.copy(vector_rows, spread[v][:])
 
         tx_row = sb.tile([P, SLOTS], F32, name="tx_row")
         nc.vector.tensor_copy(tx_row[:], tx_pool[:].indirect(offsets[:]))
@@ -86,9 +84,9 @@ def tile_attend_grouter_W_kernel(tc, xT, W, dg, lb, ce, tx, offs, out):
             nc.tensor.transpose(tx_bank[:, r, :], tx_row[:, r::PACK], ident[:])
         neg_tx = sb.tile([P, PACK], F32, name="neg_tx")
         nc.scalar.activation(neg_tx[:], tx_bank[:, :, 0], ACT.Copy, scale=-1.0)
-        neg_lb = [sb.tile([P, E], F32, name=f"neg_lb{r}", tag=f"neg_lb{r}") for r in range(PACK)]
-        for r in range(PACK):
-            nc.scalar.activation(neg_lb[r][:], spread[1][:], ACT.Copy, scale=neg_tx[:, r : r + 1])
+        numerators = sb.tile([P, PACK, 2], F32, name="numerators")
+        nc.gpsimd.memset(numerators[:], -1.0)
+        nc.scalar.copy(numerators[:, :, 0], tx_bank[:, :, 0])
 
         x_by_d = sb.tile([P, PACK, P, PACK], BF16, name="x_by_d", align_bytes=64)
         x_flat = x_by_d[:].rearrange("p r s t -> p (r s t)")
@@ -133,7 +131,7 @@ def tile_attend_grouter_W_kernel(tc, xT, W, dg, lb, ce, tx, offs, out):
         )
         nc.vector.tensor_copy(x_by_d[:, :, :, 3].rearrange("p r s -> p s r"), planes[3][:].indirect(offsets[:]))
 
-        xd_codes = sb.tile([P, SLOTS], U32, name="xd_codes", align_bytes=64)
+        xd_codes = sb.tile([P, SLOTS], U32, name="xd_codes", tag="xd_codes", align_bytes=64)
         xd_scales = sb.tile([P, SLOTS], U8, name="xd_scales", align_bytes=64)
         nc.vector.quantize_mx(out=xd_codes[:].bitcast(E4M3X4), scales=xd_scales[:], in_=x_flat)
 
@@ -154,40 +152,61 @@ def tile_attend_grouter_W_kernel(tc, xT, W, dg, lb, ce, tx, offs, out):
             )
 
         words = x_flat.bitcast(F32).rearrange("p (r s u) -> p r s u", r=PACK, u=2)
-        turned_last = ps.tile([P, PACK, P], F32, name="turned_last", tag="bank7")
+        turned_last = ps.tile([P, PACK, P], F32, name="turned_last", tag="bank1")
         for r in range(PACK):
             nc.tensor.transpose(turned_last[:, r, :], words[:, r, :, 1], ident[:])
 
-        scores = [ps.tile([P, E], F32, name=f"scores{r}", tag=f"bank{r}") for r in range(PACK)]
+        x_by_i[(3,)] = sb.tile([P, 1, P, PACK], BF16, name="x_by_i3", tag="w_grouped0", align_bytes=64)
+        values = turned_last[:].rearrange("s r p -> s (r p)").bitcast(BF16)
+        nc.scalar.copy(x_by_i[(3,)][:, 0], values.rearrange("s (r p t) -> s t p r", r=PACK, t=2)[:, 1])
+
+        def score_product(result, stationary, moving):
+            nc.tensor.matmul_mx(
+                out=result,
+                lhsT=stationary[0].bitcast(E4M3X4),
+                lhsT_scale=stationary[1],
+                rhs=moving[0].bitcast(E4M3X4),
+                rhs_scale=moving[1],
+                start=True,
+                stop=True,
+            )
+
+        def w_part(cols):
+            return w_codes[:, cols], w_scales[:, cols]
+
+        def x_part(slots):
+            return xd_codes[:, slots], xd_scales[:, slots]
+
+        blocks = [slice(j * P, (j + 1) * P) for j in range(PACK)]
+        groups = (slice(P, 2 * P), slice(2 * P, SLOTS))
+        direct = ps.tile([P, E], F32, name="direct", tag="bank0")
         a_turned = {}
-        for h in range(2):
-            for pair in range(2):
-                pair_slots = slice(2 * P * pair, 2 * P * (pair + 1))
-                bank = ps.tile([P, 2, 2 * P], F32, name=f"a_turned{pair}{h}", tag=f"bank{4 + (2 * h + pair) % 3}")
-                for k in range(2):
-                    j = 2 * h + k
-                    cols = slice(j * P, (j + 1) * P)
-                    nc.tensor.matmul_mx(
-                        out=bank[:, k, :],
-                        lhsT=w_codes[:, cols].bitcast(E4M3X4),
-                        lhsT_scale=w_scales[:, cols],
-                        rhs=xd_codes[:, pair_slots].bitcast(E4M3X4),
-                        rhs_scale=xd_scales[:, pair_slots],
-                        start=True,
-                        stop=True,
-                    )
-                    a_turned[pair, j] = bank[:, k, :]
-        for pair in range(2):
+        score_product(direct[:, halves[0]], x_part(slice(0, P)), w_part(halves[0]))
+        for j in range(2):
+            bank = ps.tile([P, SLOTS], F32, name=f"a_turned{j}", tag=f"bank{4 + j}")
+            for group, slots in enumerate(groups):
+                score_product(bank[:, slots], w_part(blocks[j]), x_part(slots))
+                a_turned[group, j] = bank[:, slots]
+        score_product(direct[:, halves[1]], x_part(slice(0, P)), w_part(halves[1]))
+        for group, slots in enumerate(groups):
+            width = slots.stop - slots.start
+            bank = ps.tile([P, 2, width], F32, name=f"a_late{group}", tag=f"bank{2 + group}")
+            for j in range(2, PACK):
+                score_product(bank[:, j - 2, :], w_part(blocks[j]), x_part(slots))
+                a_turned[group, j] = bank[:, j - 2, :]
+        scores = [direct] + [ps.tile([P, E], F32, name=f"scores{r}", tag=f"bank{r}") for r in range(1, PACK)]
+        by_expert = [
+            sb.tile([P, 2, SLOTS], F32, name=f"by_expert{h}", tag=tag, align_bytes=64)
+            for h, tag in enumerate(("w_grouped1", "by_expert1"))
+        ]
+        for group, slots in enumerate(groups):
             for j in range(PACK):
-                by_expert = sb.tile([P, 2, P], F32, name=f"by_expert{pair}{j}", tag=f"by_expert{pair}{j}", align_bytes=64)
-                ce_column = columns[:, 0, j : j + 1]
                 nc.scalar.activation(
-                    by_expert[:].rearrange("e r s -> e (r s)"), a_turned[pair, j], ACT.Copy, scale=ce_column
+                    by_expert[j // 2][:, j % 2, slots], a_turned[group, j], ACT.Copy, scale=columns[:, 0, j : j + 1]
                 )
-                for member in range(2):
-                    nc.tensor.transpose(
-                        scores[2 * pair + member][:, j * P : (j + 1) * P], by_expert[:, member, :], ident[:]
-                    )
+            for r in range(slots.start // P, slots.stop // P):
+                for j in range(PACK):
+                    nc.tensor.transpose(scores[r][:, blocks[j]], by_expert[j // 2][:, j % 2, blocks[r]], ident[:])
 
         def column(name):
             return [sb.tile([P, 1], F32, name=f"{name}{r}") for r in range(PACK)]
@@ -195,18 +214,16 @@ def tile_attend_grouter_W_kernel(tc, xT, W, dg, lb, ce, tx, offs, out):
         def rows(name):
             return [sb.tile([P, E], F32, name=f"{name}{r}") for r in range(PACK)]
 
-        neg_max, neg_s, factor, total = (column(n) for n in ("neg_max", "neg_s", "factor", "total"))
+        neg_max, tx_s, factor, total = (column(n) for n in ("neg_max", "tx_s", "factor", "total"))
         inv_total = sb.tile([P, PACK], F32, name="inv_total")
-        q, neg_ph = (rows(n) for n in ("q", "neg_ph"))
-        neg_h = [
-            sb.tile([P, E], F32, name=f"neg_h{r}", tag=f"neg_h{r}" if r else "w_grouped1", align_bytes=64)
-            for r in range(PACK)
+        weights = sb.tile([P, PACK, 2], F32, name="weights")
+        neg_z, q, ph = (rows(n) for n in ("neg_z", "q", "ph"))
+        h_rows = [
+            sb.tile([P, E], F32, name=f"h{r}", tag=f"h{r}" if r else "w_raw1", align_bytes=64) for r in range(PACK)
         ]
-        for r in range(PACK):
-            nc.vector.scalar_tensor_tensor(
-                neg_h[r][:], dg_sb[r][:], neg_tx[:, r : r + 1], neg_lb[r][:], ALU.mult, ALU.add
-            )
-        neg_z = sb.tile([P, PACK, E], F32, name="neg_z", tag=f"neg_lb{PACK - 1}")
+        nc.vector.tensor_tensor(h_rows[0][:], dg_sb[0][:], spread[1][:], ALU.add)
+        for r in range(1, PACK):
+            nc.gpsimd.tensor_tensor(h_rows[r][:], dg_sb[r][:], lb_rows[:], ALU.add)
 
         centred_turned = [
             [ps.tile([P, 2, P], F32, name=f"centred{pair}{j}", tag=f"bank{4 + 2 * pair + j}") for j in range(2)]
@@ -214,35 +231,37 @@ def tile_attend_grouter_W_kernel(tc, xT, W, dg, lb, ce, tx, offs, out):
         ]
 
         def exponentials(r):
-            nc.vector.tensor_scalar(
-                neg_z[:, r, :], scores[r][:], neg_tx[:, r : r + 1], None, ALU.mult, ALU.min, accum_out=neg_max[r][:]
-            )
-            nc.scalar.activation(
-                q[r][:], neg_z[:, r, :], ACT.Exp, bias=neg_max[r][:], scale=-1.0, accum_out=total[r][:]
-            )
+            if r == 0:
+                nc.vector.scalar_tensor_tensor(
+                    neg_z[r][:], scores[r][:], neg_tx[:, r : r + 1], ce_rows[:, 0, :], ALU.mult, ALU.mult
+                )
+                nc.vector.tensor_reduce(neg_max[r][:], neg_z[r][:], mybir.AxisListType.X, ALU.min)
+            else:
+                nc.vector.tensor_scalar(
+                    neg_z[r][:], scores[r][:], neg_tx[:, r : r + 1], None, ALU.mult, ALU.min, accum_out=neg_max[r][:]
+                )
+            nc.scalar.activation(q[r][:], neg_z[r][:], ACT.Exp, bias=neg_max[r][:], scale=-1.0, accum_out=total[r][:])
 
         def inverse(r):
             nc.vector.reciprocal(inv_total[:, r : r + 1], total[r][:])
+            nc.scalar.activation(weights[:, r, :], numerators[:, r, :], ACT.Copy, scale=inv_total[:, r : r + 1])
 
         def weighted_sum(r):
             nc.vector.scalar_tensor_tensor(
-                neg_ph[r][:], q[r][:], inv_total[:, r : r + 1], neg_h[r][:], ALU.mult, ALU.mult, accum_out=neg_s[r][:]
+                ph[r][:], q[r][:], weights[:, r, 0:1], h_rows[r][:], ALU.mult, ALU.mult, accum_out=tx_s[r][:]
             )
 
         def centre_turned(r):
-            nc.vector.tensor_scalar(factor[r][:], neg_s[r][:], inv_total[:, r : r + 1], -1.0, ALU.mult, ALU.mult)
+            nc.vector.tensor_scalar(factor[r][:], tx_s[r][:], weights[:, r, 1:2], None, ALU.mult)
             scaled_q = sb.tile([P, HALF], F32, name=f"scaled_q{r}")
             if r < PACK - 1:
                 nc.scalar.activation(scaled_q[:], q[r][:, :HALF], ACT.Copy, scale=factor[r][:])
             else:
-                neg_inv = sb.tile([P, 1], F32, name="neg_inv")
-                nc.scalar.activation(neg_inv[:], inv_total[:, r : r + 1], ACT.Copy, scale=-1.0)
                 neg_p = sb.tile([P, HALF], F32, name="neg_p")
-                nc.scalar.activation(neg_p[:], q[r][:, :HALF], ACT.Copy, scale=neg_inv[:])
+                nc.scalar.activation(neg_p[:], q[r][:, :HALF], ACT.Copy, scale=weights[:, r, 1:2])
                 for j in range(2):
-                    part = slice(j * P, (j + 1) * P)
-                    nc.scalar.activation(scaled_q[:, part], neg_p[:, part], ACT.Copy, scale=neg_s[r][:])
-            for term, source in enumerate((neg_ph[r], scaled_q)):
+                    nc.scalar.activation(scaled_q[:, blocks[j]], neg_p[:, blocks[j]], ACT.Copy, scale=tx_s[r][:])
+            for term, source in enumerate((ph[r], scaled_q)):
                 for j in range(2):
                     nc.tensor.matmul(
                         centred_turned[r // 2][j][:, r % 2, :],
@@ -259,25 +278,21 @@ def tile_attend_grouter_W_kernel(tc, xT, W, dg, lb, ce, tx, offs, out):
                 if 0 <= step - lag < PACK:
                     stage(step - lag)
 
-        x_by_i[(3,)] = sb.tile([P, 1, P, PACK], BF16, name="x_by_i3", tag="by_expert13", align_bytes=64)
-        values = turned_last[:].rearrange("s r p -> s (r p)").bitcast(BF16)
-        nc.scalar.copy(x_by_i[(3,)][:, 0], values.rearrange("s (r p t) -> s t p r", r=PACK, t=2)[:, 1])
-
-        neg_centred = sb.tile([P, PACK, HALF], F32, name="neg_centred", tag=f"neg_h{PACK - 1}", align_bytes=64)
+        centred = sb.tile([P, PACK, HALF], F32, name="centred", tag="h2", align_bytes=64)
         for r in range(PACK):
             nc.vector.scalar_tensor_tensor(
-                neg_centred[:, r, :], q[r][:, halves[1]], factor[r][:], neg_ph[r][:, halves[1]], ALU.mult, ALU.add
+                centred[:, r, :], q[r][:, halves[1]], factor[r][:], ph[r][:, halves[1]], ALU.mult, ALU.add
             )
         g_codes = sb.tile([P, E], U32, name="g_codes", align_bytes=64)
         g_scales = sb.tile([P, E], U8, name="g_scales", align_bytes=64)
         g_by_i = [sb.tile([P, HALF, PACK], BF16, name=f"g_by_i{h}", tag=f"g_by_i{h}", align_bytes=64) for h in range(2)]
         nc.vector.tensor_tensor(
             g_by_i[1][:].rearrange("s (c i) r -> s c r i", i=PACK),
-            neg_centred[:].rearrange("s r (c i) -> s c r i", i=PACK),
-            neg_ce_rows[:].to_broadcast([P, PACK, HALF]).rearrange("s r (c i) -> s c r i", i=PACK),
+            centred[:].rearrange("s r (c i) -> s c r i", i=PACK),
+            ce_rows[:, :, halves[1]].to_broadcast([P, PACK, HALF]).rearrange("s r (c i) -> s c r i", i=PACK),
             ALU.mult,
         )
-        quantise_turned((2,), f"neg_h{PACK - 1}")
+        quantise_turned((2,), "h2")
 
         g_words = g_by_i[0][:].rearrange("s e r -> s (e r)").bitcast(F32).rearrange("s (j e w) -> s j e w", j=2, w=2)
         back = [ps.tile([P, 2, P], F32, name=f"g_back{j}", tag=f"bank{j}") for j in range(2)]
@@ -288,7 +303,7 @@ def tile_attend_grouter_W_kernel(tc, xT, W, dg, lb, ce, tx, offs, out):
                     g_turned[:],
                     centred_turned[pair][j][:].rearrange("e k s -> e s k"),
                     ACT.Copy,
-                    scale=neg_ce_columns[:, j : j + 1],
+                    scale=columns[:, 0, j : j + 1],
                 )
                 words = g_turned[:].rearrange("e s k -> e (s k)").bitcast(F32)
                 nc.tensor.transpose(back[j][:, pair, :], words, ident[:])

@@ -160,6 +160,13 @@ def tile_attend_grouter_W_kernel(tc, xT, W, dg, lb, ce, tx, offs, out):
         values = turned_last[:].rearrange("s r p -> s (r p)").bitcast(BF16)
         nc.scalar.copy(x_by_i[(3,)][:, 0], values.rearrange("s (r p t) -> s t p r", r=PACK, t=2)[:, 1])
 
+        h_rows = [
+            sb.tile([P, E], F32, name=f"h{r}", tag=tag, align_bytes=64) for r, tag in enumerate(("w_raw1", "w_grouped1", "h2", "h3"))
+        ]
+        nc.vector.tensor_tensor(h_rows[0][:], dg_sb[0][:], spread[1][:], ALU.add)
+        for r in range(1, PACK):
+            nc.gpsimd.tensor_tensor(h_rows[r][:], dg_sb[r][:], lb_rows[:], ALU.add)
+
         def score_product(result, stationary, moving):
             nc.tensor.matmul_mx(
                 out=result,
@@ -197,7 +204,7 @@ def tile_attend_grouter_W_kernel(tc, xT, W, dg, lb, ce, tx, offs, out):
         scores = [direct] + [ps.tile([P, E], F32, name=f"scores{r}", tag=f"bank{r}") for r in range(1, PACK)]
         by_expert = [
             sb.tile([P, 2, SLOTS], F32, name=f"by_expert{h}", tag=tag, align_bytes=64)
-            for h, tag in enumerate(("w_grouped1", "by_expert1"))
+            for h, tag in enumerate(("dg0", "by_expert1"))
         ]
         for group, slots in enumerate(groups):
             for j in range(PACK):
@@ -218,13 +225,6 @@ def tile_attend_grouter_W_kernel(tc, xT, W, dg, lb, ce, tx, offs, out):
         inv_total = sb.tile([P, PACK], F32, name="inv_total")
         weights = sb.tile([P, PACK, 2], F32, name="weights")
         neg_z, q, ph = (rows(n) for n in ("neg_z", "q", "ph"))
-        h_rows = [
-            sb.tile([P, E], F32, name=f"h{r}", tag=f"h{r}" if r else "w_raw1", align_bytes=64) for r in range(PACK)
-        ]
-        nc.vector.tensor_tensor(h_rows[0][:], dg_sb[0][:], spread[1][:], ALU.add)
-        for r in range(1, PACK):
-            nc.gpsimd.tensor_tensor(h_rows[r][:], dg_sb[r][:], lb_rows[:], ALU.add)
-
         centred_turned = [
             [ps.tile([P, 2, P], F32, name=f"centred{pair}{j}", tag=f"bank{4 + 2 * pair + j}") for j in range(2)]
             for pair in range(2)

@@ -85,7 +85,7 @@ def tile_attend_grouter_W_kernel(tc, xT, W, dg, lb, ce, tx, offs, out):
         neg_tx = sb.tile([P, PACK], F32, name="neg_tx")
         nc.scalar.activation(neg_tx[:], tx_bank[:, :, 0], ACT.Copy, scale=-1.0)
         numerators = sb.tile([P, PACK, 2], F32, name="numerators")
-        nc.gpsimd.memset(numerators[:], -1.0)
+        nc.vector.memset(numerators[:], -1.0)
         nc.scalar.copy(numerators[:, :, 0], tx_bank[:, :, 0])
 
         x_by_d = sb.tile([P, PACK, P, PACK], BF16, name="x_by_d", align_bytes=64)
@@ -283,8 +283,10 @@ def tile_attend_grouter_W_kernel(tc, xT, W, dg, lb, ce, tx, offs, out):
             nc.vector.scalar_tensor_tensor(
                 centred[:, r, :], q[r][:, halves[1]], factor[r][:], ph[r][:, halves[1]], ALU.mult, ALU.add
             )
-        g_codes = sb.tile([P, E], U32, name="g_codes", align_bytes=64)
-        g_scales = sb.tile([P, E], U8, name="g_scales", align_bytes=64)
+        g_codes = sb.tile([P, E + HALF], U32, name="g_codes", align_bytes=64)
+        g_scales = sb.tile([P, E + HALF], U8, name="g_scales", align_bytes=64)
+        nc.vector.memset(g_codes[:, E:], 0)
+        nc.vector.memset(g_scales[:, E:], 0)
         g_by_i = [sb.tile([P, HALF, PACK], BF16, name=f"g_by_i{h}", tag=f"g_by_i{h}", align_bytes=64) for h in range(2)]
         nc.vector.tensor_tensor(
             g_by_i[1][:].rearrange("s (c i) r -> s c r i", i=PACK),
@@ -320,21 +322,20 @@ def tile_attend_grouter_W_kernel(tc, xT, W, dg, lb, ce, tx, offs, out):
         quantise_turned((3,), "g_by_i0")
 
         out_rows = out.rearrange("(p t) e -> t p e", t=PACK)
-        for t in range(PACK):
-            acc = ps.tile([P, E], F32, name=f"acc{t}", tag=f"bank{2 + t}")
+        products = [(t, 7 - t, HALF, halves[0]) for t in range(2)]
+        products.extend((t, t, 0, slice(0, E)) for t in (2, 3))
+        products.extend((t, 4 + t, 0, halves[0]) for t in range(2))
+        for step, (t, bank_number, first, part) in enumerate(products):
+            acc = ps.tile([P, E], F32, name=f"acc{step}", tag=f"bank{bank_number}")
             nc.tensor.matmul_mx(
                 out=acc[:],
                 lhsT=xi_codes[t].bitcast(E4M3X4),
                 lhsT_scale=xi_scales[t],
-                rhs=g_codes[:].bitcast(E5M2X4),
-                rhs_scale=g_scales[:],
+                rhs=g_codes[:, first : first + E].bitcast(E5M2X4),
+                rhs_scale=g_scales[:, first : first + E],
                 start=True,
                 stop=True,
             )
-            copy = (nc.scalar.copy, nc.vector.tensor_copy)[t % 2]
-            pieces = 2 if t in (0, PACK - 1) else 1
-            for piece in range(pieces):
-                part = slice(piece * E // pieces, (piece + 1) * E // pieces)
-                result = sb.tile([P, E // pieces], F32, name=f"result{t}_{piece}")
-                copy(result[:], acc[:, part])
-                nc.sync.dma_start(out_rows[t][:, part], result[:])
+            result = sb.tile([P, part.stop - part.start], F32, name=f"result{step}")
+            (nc.scalar.copy, nc.vector.tensor_copy)[step % 2](result[:], acc[:, part])
+            nc.sync.dma_start(out_rows[t][:, first + part.start : first + part.stop], result[:])

@@ -40,7 +40,7 @@ def tile_attend_grouter_W_kernel(tc, xT, W, dg, lb, ce, tx, offs, out):
         offsets = sb.tile([P, SLOTS // 16], U16, name="offsets")
         nc.sync.dma_start(offsets[:], offs)
         tx_first = sb.tile([1, TOKENS], F32, name="tx_first", tag="tx_first")
-        nc.sync.dma_start(tx_first[:], tx[0:1, :])
+        nc.scalar.dma_start(tx_first[:], tx[0:1, :])
         x_rows = xT.rearrange("(p t) n -> t p n", t=PACK)
         planes = [sb.tile([P, TOKENS], F32, name=f"plane{t}", tag=f"plane{t}", align_bytes=64) for t in range(PACK)]
         nc.sync.dma_start(planes[0][:], x_rows[0])

@@ -278,15 +278,14 @@ def tile_attend_grouter_W_kernel(tc, xT, W, dg, lb, ce, tx, offs, out):
                 if 0 <= step - lag < PACK:
                     stage(step - lag)
 
+        quantise_turned((3,), "h3")
         centred = sb.tile([P, PACK, HALF], F32, name="centred", tag="h2", align_bytes=64)
         for r in range(PACK):
             nc.vector.scalar_tensor_tensor(
                 centred[:, r, :], q[r][:, halves[1]], factor[r][:], ph[r][:, halves[1]], ALU.mult, ALU.add
             )
-        g_codes = sb.tile([P, E + HALF], U32, name="g_codes", align_bytes=64)
-        g_scales = sb.tile([P, E + HALF], U8, name="g_scales", align_bytes=64)
-        nc.vector.memset(g_codes[:, E:], 0)
-        nc.vector.memset(g_scales[:, E:], 0)
+        g_codes = sb.tile([P, E], U32, name="g_codes", align_bytes=64)
+        g_scales = sb.tile([P, E], U8, name="g_scales", align_bytes=64)
         g_by_i = [sb.tile([P, HALF, PACK], BF16, name=f"g_by_i{h}", tag=f"g_by_i{h}", align_bytes=64) for h in range(2)]
         nc.vector.tensor_tensor(
             g_by_i[1][:].rearrange("s (c i) r -> s c r i", i=PACK),
@@ -319,23 +318,19 @@ def tile_attend_grouter_W_kernel(tc, xT, W, dg, lb, ce, tx, offs, out):
                 in_=g_by_i[h][:, part].rearrange("s e r -> s (e r)"),
             )
 
-        quantise_turned((3,), "g_by_i0")
-
-        out_rows = out.rearrange("(p t) e -> t p e", t=PACK)
-        products = [(t, 7 - t, HALF, halves[0]) for t in range(2)]
-        products.extend((t, t, 0, slice(0, E)) for t in (2, 3))
-        products.extend((t, 4 + t, 0, halves[0]) for t in range(2))
-        for step, (t, bank_number, first, part) in enumerate(products):
-            acc = ps.tile([P, E], F32, name=f"acc{step}", tag=f"bank{bank_number}")
+        out_rows = out.rearrange("(p t) e -> p t e", t=PACK)
+        for step in range(2 * PACK):
+            cols, t = halves[1 - step // PACK], step % PACK
+            acc = ps.tile([P, HALF], F32, name=f"acc{step}", tag=f"bank{(2 + step) % 8}")
             nc.tensor.matmul_mx(
                 out=acc[:],
                 lhsT=xi_codes[t].bitcast(E4M3X4),
                 lhsT_scale=xi_scales[t],
-                rhs=g_codes[:, first : first + E].bitcast(E5M2X4),
-                rhs_scale=g_scales[:, first : first + E],
+                rhs=g_codes[:, cols].bitcast(E5M2X4),
+                rhs_scale=g_scales[:, cols],
                 start=True,
                 stop=True,
             )
-            result = sb.tile([P, part.stop - part.start], F32, name=f"result{step}")
-            (nc.scalar.copy, nc.vector.tensor_copy)[step % 2](result[:], acc[:, part])
-            nc.sync.dma_start(out_rows[t][:, first + part.start : first + part.stop], result[:])
+            result = sb.tile([P, HALF], F32, name=f"result{step}")
+            (nc.scalar.copy, nc.vector.tensor_copy)[step % 2](result[:], acc[:])
+            nc.sync.dma_start(out_rows[:, t, cols], result[:])

@@ -17,6 +17,7 @@ P = 128
 PACK = 4
 D, E, SLOTS, TOKENS = 512, 512, 512, 2048
 HALF = E // 2
+DIRECT = 2
 SCALAR_W = 96
 
 FLOPS = 2 * 2 * D * E * SLOTS
@@ -138,21 +139,28 @@ def tile_attend_grouter_W_kernel(tc, xT, W, dg, lb, ce, tx, offs, out):
         w_codes = sb.tile([P, E], U32, name="w_codes", align_bytes=64)
         w_scales = sb.tile([P, E], U8, name="w_scales", align_bytes=64)
         halves = [slice(h * HALF, (h + 1) * HALF) for h in range(2)]
-        for h in range(2):
-            w_grouped = sb.tile([P, HALF, PACK], BF16, name=f"w_grouped{h}", tag=f"w_grouped{h}", align_bytes=64)
-            if h == 0:
-                interleave(nc.scalar.copy, w_grouped[:], w_raw[h][:])
-            else:
-                interleave(nc.scalar.copy, w_grouped[:, :SCALAR_W], w_raw[h][:, :, :SCALAR_W])
-                interleave(nc.vector.tensor_copy, w_grouped[:, SCALAR_W:], w_raw[h][:, :, SCALAR_W:])
+        blocks = [slice(j * P, (j + 1) * P) for j in range(PACK)]
+        w_grouped = [
+            sb.tile([P, HALF, PACK], BF16, name=f"w_grouped{h}", tag=f"w_grouped{h}", align_bytes=64) for h in range(2)
+        ]
+
+        def quantise_w(h, cols):
+            whole = slice(h * HALF + cols.start, h * HALF + cols.stop)
             nc.vector.quantize_mx(
-                out=w_codes[:, halves[h]].bitcast(E4M3X4),
-                scales=w_scales[:, halves[h]],
-                in_=w_grouped[:].rearrange("p e t -> p (e t)"),
+                out=w_codes[:, whole].bitcast(E4M3X4),
+                scales=w_scales[:, whole],
+                in_=w_grouped[h][:, cols].rearrange("p e t -> p (e t)"),
             )
 
+        for j in range(2):
+            interleave(nc.scalar.copy, w_grouped[0][:, blocks[j]], w_raw[0][:, :, blocks[j]])
+            quantise_w(0, blocks[j])
+        interleave(nc.scalar.copy, w_grouped[1][:, :SCALAR_W], w_raw[1][:, :, :SCALAR_W])
+        interleave(nc.vector.tensor_copy, w_grouped[1][:, SCALAR_W:], w_raw[1][:, :, SCALAR_W:])
+        quantise_w(1, slice(0, HALF))
+
         words = x_flat.bitcast(F32).rearrange("p (r s u) -> p r s u", r=PACK, u=2)
-        turned_last = ps.tile([P, PACK, P], F32, name="turned_last", tag="bank1")
+        turned_last = ps.tile([P, PACK, P], F32, name="turned_last", tag="bank2")
         for r in range(PACK):
             nc.tensor.transpose(turned_last[:, r, :], words[:, r, :, 1], ident[:])
 
@@ -161,11 +169,12 @@ def tile_attend_grouter_W_kernel(tc, xT, W, dg, lb, ce, tx, offs, out):
         nc.scalar.copy(x_by_i[(3,)][:, 0], values.rearrange("s (r p t) -> s t p r", r=PACK, t=2)[:, 1])
 
         h_rows = [
-            sb.tile([P, E], F32, name=f"h{r}", tag=tag, align_bytes=64) for r, tag in enumerate(("w_raw1", "w_grouped1", "h2", "h3"))
+            sb.tile([P, E], F32, name=f"h{r}", tag=tag, align_bytes=64)
+            for r, tag in enumerate(("w_grouped1", "h1", "h2", "h3"))
         ]
-        nc.vector.tensor_tensor(h_rows[0][:], dg_sb[0][:], spread[1][:], ALU.add)
-        for r in range(1, PACK):
-            nc.gpsimd.tensor_tensor(h_rows[r][:], dg_sb[r][:], lb_rows[:], ALU.add)
+        for r in range(PACK):
+            cols = halves[1] if r == 0 else slice(0, E)
+            nc.gpsimd.tensor_tensor(h_rows[r][:, cols], dg_sb[r][:, cols], lb_rows[:, cols], ALU.add)
 
         def score_product(result, stationary, moving):
             nc.tensor.matmul_mx(
@@ -184,36 +193,42 @@ def tile_attend_grouter_W_kernel(tc, xT, W, dg, lb, ce, tx, offs, out):
         def x_part(slots):
             return xd_codes[:, slots], xd_scales[:, slots]
 
-        blocks = [slice(j * P, (j + 1) * P) for j in range(PACK)]
-        groups = (slice(P, 2 * P), slice(2 * P, SLOTS))
-        direct = ps.tile([P, E], F32, name="direct", tag="bank0")
-        a_turned = {}
-        score_product(direct[:, halves[0]], x_part(slice(0, P)), w_part(halves[0]))
-        for j in range(2):
-            bank = ps.tile([P, SLOTS], F32, name=f"a_turned{j}", tag=f"bank{4 + j}")
-            for group, slots in enumerate(groups):
-                score_product(bank[:, slots], w_part(blocks[j]), x_part(slots))
-                a_turned[group, j] = bank[:, slots]
-        score_product(direct[:, halves[1]], x_part(slice(0, P)), w_part(halves[1]))
-        for group, slots in enumerate(groups):
-            width = slots.stop - slots.start
-            bank = ps.tile([P, 2, width], F32, name=f"a_late{group}", tag=f"bank{2 + group}")
-            for j in range(2, PACK):
-                score_product(bank[:, j - 2, :], w_part(blocks[j]), x_part(slots))
-                a_turned[group, j] = bank[:, j - 2, :]
-        scores = [direct] + [ps.tile([P, E], F32, name=f"scores{r}", tag=f"bank{r}") for r in range(1, PACK)]
-        by_expert = [
-            sb.tile([P, 2, SLOTS], F32, name=f"by_expert{h}", tag=tag, align_bytes=64)
-            for h, tag in enumerate(("dg0", "by_expert1"))
+        first_halves = ps.tile([P, DIRECT, HALF], F32, name="first_halves", tag="bank0")
+        direct = [
+            (first_halves[:, r, :], ps.tile([P, HALF], F32, name=f"second_half{r}", tag=f"bank{4 + r}")[:])
+            for r in range(DIRECT)
         ]
-        for group, slots in enumerate(groups):
+        late_slots = slice(DIRECT * P, SLOTS)
+        a_turned = [
+            ps.tile([P, 2, SLOTS - DIRECT * P], F32, name=f"a_turned{h}", tag=f"bank{(1, 7)[h]}") for h in range(2)
+        ]
+        for j in range(2):
+            for r in range(DIRECT):
+                score_product(direct[r][0][:, blocks[j]], x_part(blocks[r]), w_part(blocks[j]))
+            score_product(a_turned[0][:, j, :], w_part(blocks[j]), x_part(late_slots))
+        for r in range(DIRECT):
+            score_product(direct[r][1], x_part(blocks[r]), w_part(halves[1]))
+        for j in range(2, PACK):
+            score_product(a_turned[1][:, j - 2, :], w_part(blocks[j]), x_part(late_slots))
+        neg_z = [sb.tile([P, E], F32, name=f"neg_z{r}") for r in range(PACK)]
+
+        def scale_direct(r, h):
+            nc.vector.scalar_tensor_tensor(
+                neg_z[r][:, halves[h]], direct[r][h], neg_tx[:, r : r + 1], ce_rows[:, 0, halves[h]], ALU.mult, ALU.mult
+            )
+
+        for r in range(DIRECT):
+            scale_direct(r, 0)
+        nc.vector.tensor_tensor(h_rows[0][:, halves[0]], dg_sb[0][:, halves[0]], spread[1][:, halves[0]], ALU.add)
+        by_expert = sb.tile([P, PACK, SLOTS - DIRECT * P], F32, name="by_expert")
+        for j in range(PACK):
+            nc.scalar.activation(
+                by_expert[:, j, :], a_turned[j // 2][:, j % 2, :], ACT.Copy, scale=columns[:, 0, j : j + 1]
+            )
+        scores = {r: ps.tile([P, E], F32, name=f"scores{r}", tag=f"bank{r}") for r in range(DIRECT, PACK)}
+        for r in range(DIRECT, PACK):
             for j in range(PACK):
-                nc.scalar.activation(
-                    by_expert[j // 2][:, j % 2, slots], a_turned[group, j], ACT.Copy, scale=columns[:, 0, j : j + 1]
-                )
-            for r in range(slots.start // P, slots.stop // P):
-                for j in range(PACK):
-                    nc.tensor.transpose(scores[r][:, blocks[j]], by_expert[j // 2][:, j % 2, blocks[r]], ident[:])
+                nc.tensor.transpose(scores[r][:, blocks[j]], by_expert[:, j, blocks[r - DIRECT]], ident[:])
 
         def column(name):
             return [sb.tile([P, 1], F32, name=f"{name}{r}") for r in range(PACK)]
@@ -224,17 +239,15 @@ def tile_attend_grouter_W_kernel(tc, xT, W, dg, lb, ce, tx, offs, out):
         neg_max, tx_s, factor, total = (column(n) for n in ("neg_max", "tx_s", "factor", "total"))
         inv_total = sb.tile([P, PACK], F32, name="inv_total")
         weights = sb.tile([P, PACK, 2], F32, name="weights")
-        neg_z, q, ph = (rows(n) for n in ("neg_z", "q", "ph"))
+        q, ph = (rows(n) for n in ("q", "ph"))
         centred_turned = [
             [ps.tile([P, 2, P], F32, name=f"centred{pair}{j}", tag=f"bank{4 + 2 * pair + j}") for j in range(2)]
             for pair in range(2)
         ]
 
         def exponentials(r):
-            if r == 0:
-                nc.vector.scalar_tensor_tensor(
-                    neg_z[r][:], scores[r][:], neg_tx[:, r : r + 1], ce_rows[:, 0, :], ALU.mult, ALU.mult
-                )
+            if r < DIRECT:
+                scale_direct(r, 1)
                 nc.vector.tensor_reduce(neg_max[r][:], neg_z[r][:], mybir.AxisListType.X, ALU.min)
             else:
                 nc.vector.tensor_scalar(

@@ -17,6 +17,7 @@ P = 128
 PACK = 4
 D, E, SLOTS, TOKENS = 512, 512, 512, 2048
 HALF = E // 2
+SCALAR_SLOTS = 128
 DIRECT = 2
 SCALAR_W = 96
 
@@ -123,14 +124,25 @@ def tile_attend_grouter_W_kernel(tc, xT, W, dg, lb, ce, tx, offs, out):
         nc.vector.tensor_copy(
             x_by_d[:, :, :, 0:2].rearrange("p r s t -> p s t r"), picked[:].rearrange("p t (s r) -> p s t r", r=PACK)
         )
-        picked_third = sb.tile([P, SLOTS], BF16, name="picked_third")
-        nc.vector.tensor_copy(picked_third[:], planes[2][:].indirect(offsets[:]))
-        turn_plane(2, picked_third[:], x_by_i[(2,)][:, 0])
+        picked_late = sb.tile([P, 2, SLOTS], BF16, name="picked_late")
+        nc.vector.tensor_copy(picked_late[:, 0, :], planes[2][:].indirect(offsets[:]))
+        turn_plane(2, picked_late[:, 0, :], x_by_i[(2,)][:, 0])
         quantise_turned((0, 1), "plane2")
+        first = SLOTS - SCALAR_SLOTS
         nc.vector.tensor_copy(
-            x_by_d[:, :, :, 2].rearrange("p r s -> p s r"), picked_third[:].rearrange("p (s r) -> p s r", r=PACK)
+            x_by_d[:, :, : first // PACK, 2].rearrange("p r s -> p s r"),
+            picked_late[:, 0, :first].rearrange("p (s r) -> p s r", r=PACK),
         )
-        nc.vector.tensor_copy(x_by_d[:, :, :, 3].rearrange("p r s -> p s r"), planes[3][:].indirect(offsets[:]))
+        nc.vector.tensor_copy(
+            x_by_d[:, :, : first // PACK, 3].rearrange("p r s -> p s r"),
+            planes[3][:].indirect(offsets[:, : first // 16]),
+        )
+        nc.scalar.activation(picked_late[:, 1, first:], planes[3][:].indirect(offsets[:, first // 16 :]), ACT.Copy)
+        nc.scalar.copy(
+            x_by_d[:, :, first // PACK :, 2:4].rearrange("p r s t -> p s t r"),
+            picked_late[:, :, first:].rearrange("p t (s r) -> p s t r", r=PACK),
+        )
+        quantise_turned((2,), "plane3")
 
         xd_codes = sb.tile([P, SLOTS], U32, name="xd_codes", tag="xd_codes", align_bytes=64)
         xd_scales = sb.tile([P, SLOTS], U8, name="xd_scales", align_bytes=64)
@@ -291,7 +303,6 @@ def tile_attend_grouter_W_kernel(tc, xT, W, dg, lb, ce, tx, offs, out):
                 if 0 <= step - lag < PACK:
                     stage(step - lag)
 
-        quantise_turned((3,), "h3")
         centred = sb.tile([P, PACK, HALF], F32, name="centred", tag="h2", align_bytes=64)
         for r in range(PACK):
             nc.vector.scalar_tensor_tensor(
@@ -306,7 +317,7 @@ def tile_attend_grouter_W_kernel(tc, xT, W, dg, lb, ce, tx, offs, out):
             ce_rows[:, :, halves[1]].to_broadcast([P, PACK, HALF]).rearrange("s r (c i) -> s c r i", i=PACK),
             ALU.mult,
         )
-        quantise_turned((2,), "h2")
+        quantise_turned((3,), "h2")
 
         g_words = g_by_i[0][:].rearrange("s e r -> s (e r)").bitcast(F32).rearrange("s (j e w) -> s j e w", j=2, w=2)
         back = [ps.tile([P, 2, P], F32, name=f"g_back{j}", tag=f"bank{j}") for j in range(2)]

@@ -17,6 +17,7 @@ P = 128
 PACK = 4
 D, E, SLOTS, TOKENS = 512, 512, 512, 2048
 HALF = E // 2
+SUMMED = 1
 SCALAR_SLOTS = 128
 DIRECT = 2
 SCALAR_W = 96
@@ -277,25 +278,33 @@ def tile_attend_grouter_W_kernel(tc, xT, W, dg, lb, ce, tx, offs, out):
             )
 
         def centre_turned(r):
-            nc.vector.tensor_scalar(factor[r][:], tx_s[r][:], weights[:, r, 1:2], None, ALU.mult)
             scaled_q = sb.tile([P, HALF], F32, name=f"scaled_q{r}")
             if r < PACK - 1:
-                nc.scalar.activation(scaled_q[:], q[r][:, :HALF], ACT.Copy, scale=factor[r][:])
+                nc.scalar.activation(factor[r][:], tx_s[r][:], ACT.Copy, scale=weights[:, r, 1:2])
+                scaled = blocks[0] if r == SUMMED else halves[0]
+                nc.scalar.activation(scaled_q[:, scaled], q[r][:, scaled], ACT.Copy, scale=factor[r][:])
+                if r == SUMMED:
+                    nc.vector.scalar_tensor_tensor(
+                        scaled_q[:, blocks[1]], q[r][:, blocks[1]], factor[r][:], ph[r][:, blocks[1]], ALU.mult, ALU.add
+                    )
             else:
+                nc.vector.tensor_scalar(factor[r][:], tx_s[r][:], weights[:, r, 1:2], None, ALU.mult)
                 neg_p = sb.tile([P, HALF], F32, name="neg_p")
                 nc.scalar.activation(neg_p[:], q[r][:, :HALF], ACT.Copy, scale=weights[:, r, 1:2])
                 for j in range(2):
                     nc.scalar.activation(scaled_q[:, blocks[j]], neg_p[:, blocks[j]], ACT.Copy, scale=tx_s[r][:])
             for term, source in enumerate((ph[r], scaled_q)):
                 for j in range(2):
-                    nc.tensor.matmul(
-                        centred_turned[r // 2][j][:, r % 2, :],
-                        source[:, j * P : (j + 1) * P],
-                        ident[:],
-                        is_transpose=True,
-                        start=term == 0,
-                        stop=term == 1,
-                    )
+                    summed = r == SUMMED and j == 1
+                    if term == 1 or not summed:
+                        nc.tensor.matmul(
+                            centred_turned[r // 2][j][:, r % 2, :],
+                            source[:, blocks[j]],
+                            ident[:],
+                            is_transpose=True,
+                            start=term == 0 or summed,
+                            stop=term == 1,
+                        )
 
         stages = ((exponentials, 0), (inverse, 2), (centre_turned, 4), (weighted_sum, 3))
         for step in range(PACK + max(lag for stage, lag in stages)):
@@ -304,20 +313,22 @@ def tile_attend_grouter_W_kernel(tc, xT, W, dg, lb, ce, tx, offs, out):
                     stage(step - lag)
 
         centred = sb.tile([P, PACK, HALF], F32, name="centred", tag="h2", align_bytes=64)
-        for r in range(PACK):
+        sums = [(r, slice(0, HALF)) for r in range(PACK - 1)] + [(PACK - 1, blocks[k]) for k in range(2)]
+        for r, part in sums:
+            cols = slice(HALF + part.start, HALF + part.stop)
             nc.vector.scalar_tensor_tensor(
-                centred[:, r, :], q[r][:, halves[1]], factor[r][:], ph[r][:, halves[1]], ALU.mult, ALU.add
+                centred[:, r, part], q[r][:, cols], factor[r][:], ph[r][:, cols], ALU.mult, ALU.add
             )
         g_codes = sb.tile([P, E], U32, name="g_codes", align_bytes=64)
         g_scales = sb.tile([P, E], U8, name="g_scales", align_bytes=64)
         g_by_i = [sb.tile([P, HALF, PACK], BF16, name=f"g_by_i{h}", tag=f"g_by_i{h}", align_bytes=64) for h in range(2)]
-        nc.vector.tensor_tensor(
-            g_by_i[1][:].rearrange("s (c i) r -> s c r i", i=PACK),
-            centred[:].rearrange("s r (c i) -> s c r i", i=PACK),
-            ce_rows[:, :, halves[1]].to_broadcast([P, PACK, HALF]).rearrange("s r (c i) -> s c r i", i=PACK),
-            ALU.mult,
-        )
-        quantise_turned((3,), "h2")
+        for k in range(2):
+            nc.vector.tensor_tensor(
+                g_by_i[1][:, blocks[k]].rearrange("s (c i) r -> s c r i", i=PACK),
+                centred[:, :, blocks[k]].rearrange("s r (c i) -> s c r i", i=PACK),
+                ce_rows[:, :, blocks[2 + k]].to_broadcast([P, PACK, P]).rearrange("s r (c i) -> s c r i", i=PACK),
+                ALU.mult,
+            )
 
         g_words = g_by_i[0][:].rearrange("s e r -> s (e r)").bitcast(F32).rearrange("s (j e w) -> s j e w", j=2, w=2)
         back = [ps.tile([P, 2, P], F32, name=f"g_back{j}", tag=f"bank{j}") for j in range(2)]
@@ -334,13 +345,14 @@ def tile_attend_grouter_W_kernel(tc, xT, W, dg, lb, ce, tx, offs, out):
                 nc.tensor.transpose(back[j][:, pair, :], words, ident[:])
         for j in range(2):
             nc.scalar.copy(g_words[:, j], back[j][:].rearrange("s w e -> s e w"))
-        for h, part in ((1, slice(0, HALF)), (0, slice(0, P)), (0, slice(P, HALF))):
-            cols = slice(h * HALF + part.start, h * HALF + part.stop)
+        for j in (2, 3, 0, 1):
             nc.vector.quantize_mx(
-                out=g_codes[:, cols].bitcast(E5M2X4),
-                scales=g_scales[:, cols],
-                in_=g_by_i[h][:, part].rearrange("s e r -> s (e r)"),
+                out=g_codes[:, blocks[j]].bitcast(E5M2X4),
+                scales=g_scales[:, blocks[j]],
+                in_=g_by_i[j // 2][:, blocks[j % 2]].rearrange("s e r -> s (e r)"),
             )
+            if j == 3:
+                quantise_turned((3,), "g_by_i1")
 
         out_rows = out.rearrange("(p t) e -> p t e", t=PACK)
         for step in range(2 * PACK):

from contextlib import ExitStack

import concourse.mybir as mybir
from concourse.masks import make_identity

F32 = mybir.dt.float32
BF16 = mybir.dt.bfloat16
U32 = mybir.dt.uint32
U16 = mybir.dt.uint16
U8 = mybir.dt.uint8
E4M3X4 = mybir.dt.float8_e4m3fn_x4
E5M2X4 = mybir.dt.float8_e5m2_x4
ALU = mybir.AluOpType
ACT = mybir.ActivationFunctionType

P = 128
PACK = 4
D, E, SLOTS, TOKENS = 512, 512, 512, 2048
HALF = E // 2
SUMMED = 1
SCALAR_SLOTS = 128
DIRECT = 2
SCALAR_W = 96

FLOPS = 2 * 2 * D * E * SLOTS


def interleave(copy, dst, src):
    copy(out=dst.rearrange("p (c i) t -> p c t i", i=PACK), in_=src.rearrange("p t (c i) -> p c t i", i=PACK))


def tile_attend_grouter_W_kernel(tc, xT, W, dg, lb, ce, tx, offs, out):
    nc = tc.nc
    with ExitStack() as ctx:
        sb = ctx.enter_context(tc.tile_pool(name="sb", bufs=1))
        ps = ctx.enter_context(tc.psum_pool(name="ps", bufs=1))

        vectors = sb.tile([P, P], F32, name="vectors")
        nc.gpsimd.memset(vectors[:], 0.0)
        ident = sb.tile([P, P], F32, name="ident")
        make_identity(nc, ident[:])

        offsets = sb.tile([P, SLOTS // 16], U16, name="offsets")
        nc.sync.dma_start(offsets[:], offs)
        tx_first = sb.tile([1, TOKENS], F32, name="tx_first", tag="tx_first")
        nc.scalar.dma_start(tx_first[:], tx[0:1, :])
        x_rows = xT.rearrange("(p t) n -> t p n", t=PACK)
        planes = [sb.tile([P, TOKENS], F32, name=f"plane{t}", tag=f"plane{t}", align_bytes=64) for t in range(PACK)]
        nc.sync.dma_start(planes[0][:], x_rows[0])
        for v, source in enumerate((ce, lb)):
            nc.sync.dma_start(vectors[v * PACK : (v + 1) * PACK, :], source[0].rearrange("(j e) -> j e", e=P))
        for t in range(1, PACK):
            nc.sync.dma_start(planes[t][:], x_rows[t])

        w_rows = W.rearrange("(p t) e -> p t e", t=PACK)
        w_raw = [sb.tile([P, PACK, HALF], F32, name=f"w_raw{h}", tag=f"w_raw{h}", align_bytes=64) for h in range(2)]
        for h in range(2):
            nc.sync.dma_start(w_raw[h][:], w_rows[:, :, h * HALF : (h + 1) * HALF])

        dg_rows = dg.rearrange("(s r) e -> r s e", r=PACK)
        dg_sb = [sb.tile([P, E], F32, name=f"dg{r}", tag=f"dg{r}", align_bytes=64) for r in range(PACK)]
        for r in range(PACK):
            nc.sync.dma_start(dg_sb[r][:], dg_rows[r])

        tx_pool = sb.tile([P, TOKENS], F32, name="tx_pool")
        nc.vector.memset(tx_pool[:], 0.0)
        nc.vector.tensor_copy(tx_pool[0:1, :], tx_first[:])

        turned_vectors = ps.tile([P, P], F32, name="turned_vectors", tag="bank3")
        nc.tensor.transpose(turned_vectors[:], vectors[:], ident[:])
        columns = sb.tile([P, 2, PACK], F32, name="columns")
        nc.scalar.copy(columns[:].rearrange("e v j -> e (v j)"), turned_vectors[:, : 2 * PACK])
        spread = [ps.tile([P, E], F32, name=f"spread{v}", tag=f"bank{4 + 2 * v}") for v in range(2)]
        ce_rows = sb.tile([P, 1, E], F32, name="ce_rows")
        lb_rows = sb.tile([P, E], F32, name="lb_rows")
        for v, vector_rows in enumerate((ce_rows[:, 0, :], lb_rows[:])):
            for j in range(PACK):
                nc.tensor.transpose(
                    spread[v][:, j * P : (j + 1) * P], columns[:, v, j : j + 1].to_broadcast([P, P]), ident[:]
                )
            nc.scalar.copy(vector_rows, spread[v][:])

        tx_row = sb.tile([P, SLOTS], F32, name="tx_row")
        nc.vector.tensor_copy(tx_row[:], tx_pool[:].indirect(offsets[:]))
        tx_bank = ps.tile([P, PACK, P], F32, name="tx_bank", tag="bank3")
        for r in range(PACK):
            nc.tensor.transpose(tx_bank[:, r, :], tx_row[:, r::PACK], ident[:])
        neg_tx = sb.tile([P, PACK], F32, name="neg_tx")
        nc.scalar.activation(neg_tx[:], tx_bank[:, :, 0], ACT.Copy, scale=-1.0)
        numerators = sb.tile([P, PACK, 2], F32, name="numerators")
        nc.vector.memset(numerators[:], -1.0)
        nc.scalar.copy(numerators[:, :, 0], tx_bank[:, :, 0])

        x_by_d = sb.tile([P, PACK, P, PACK], BF16, name="x_by_d", align_bytes=64)
        x_flat = x_by_d[:].rearrange("p r s t -> p (r s t)")
        x_by_i = {
            planes_of: sb.tile([P, len(planes_of), P, PACK], BF16, name=f"x_by_i{planes_of[0]}", tag=tag, align_bytes=64)
            for planes_of, tag in (((0, 1), "x_by_i0"), ((2,), "x_by_i2"))
        }
        xi_codes, xi_scales = {}, {}

        def turn_plane(t, gathered, turned_plane):
            turned = ps.tile([P, 2, P], F32, name=f"turned{t}", tag=f"bank{(4, 3, 4)[t]}")
            for w in range(2):
                nc.tensor.transpose(turned[:, w, :], gathered.bitcast(F32)[:, w::2], ident[:])
            words = turned_plane.rearrange("s p r -> s (p r)").bitcast(F32)
            nc.scalar.copy(words.rearrange("s (p w) -> s p w", w=2), turned[:].rearrange("s w p -> s p w"))

        def quantise_turned(planes_of, tag):
            n = len(planes_of)
            codes = sb.tile([P, n, P], U32, name=f"xi_codes{planes_of[0]}", tag=tag, align_bytes=64)
            scales = sb.tile([P, n, P], U8, name=f"xi_scales{planes_of[0]}", align_bytes=64)
            nc.vector.quantize_mx(
                out=codes[:].rearrange("s t p -> s (t p)").bitcast(E4M3X4),
                scales=scales[:].rearrange("s t p -> s (t p)"),
                in_=x_by_i[planes_of][:].rearrange("s t p r -> s (t p r)"),
            )
            for k, t in enumerate(planes_of):
                xi_codes[t], xi_scales[t] = codes[:, k, :], scales[:, k, :]

        picked = sb.tile([P, 2, SLOTS], BF16, name="picked", tag="tx_first")
        for t in range(2):
            nc.vector.tensor_copy(picked[:, t, :], planes[t][:].indirect(offsets[:]))
            turn_plane(t, picked[:, t, :], x_by_i[0, 1][:, t])
        nc.vector.tensor_copy(
            x_by_d[:, :, :, 0:2].rearrange("p r s t -> p s t r"), picked[:].rearrange("p t (s r) -> p s t r", r=PACK)
        )
        picked_late = sb.tile([P, 2, SLOTS], BF16, name="picked_late")
        nc.vector.tensor_copy(picked_late[:, 0, :], planes[2][:].indirect(offsets[:]))
        turn_plane(2, picked_late[:, 0, :], x_by_i[(2,)][:, 0])
        quantise_turned((0, 1), "plane2")
        first = SLOTS - SCALAR_SLOTS
        nc.vector.tensor_copy(
            x_by_d[:, :, : first // PACK, 2].rearrange("p r s -> p s r"),
            picked_late[:, 0, :first].rearrange("p (s r) -> p s r", r=PACK),
        )
        nc.vector.tensor_copy(
            x_by_d[:, :, : first // PACK, 3].rearrange("p r s -> p s r"),
            planes[3][:].indirect(offsets[:, : first // 16]),
        )
        nc.scalar.activation(picked_late[:, 1, first:], planes[3][:].indirect(offsets[:, first // 16 :]), ACT.Copy)
        nc.scalar.copy(
            x_by_d[:, :, first // PACK :, 2:4].rearrange("p r s t -> p s t r"),
            picked_late[:, :, first:].rearrange("p t (s r) -> p s t r", r=PACK),
        )
        quantise_turned((2,), "plane3")

        xd_codes = sb.tile([P, SLOTS], U32, name="xd_codes", tag="xd_codes", align_bytes=64)
        xd_scales = sb.tile([P, SLOTS], U8, name="xd_scales", align_bytes=64)
        nc.vector.quantize_mx(out=xd_codes[:].bitcast(E4M3X4), scales=xd_scales[:], in_=x_flat)

        w_codes = sb.tile([P, E], U32, name="w_codes", align_bytes=64)
        w_scales = sb.tile([P, E], U8, name="w_scales", align_bytes=64)
        halves = [slice(h * HALF, (h + 1) * HALF) for h in range(2)]
        blocks = [slice(j * P, (j + 1) * P) for j in range(PACK)]
        w_grouped = [
            sb.tile([P, HALF, PACK], BF16, name=f"w_grouped{h}", tag=f"w_grouped{h}", align_bytes=64) for h in range(2)
        ]

        def quantise_w(h, cols):
            whole = slice(h * HALF + cols.start, h * HALF + cols.stop)
            nc.vector.quantize_mx(
                out=w_codes[:, whole].bitcast(E4M3X4),
                scales=w_scales[:, whole],
                in_=w_grouped[h][:, cols].rearrange("p e t -> p (e t)"),
            )

        for j in range(2):
            interleave(nc.scalar.copy, w_grouped[0][:, blocks[j]], w_raw[0][:, :, blocks[j]])
            quantise_w(0, blocks[j])
        interleave(nc.scalar.copy, w_grouped[1][:, :SCALAR_W], w_raw[1][:, :, :SCALAR_W])
        interleave(nc.vector.tensor_copy, w_grouped[1][:, SCALAR_W:], w_raw[1][:, :, SCALAR_W:])
        quantise_w(1, slice(0, HALF))

        words = x_flat.bitcast(F32).rearrange("p (r s u) -> p r s u", r=PACK, u=2)
        turned_last = ps.tile([P, PACK, P], F32, name="turned_last", tag="bank2")
        for r in range(PACK):
            nc.tensor.transpose(turned_last[:, r, :], words[:, r, :, 1], ident[:])

        x_by_i[(3,)] = sb.tile([P, 1, P, PACK], BF16, name="x_by_i3", tag="w_grouped0", align_bytes=64)
        values = turned_last[:].rearrange("s r p -> s (r p)").bitcast(BF16)
        nc.scalar.copy(x_by_i[(3,)][:, 0], values.rearrange("s (r p t) -> s t p r", r=PACK, t=2)[:, 1])

        h_rows = [
            sb.tile([P, E], F32, name=f"h{r}", tag=tag, align_bytes=64)
            for r, tag in enumerate(("w_grouped1", "h1", "h2", "h3"))
        ]
        for r in range(PACK):
            cols = halves[1] if r == 0 else slice(0, E)
            nc.gpsimd.tensor_tensor(h_rows[r][:, cols], dg_sb[r][:, cols], lb_rows[:, cols], ALU.add)

        def score_product(result, stationary, moving):
            nc.tensor.matmul_mx(
                out=result,
                lhsT=stationary[0].bitcast(E4M3X4),
                lhsT_scale=stationary[1],
                rhs=moving[0].bitcast(E4M3X4),
                rhs_scale=moving[1],
                start=True,
                stop=True,
            )

        def w_part(cols):
            return w_codes[:, cols], w_scales[:, cols]

        def x_part(slots):
            return xd_codes[:, slots], xd_scales[:, slots]

        first_halves = ps.tile([P, DIRECT, HALF], F32, name="first_halves", tag="bank0")
        direct = [
            (first_halves[:, r, :], ps.tile([P, HALF], F32, name=f"second_half{r}", tag=f"bank{4 + r}")[:])
            for r in range(DIRECT)
        ]
        late_slots = slice(DIRECT * P, SLOTS)
        a_turned = [
            ps.tile([P, 2, SLOTS - DIRECT * P], F32, name=f"a_turned{h}", tag=f"bank{(1, 7)[h]}") for h in range(2)
        ]
        for j in range(2):
            for r in range(DIRECT):
                score_product(direct[r][0][:, blocks[j]], x_part(blocks[r]), w_part(blocks[j]))
            score_product(a_turned[0][:, j, :], w_part(blocks[j]), x_part(late_slots))
        for r in range(DIRECT):
            score_product(direct[r][1], x_part(blocks[r]), w_part(halves[1]))
        for j in range(2, PACK):
            score_product(a_turned[1][:, j - 2, :], w_part(blocks[j]), x_part(late_slots))
        neg_z = [sb.tile([P, E], F32, name=f"neg_z{r}") for r in range(PACK)]

        def scale_direct(r, h):
            nc.vector.scalar_tensor_tensor(
                neg_z[r][:, halves[h]], direct[r][h], neg_tx[:, r : r + 1], ce_rows[:, 0, halves[h]], ALU.mult, ALU.mult
            )

        for r in range(DIRECT):
            scale_direct(r, 0)
        nc.vector.tensor_tensor(h_rows[0][:, halves[0]], dg_sb[0][:, halves[0]], spread[1][:, halves[0]], ALU.add)
        by_expert = sb.tile([P, PACK, SLOTS - DIRECT * P], F32, name="by_expert")
        for j in range(PACK):
            nc.scalar.activation(
                by_expert[:, j, :], a_turned[j // 2][:, j % 2, :], ACT.Copy, scale=columns[:, 0, j : j + 1]
            )
        scores = {r: ps.tile([P, E], F32, name=f"scores{r}", tag=f"bank{r}") for r in range(DIRECT, PACK)}
        for r in range(DIRECT, PACK):
            for j in range(PACK):
                nc.tensor.transpose(scores[r][:, blocks[j]], by_expert[:, j, blocks[r - DIRECT]], ident[:])

        def column(name):
            return [sb.tile([P, 1], F32, name=f"{name}{r}") for r in range(PACK)]

        def rows(name):
            return [sb.tile([P, E], F32, name=f"{name}{r}") for r in range(PACK)]

        neg_max, tx_s, factor, total = (column(n) for n in ("neg_max", "tx_s", "factor", "total"))
        inv_total = sb.tile([P, PACK], F32, name="inv_total")
        weights = sb.tile([P, PACK, 2], F32, name="weights")
        q, ph = (rows(n) for n in ("q", "ph"))
        centred_turned = [
            [ps.tile([P, 2, P], F32, name=f"centred{pair}{j}", tag=f"bank{4 + 2 * pair + j}") for j in range(2)]
            for pair in range(2)
        ]

        def exponentials(r):
            if r < DIRECT:
                scale_direct(r, 1)
                nc.vector.tensor_reduce(neg_max[r][:], neg_z[r][:], mybir.AxisListType.X, ALU.min)
            else:
                nc.vector.tensor_scalar(
                    neg_z[r][:], scores[r][:], neg_tx[:, r : r + 1], None, ALU.mult, ALU.min, accum_out=neg_max[r][:]
                )
            nc.scalar.activation(q[r][:], neg_z[r][:], ACT.Exp, bias=neg_max[r][:], scale=-1.0, accum_out=total[r][:])

        def inverse(r):
            nc.vector.reciprocal(inv_total[:, r : r + 1], total[r][:])
            nc.scalar.activation(weights[:, r, :], numerators[:, r, :], ACT.Copy, scale=inv_total[:, r : r + 1])

        def weighted_sum(r):
            nc.vector.scalar_tensor_tensor(
                ph[r][:], q[r][:], weights[:, r, 0:1], h_rows[r][:], ALU.mult, ALU.mult, accum_out=tx_s[r][:]
            )

        def centre_turned(r):
            scaled_q = sb.tile([P, HALF], F32, name=f"scaled_q{r}")
            if r < PACK - 1:
                nc.scalar.activation(factor[r][:], tx_s[r][:], ACT.Copy, scale=weights[:, r, 1:2])
                scaled = blocks[0] if r == SUMMED else halves[0]
                nc.scalar.activation(scaled_q[:, scaled], q[r][:, scaled], ACT.Copy, scale=factor[r][:])
                if r == SUMMED:
                    nc.vector.scalar_tensor_tensor(
                        scaled_q[:, blocks[1]], q[r][:, blocks[1]], factor[r][:], ph[r][:, blocks[1]], ALU.mult, ALU.add
                    )
            else:
                nc.vector.tensor_scalar(factor[r][:], tx_s[r][:], weights[:, r, 1:2], None, ALU.mult)
                neg_p = sb.tile([P, HALF], F32, name="neg_p")
                nc.scalar.activation(neg_p[:], q[r][:, :HALF], ACT.Copy, scale=weights[:, r, 1:2])
                for j in range(2):
                    nc.scalar.activation(scaled_q[:, blocks[j]], neg_p[:, blocks[j]], ACT.Copy, scale=tx_s[r][:])
            for term, source in enumerate((ph[r], scaled_q)):
                for j in range(2):
                    summed = r == SUMMED and j == 1
                    if term == 1 or not summed:
                        nc.tensor.matmul(
                            centred_turned[r // 2][j][:, r % 2, :],
                            source[:, blocks[j]],
                            ident[:],
                            is_transpose=True,
                            start=term == 0 or summed,
                            stop=term == 1,
                        )

        stages = ((exponentials, 0), (inverse, 2), (centre_turned, 4), (weighted_sum, 3))
        for step in range(PACK + max(lag for stage, lag in stages)):
            for stage, lag in stages:
                if 0 <= step - lag < PACK:
                    stage(step - lag)

        centred = sb.tile([P, PACK, HALF], F32, name="centred", tag="h2", align_bytes=64)
        sums = [(r, slice(0, HALF)) for r in range(PACK - 1)] + [(PACK - 1, blocks[k]) for k in range(2)]
        for r, part in sums:
            cols = slice(HALF + part.start, HALF + part.stop)
            nc.vector.scalar_tensor_tensor(
                centred[:, r, part], q[r][:, cols], factor[r][:], ph[r][:, cols], ALU.mult, ALU.add
            )
        g_codes = sb.tile([P, E], U32, name="g_codes", align_bytes=64)
        g_scales = sb.tile([P, E], U8, name="g_scales", align_bytes=64)
        g_by_i = [sb.tile([P, HALF, PACK], BF16, name=f"g_by_i{h}", tag=f"g_by_i{h}", align_bytes=64) for h in range(2)]
        for k in range(2):
            nc.vector.tensor_tensor(
                g_by_i[1][:, blocks[k]].rearrange("s (c i) r -> s c r i", i=PACK),
                centred[:, :, blocks[k]].rearrange("s r (c i) -> s c r i", i=PACK),
                ce_rows[:, :, blocks[2 + k]].to_broadcast([P, PACK, P]).rearrange("s r (c i) -> s c r i", i=PACK),
                ALU.mult,
            )

        g_words = g_by_i[0][:].rearrange("s e r -> s (e r)").bitcast(F32).rearrange("s (j e w) -> s j e w", j=2, w=2)
        back = [ps.tile([P, 2, P], F32, name=f"g_back{j}", tag=f"bank{j}") for j in range(2)]
        for pair in range(2):
            for j in range(2):
                g_turned = sb.tile([P, P, 2], BF16, name=f"g_turned{pair}{j}")
                nc.scalar.activation(
                    g_turned[:],
                    centred_turned[pair][j][:].rearrange("e k s -> e s k"),
                    ACT.Copy,
                    scale=columns[:, 0, j : j + 1],
                )
                words = g_turned[:].rearrange("e s k -> e (s k)").bitcast(F32)
                nc.tensor.transpose(back[j][:, pair, :], words, ident[:])
        for j in range(2):
            nc.scalar.copy(g_words[:, j], back[j][:].rearrange("s w e -> s e w"))
        for j in (2, 3, 0, 1):
            nc.vector.quantize_mx(
                out=g_codes[:, blocks[j]].bitcast(E5M2X4),
                scales=g_scales[:, blocks[j]],
                in_=g_by_i[j // 2][:, blocks[j % 2]].rearrange("s e r -> s (e r)"),
            )
            if j == 3:
                quantise_turned((3,), "g_by_i1")

        out_rows = out.rearrange("(p t) e -> p t e", t=PACK)
        for step in range(2 * PACK):
            cols, t = halves[1 - step // PACK], step % PACK
            acc = ps.tile([P, HALF], F32, name=f"acc{step}", tag=f"bank{(2 + step) % 8}")
            nc.tensor.matmul_mx(
                out=acc[:],
                lhsT=xi_codes[t].bitcast(E4M3X4),
                lhsT_scale=xi_scales[t],
                rhs=g_codes[:, cols].bitcast(E5M2X4),
                rhs_scale=g_scales[:, cols],
                start=True,
                stop=True,
            )
            result = sb.tile([P, HALF], F32, name=f"result{step}")
            (nc.scalar.copy, nc.vector.tensor_copy)[step % 2](result[:], acc[:])
            nc.sync.dma_start(out_rows[:, t, cols], result[:])
